import numpy as np, ml_dtypes
CORES = [35,38,43,46]
N = 4
BF = ml_dtypes.bfloat16
def gentries(a):
    return np.ascontiguousarray(a.reshape(8, 16, -1).transpose(0, 2, 1)).reshape(8, -1)
def gtable(e):
    e = np.asarray(e); return np.ascontiguousarray(e.reshape(8, -1, 16).transpose(0, 2, 1)).reshape(128, -1).astype(np.int32)
W, LW, RO, E, LN = 4096, 12, 3, 1, 2
T = 3 * W // 4
def curves(rng):
    p = rng.choice(np.array([0.7, 1.0, 1.4], np.float32), (N, 8, 16, 1))
    return np.minimum((16 * rng.random((N, 8, 16, W), dtype=np.float32) ** p).astype(np.int64), 15)
def load(rng):
    return ((0.5 + 1.5 * rng.random((N, 128, W), dtype=np.float32)) * np.exp2(2 * rng.random((N, 1, W)) - 1).astype(np.float32)).astype(np.float32)
def roots(rng):
    return (0.875 + 0.25 * rng.random((N, 128, 5))).astype(np.float32)
def warp(rng, *lead):
    u = np.sort(rng.random(lead + (W,)), axis=-1); k = rng.integers(1, 4, lead + (1,)); a = rng.uniform(-0.9, 0.9, lead + (1,))
    w = np.clip(np.floor(W * (u + a * np.array([0.15915, 0.07957, 0.05305])[k - 1] * np.sin(6.283185307179586 * k * u))).astype(np.int64), 0, W - 1)
    back = rng.integers(1, 40, lead + (W // 16,)) * (rng.random(lead + (W // 16,)) < 0.15)
    turn = 7 * (rng.random(lead + (W // 8,)) < 0.1)
    i = np.maximum(np.arange(W) - np.repeat(back, 16, axis=-1), 0) ^ np.repeat(turn, 8, axis=-1)
    return np.take_along_axis(w, i, -1)
def cliffs(rng, *lead):
    j = np.arange(W); w = np.sort(rng.integers(0, W - 1, lead + (W,)), axis=-1)[..., np.minimum(4 * j // 3, W - 1)]; r = rng.random(lead + (W,))
    e = np.where(j < T, np.where(r < 0.45, w, 0), np.where(r < 0.6, W - 1, 0))
    e[..., 0] = 0; e[..., W - 1] = W - 1
    return e
def pack(x, v, rt, e, ga):
    return {"xs": np.ascontiguousarray(x.reshape(N, 128, W)).astype(np.float32).astype(BF), "pay": v.astype(BF), "rho": rt.astype(np.float32),
            "ew": np.stack([gtable(a.reshape(8, -1)) for a in e]), "gam": np.stack([gtable(a) for a in ga])}
def setup_inputs(rng):
    return pack(curves(rng), load(rng), roots(rng), warp(rng, N, 8, RO, E), warp(rng, N, 8))
def setup_inputs_spread(rng):
    p = np.exp2(rng.uniform(-2, 2, (N, 8, 1, W))).astype(np.float32)
    x = np.minimum((16 * rng.random((N, 8, 16, W), dtype=np.float32) ** p).astype(np.int64), 15)
    e = warp(rng, N, 8, RO, E); e[:, 1::2] = rng.integers(0, W, (N, 4, RO, E, W))
    return pack(x, load(rng), roots(rng), e, warp(rng, N, 8))
def setup_inputs_ends(rng):
    x = 15 * (rng.random((N, 8, 16, W)) < rng.choice(np.array([0.15, 0.5, 0.85]), (N, 8, 1, 1))).astype(np.int64)
    x[0, 0] = 15; x[0, 4] = 15; x[0, 7] = 15; x[N - 1, 7] = 0; x[2, 3] = 0
    x[1, 7] = 0; x[1, 7, 15, W - 1] = 15
    e = cliffs(rng, N, 8, RO, E); ga = cliffs(rng, N, 8)
    e[:, 2::3] = (W - 1) * rng.integers(0, 2, e[:, 2::3].shape)
    e[1, 7, 0, 1:, T:W - 1] = 0; e[1, 7, 0, 0, T:] = ga[2, 0, T:]
    h = T + int(np.argmax(e[1, 7, 0, 0, T:] == W - 1)); e[1, 7, 0, 0, h] = 0
    for q, g in ((N - 1, 6), (1, 3)):
        a = (q + 1) % N
        x[q, g] = 0; x[q, g, 15, W - 1] = 1
        ga[a, g + 1, W - 32:W - 1] = 0
        e[q, g, 0, 1:, T:W - 1] = 0; e[q, g, 0, 0, T:] = ga[a, g + 1, T:]; e[q, g, 0, 0, W - 1] = 0
    v = np.where(rng.random((N, 128, W)) < 0.7, 4.0, 0.25)
    rt = 0.875 + 0.25 * rng.integers(0, 2, (N, 128, 5))
    return pack(x, v.astype(np.float32), rt, e, ga)
def setup_inputs_corners(rng):
    j = np.arange(W)
    kinds = np.stack([j, W - 1 - j, 0 * j, 0 * j + W - 1, np.minimum(3 * j, W - 1), np.minimum(4 * j, W - 1), j >> 1, (5 * j) & (W - 1)])
    o = rng.permutation(8); k = o[(np.arange(N)[:, None] + np.arange(8)) % 8]
    ga = kinds[k]; e = kinds[rng.integers(0, 8, (N, 8, RO, E))]
    e = np.where(rng.random((N, 8, RO, E, 1)) < 0.3, rng.integers(0, W, e.shape), e)
    x = curves(rng); off = int(rng.integers(0, 8))
    for q in range(N):
        for g in range(8):
            m = (3 * q + g + off) % 8
            if m == 0: x[q, g] = 0
            elif m == 1: x[q, g] = 15
            elif m == 2: x[q, g] = rng.integers(0, 16, (16, 1))
            elif m == 3: x[q, g] = (16 * j) >> LW
            elif m == 4: x[q, g] = 0; x[q, g, :, W - 1] = 15
    return pack(x, load(rng), roots(rng), e, ga)
def setup_inputs_ties(rng):
    x = curves(rng); e = warp(rng, N, 8, RO, E); ga = warp(rng, N, 8); j = np.arange(W); a = int(rng.integers(0, N)); b = (a + 1) % N
    x[:, ::2] = np.where((j & 2) > 0, 15, np.minimum(x[:, ::2], 14))
    x[a, 1::2] = 15; x[b, 1::4] = rng.integers(0, 16, (2, 16, 1))
    base = (j & ~3) | 2
    e[:, ::2, 0, 0] = base + rng.integers(0, 2, (N, 4, W)); ga[:, 1::2] = base + rng.integers(0, 2, (N, 4, W))
    e[1::2, ::2, 0, 0, W - 1] = W - 4
    x[1::2, ::2, :, W - 4] = 15; x[1::2, ::2, int(rng.integers(0, 16)), W - 4] = 14
    x[0, 6] = np.where((j & 2) == 0, 15, np.minimum(x[0, 6], 14)); ga[1, 7] = (j & ~3) + 1; e[0, 6, 0] = warp(rng, E)
    return pack(x, load(rng), roots(rng), e, ga)
def check_ranges(d):
    bad = []
    for k, lo, hi in (("xs", 0, 15), ("pay", 0.25, 4), ("rho", 0.875, 1.125), ("ew", 0, W - 1), ("gam", 0, W - 1)):
        v = np.asarray(d[k]).astype(np.float64)
        if not (np.min(v) >= lo and np.max(v) <= hi): bad.append("range of " + k)
    v = np.asarray(d["xs"]).astype(np.float64)
    if not np.all(v == np.floor(v)): bad.append("xs is not whole")
    return bad
def pick(a, c):
    return np.take_along_axis(a, c[:, :, None, :], 3)
def inverse(w):
    w = w.reshape(-1, W); top = np.maximum.accumulate(w, axis=1)
    before = np.concatenate([np.full((len(w), 1), -1, np.int64), top[:, :-1]], axis=1)
    i, j = np.nonzero(w > before); t = np.zeros(w.shape, np.int64); t[i, w[i, j]] = j
    return np.maximum.accumulate(t, axis=1).reshape(N, 8, W)
def root(rt, c):
    s = np.concatenate([np.minimum(np.abs(c[..., 1:] - c[..., :-1]), 4), np.ones((N, 8, 1), np.int64)], axis=-1)
    return pick(rt, s)
def reference(xs, pay, rho, ew, gam):
    x = xs.astype(np.int64).reshape(N, 8, 16, W); p0 = pay.astype(np.float64).reshape(N, 8, 16, W); rt = rho.astype(np.float64).reshape(N, 8, 16, 5)
    e = np.stack([gentries(a) for a in ew]).astype(np.int64).reshape(N, 8, RO, E, W); ga = np.stack([gentries(a) for a in gam]).astype(np.int64)
    v = p0; m = np.maximum.reduce(x, axis=0)
    stay = np.broadcast_to(np.arange(W), (N, 8, W))
    for t in range(RO):
        gn = np.roll(np.roll(ga, -1, axis=0), -1, axis=1)
        tr = np.stack([stay] + [e[:, :, t, i] for i in range(E)] + [gn, inverse(gn)])
        mn = np.roll(m, -1, axis=0)[None]
        sc = np.stack([np.sum(np.abs(pick(x, c) - mn), axis=(2, 3)) for c in tr])
        b = np.argmin(sc, axis=0)
        c = np.take_along_axis(tr, b[None, :, :, None], 0)[0]
        x = pick(x, c); v = pick(v, c) * root(rt, c); ga = np.take_along_axis(ga, c, 2)
        mu = np.add.reduce(inverse(ga), axis=0) >> LN
        mu = np.broadcast_to(mu, (N, 8, W))
        x = pick(x, mu); v = pick(v, mu) * root(rt, mu); ga = np.take_along_axis(ga, mu, 2)
        m = np.maximum.reduce(x, axis=0)
        v = v + m * 0.03125
    u = v + x * 0.0625 + pick(p0, ga)
    y = (np.add.reduce(u, axis=0) * 0.25).reshape(128, W)
    n = W // N
    return {"y": np.stack([y[:, r * n:(r + 1) * n] for r in range(N)]).astype(np.float32)}

def check_inputs(d):
    bad = list(check_ranges(d))
    if not bad:
        for name, y in reference(**d).items():
            for q in range(N):
                v = np.abs(np.asarray(y[q], np.float64)); s = np.sqrt(np.mean(v * v))
                if v.max() > 3 * s or s < 2.0 ** 0: bad.append('%s of rank %d is uneven or too small' % (name, q))
    return bad

@@ -1,0 +1,707 @@
+from concourse.bass import DstId, RemoteDMATransfer
+from concourse.mybir import AluOpType as A, AxisListType, ActivationFunctionType as AF
+
+W = 4096
+PRE0, NA0, ND0, PRE, NA, ND, GA3 = 6, 0, 3, 3, 1, 2, 0
+MAG = 12582912.0
+F32, BF, F16, I32, U16 = "float32", "bfloat16", "float16", "int32", "uint16"
+
+
+def _sb(n, d):
+    return ("sbuf", [128, n], d)
+
+
+SCRATCH = {
+    "GX": _sb(5 * W, BF), "M0": _sb(W, BF), "M1": _sb(W, BF), "LX": _sb(W, BF),
+    "V": _sb(W, F32), "VD": _sb(W, F32), "PAY": _sb(W, BF),
+    "WG": _sb(W, BF), "G1": _sb(W, BF), "G2": _sb(W, BF),
+    "SW": _sb(W + 256, F32), "ST": _sb(W, F32), "RR": _sb(W, BF), "JK": _sb(2048, BF),
+    "LU": _sb(3072, F32), "NK": _sb(7 * 512, BF),
+    "PI": _sb(4, I32), "KI": _sb(256, I32), "TI": _sb(256, I32), "TJ": _sb(256, I32), "GS": _sb(256, I32), "GA": _sb(256, I32),
+    "CI": _sb(256, F32), "CG": _sb(160, F32), "CO": _sb(32, F32), "OH": _sb(16, F32), "T1": _sb(256, F32), "T2": _sb(256, F32),
+    "EE": _sb(5 * 144, BF), "ID": _sb(128, BF), "NSH": _sb(128, BF), "I16": _sb(128, BF), "I8": _sb(128, BF), "CM": _sb(128, BF),
+    "IDF": _sb(128, F32), "GM4": _sb(128, F32), "GL": _sb(128, F32), "GU": _sb(128, F32), "BIGM": _sb(16, F32),
+    "QI": _sb(128, F16), "LZ": _sb(4 * 160, F16), "S1": _sb(128, F16), "S2": _sb(128, F16),
+    "BC": _sb(256, F32), "DUMP": _sb(16, F32), "B16": _sb(16, F32), "ZR": _sb(256, F32), "PO": _sb(16, U16),
+    "TOP": _sb(260, F32), "EX": _sb(256, F32), "MM": _sb(256, F32), "NN": _sb(260, F32), "R16": _sb(32, F32), "CA": _sb(8, F32),
+    "NH": _sb(256, F16), "TR": ("sbuf", [128, 8, 2, 16], F16), "FF": _sb(20, F32), "FA": _sb(48, F32), "SO": _sb(16, U16), "SRC": _sb(256, F32),
+    "WB": _sb(256, F32), "HL": _sb(512, BF),
+    "LW": _sb(1024, I32), "EU": _sb(256, U16), "GO": _sb(256, U16), "GN": _sb(256, U16), "IN": _sb(256, U16), "HT": _sb(512, BF), "HN": _sb(1024, BF),
+    "MO": _sb(256, F16), "ML": _sb(9 * 256, F16), "MU": _sb(256, U16), "MX": _sb(256, U16), "MH": _sb(264, F16),
+    "ACC": _sb(32, F32), "SC": _sb(4, F32), "KY": _sb(4, F32), "EL": _sb(8, F32), "CS": _sb(16, U16), "CU": _sb(256, U16),
+    "DU": _sb(256, U16), "IX": _sb(256, U16), "RHO": _sb(8, F32), "RB": _sb(8, F32), "RT": _sb(192, F32),
+    "PA": ("psum", [128, 512], F32), "PB": ("psum", [128, 512], F32), "PD": ("psum", [128, 512], F32),
+    "P0": ("psum", [128, 1024], F32), "P1": ("psum", [128, 1024], F32),
+    "P4": ("psum", [128, 16, 2, 16], F32),
+}
+REMOTE = (["g%d" % t for t in range(3)]
+          + ["m%d_%d" % (t, h) for t in range(3) for h in range(2)] + ["x%d" % t for t in range(4)]
+          + ["b%d_%d" % (t, q) for t in range(4) for q in range(4)] + ["u%d" % q for q in range(4)] + ["p"])
+SEMAPHORES = ["pe", "dve", "act", "pool"] + ["r" + k for k in REMOTE] + ["q%d" % i for i in range(100)]
+
+
+def _bits(m):
+    return [e for e in range(m.bit_length()) if m >> e & 1]
+
+
+def _helper(core, T, topo):
+    return [c for c in topo.cores_of(core) if topo.die(c) == topo.die(core) and T.rank_of(c) is None][0]
+
+
+def helper_program(g, core, owner, T, topo):
+    rid, pid, _ = topo.addr(owner)
+    r = T.rank_of(owner)
+    m = topo.mask(core, owner)
+    n = len(_bits(m))
+    far = [c for c in T.cores if topo.chip(c) != topo.chip(owner)][0]
+    for t in range(4):
+        g.wait_ge(T.sem["rb%d_%d" % (t, r)], len(_bits(topo.mask(owner, core) & ~topo.mask(owner, far))))
+        dst = T.LX[:, 3072:4096] if t == 3 else T["M%d" % (t % 2)][:, 1024 * r:1024 * r + 1024]
+        g.remote_dma(dst, T.GX[:, 1024 * t:1024 * t + 1024], T.sem["rb%d_%d" % (t, r)], T.sem.q0, pid, rid, m)
+    g.wait_ge(T.sem.q0, 4 * n)
+
+
+def rank_program(g, core, T, topo):
+    r = T.rank_of(core)
+    if r is None:
+        for c in T.cores:
+            if _helper(c, T, topo) == core:
+                helper_program(g, core, c, T, topo)
+        return
+    N = len(T.cores)
+
+    Q = {"pe": g.tensor, "dve": g.vector, "act": g.scalar, "pool": g, "sp": g.sync}
+    cnt = {}
+    waited = {k: {} for k in Q}
+    lastw, readers = {}, {}
+    nq = [0]
+
+    def wait(q, tok):
+        s, v = tok[0], tok[1]
+        if waited[q].get(s, 0) < v:
+            Q[q].wait_ge(T.sem[s], v)
+            waited[q][s] = v
+
+    def deps(q, rd, wr, inorder):
+        for k in rd:
+            if k in lastw and not (q == "pe" and lastw[k][0] == "pe"):
+                wait(q, lastw[k])
+        for k in wr:
+            for tok in ([lastw[k]] if k in lastw else []) + readers.get(k, []):
+                if not (inorder and tok[0] == q):
+                    wait(q, tok)
+
+    def done(tok, rd, wr):
+        for k in rd:
+            readers.setdefault(k, []).append(tok)
+        for k in wr:
+            lastw[k] = tok
+            readers[k] = []
+
+    def op(q, fn, rd, wr):
+        ps = [k for k in rd if k[0] == "P" and len(k) == 2]
+        deps(q, rd, wr, q == "pe")
+        for k in ps:
+            for tok in readers.get(k, []):
+                if tok[0] != q:
+                    wait(q, tok)
+        cnt[q] = cnt.get(q, 0) + 1
+        fn().then_inc(T.sem[q], 1)
+        done((q, cnt[q]), rd, wr)
+
+    def fresh():
+        nq[0] += 1
+        return "q%d" % (nq[0] - 1)
+
+    def dma(q, out, in_, rd, wr, **kw):
+        deps(q, rd, wr, False)
+        s = fresh()
+        Q[q].dma_start(out, in_, **kw).then_inc(T.sem[s], 16)
+        cnt[s] = 16
+        done((s, 16), rd, wr)
+
+    def arrive(key, n, wr):
+        cnt["r" + key] = n
+        done(("r" + key, n), [], wr)
+
+    def send(trs, rd, extra=()):
+        deps("pool", list(rd) + list(extra), [], False)
+        s = fresh()
+        tot = 0
+        L = []
+        for cores, m, key, srcs, dsts, alu in trs:
+            ids = [DstId(rid=topo.addr(c)[0], pnc=topo.addr(c)[1]) for c in cores]
+            L.append(RemoteDMATransfer(dst_ids=ids, dma_engine_mask=m, remote_sem=T.sem["r" + key], srcs=srcs, dsts=dsts, alu_op=alu))
+            tot += len(_bits(m))
+        g.remote_dma_fused(L, local_sem=T.sem[s])
+        cnt[s] = tot
+        done((s, tot), rd, [])
+        return (s, tot)
+
+    V_, S_, P_ = g.vector, g.scalar, g.tensor
+
+    def ts(out, in0, s1, s2, o0, o1, rd, wr):
+        if o1 is None:
+            op("dve", lambda: V_.tensor_scalar(out, in0, s1, None, o0), rd, wr)
+        else:
+            op("dve", lambda: V_.tensor_scalar(out, in0, s1, s2, o0, o1), rd, wr)
+
+    def tt(out, a, b, o, rd, wr):
+        op("dve", lambda: V_.tensor_tensor(out, a, b, o), rd, wr)
+
+    def cp(out, a, rd, wr):
+        op("dve", lambda: V_.tensor_copy(out, a), rd, wr)
+
+    def ms(out, v, wr):
+        op("dve", lambda: V_.memset(out, v), [], wr)
+
+    def red(out, a, o, rd, wr, **kw):
+        op("dve", lambda: V_.tensor_reduce(out, a, AxisListType.X, o, **kw), rd, wr)
+
+    def mm(out, l, rhs, st, sp, rd, wr):
+        op("pe", lambda: P_.matmul(out, l, rhs, st, sp), rd, wr)
+
+    def gat(q, out, win, off, rd, wr):
+        if q == "dve":
+            op(q, lambda: V_.tensor_copy(out, win.indirect(off)), rd, wr)
+        else:
+            op(q, lambda: S_.activation(out, win.indirect(off), AF.Copy), rd, wr)
+
+    def ch(name, cs=range(4)):
+        return ["%s.%d" % (name, c) for c in cs]
+
+    def c4(t, c, base=0):
+        return t[:, base + 1024 * c:base + 1024 * c + 1024]
+
+    def o4(t, c, base=0):
+        return t[:, base + 64 * c:base + 64 * c + 64]
+
+    others = [(r + k) % N for k in range(1, N)]
+    order = others + [r]
+    far = [q for q in others if topo.chip(T.cores[q]) != topo.chip(core)]
+    near = [q for q in others if q not in far]
+    hc = _helper(core, T, topo)
+    m_far = topo.mask(core, T.cores[far[0]])
+    m_near = topo.mask(core, T.cores[near[0]]) & ~m_far
+    fb = _bits(m_far)
+    m_half = [sum(1 << e for e in fb[:len(fb) // 2]), sum(1 << e for e in fb[len(fb) // 2:])]
+    n_far, n_near = len(fb), len(_bits(m_near))
+    prev, nxt = (r - 1) % N, (r + 1) % N
+
+    def mk(q):
+        return m_far if q in far else m_near
+
+    def nk(q):
+        return n_far if q in far else n_near
+
+    dma("act", T.GS[0:112, :], T.gam[16:128, :], [], ["GSa"])
+    dma("sp", T.GS[112:128, :], T.gam[0:16, :], [], ["GSb"])
+    for c in order:
+        dma("sp", c4(T.GX, c), c4(T.xs, c), [], ["XA.%d" % c])
+    dma("act", T.LW[:, 256:512], T.ew[:, 0:256], [], ["LW.1"])
+    dma("act", T.GA[:], T.gam[:], [], ["GA"])
+
+    op("pool", lambda: g.iota(T.PI[:, 0:1], [[0, 1]], 0, 1), [], ["PI0"])
+    op("pool", lambda: g.iota(T.KI[:], [[1, 256]], 0, 0), [], ["KI"])
+    op("pool", lambda: g.iota(T.BC[:], [[1, 16], [16, 16]], 0, 0, allow_small_or_imprecise_dtypes=True), [], ["BC"])
+    CO = T.CO
+
+    def col(i):
+        return CO[:, i:i + 1]
+    ms(T.SW[:, 0:1088], 0.0, ["SW0"])
+    for k in range(1, 4):
+        op("act", lambda: S_.activation(T.SW[:, 1088 * k:1088 * k + 1088], T.SW[:, 0:1088], AF.Copy), ["SW0"], ["SW%d" % k])
+    ms(T.ZR[:], 0.0, ["ZR"])
+    ts(T.PI[:, 1:2], T.PI[:, 0:1], 15, None, A.bitwise_and, None, ["PI0"], ["PI1"])
+    ts(T.PI[:, 2:3], T.PI[:, 0:1], 16, None, A.bitwise_and, None, ["PI0"], ["PI2"])
+    cp(T.CI[:], T.KI[:], ["KI"], ["CI"])
+    cp(CO[:, 0:2], T.PI[:, 0:2], ["PI0", "PI1"], ["c0", "c1"])
+    ts(T.TI[:, 0:160], T.KI[:, 0:160], 240, None, A.bitwise_and, None, ["KI"], ["TI"])
+    tt(col(2), col(0), col(1), A.subtract, ["c0", "c1"], ["c2"])
+    ts(T.OH[:], T.CI[:, 0:16], col(1), None, A.is_equal, None, ["CI", "c1"], ["OH"])
+    cp(T.CG[:], T.TI[:, 0:160], ["TI"], ["CG"])
+    ts(col(6), T.PI[:, 2:3], 0.0625, None, A.mult, None, ["PI2"], ["c6"])
+    ts(col(8), col(0), 16.0, None, A.add, None, ["c0"], ["c8"])
+    ts(col(9), col(2), 16.0, None, A.add, None, ["c2"], ["c9"])
+    ts(col(10), col(1), 16.0, None, A.mult, None, ["c1"], ["c10"])
+    ts(col(5), T.OH[:, 0:1], -1.0, 1.0, A.mult, A.add, ["OH"], ["c5"])
+    ts(col(7), col(6), -1.0, 1.0, A.mult, A.add, ["c6"], ["c7"])
+    ts(T.T1[:, 0:160], T.CI[:, 0:160], col(8), None, A.is_equal, None, ["CI", "c8"], ["T1"])
+    ts(T.PO[:], T.CI[:, 0:16], col(10), None, A.add, None, ["CI", "c10"], ["PO"])
+    for z in range(2):
+        ts(T.LZ[:, 320 + 160 * z:480 + 160 * z], T.T1[:, 0:160], col(7 - z), None, A.mult, None, ["T1", "c6", "c7"], ["LP%d" % z])
+
+    def regroup(base, key):
+        for z in range(2):
+            for gb in range(2):
+                o = base + 160 * z + 16 - 16 * (gb - z)
+                mm(T.P4[:, 0:8, z, :], T.LZ[:, o:o + 128], T.TR[:, :, gb, :], gb == 0, gb == 1, ["TR", key + str(z)], ["P4"])
+
+    def to_blocks(src, key):
+        ts(T.NH[:], src.indirect(T.PO[:]), -2048.0, None, A.add, None, [key, "PO"], ["NH"])
+        op("dve", lambda: V_.transpose(T.TR[:], T.NH[:]), ["NH"], ["TR"])
+        regroup(320, "LP")
+
+    send([([T.cores[prev]], mk(prev), "g0", [T.GS[:]], [T.LW[:, 512:768]], 0)], ["GSa", "GSb"])
+    arrive("g0", nk(nxt), ["LW.2"])
+    ts(T.T2[:, 0:128], T.CG[:, 0:128], col(2), None, A.is_equal, None, ["CG", "c2"], ["T2"])
+    ts(T.GL[:], T.CI[:, 0:128], col(0), None, A.is_gt, None, ["CI", "c0"], ["GL"])
+    ts(T.GU[:], T.CI[:, 0:128], col(0), None, A.is_lt, None, ["CI", "c0"], ["GU"])
+    tt(T.GL[:], T.GL[:], T.T2[:, 0:128], A.mult, ["GL", "T2"], ["GL"])
+    tt(T.GU[:], T.GU[:], T.T2[:, 0:128], A.mult, ["GU", "T2"], ["GU"])
+    ts(T.GM4[:], T.T2[:, 0:128], 4.0, None, A.mult, None, ["T2"], ["GM4"])
+    ts(T.IDF[:], T.CI[:, 0:128], col(0), None, A.is_equal, None, ["CI", "c0"], ["IDF"])
+    ts(T.BIGM[:], T.CI[:, 0:16], col(1), 4096.0, A.is_le, A.mult, ["CI", "c1"], ["BIGM"])
+    ms(T.TOP[:, 0:1], 0.0, ["TOP0"])
+    ms(T.NN[:, 256:257], 4096.0, ["NNe"])
+
+    def send_x(c, X, xb, t):
+        send([([T.cores[c]], mk(c), "x%d" % t, [c4(T.GX, c, xb)], [c4(T.LX, (r - c) % N - 1)], 0)], ["%s.%d" % (X, c)])
+
+    def fold_x(X, xb, t):
+        arrive("x%d" % t, sum(nk(q) for q in others), ["LX"])
+        srcs = [c4(T.GX, r, xb)] + [c4(T.LX, k) for k in range(3)]
+        hb = T.GX[:, 1024 * t:1024 * t + 1024]
+        if t == 3:
+            send([([hc], m_near, "b3_%d" % r, srcs, [hb], 2)], ["LX", "%s.%d" % (X, r)])
+            arrive("b3_%d" % r, len(_bits(topo.mask(hc, core))), ["MF"])
+            return
+        Mb = T["M%d" % (t % 2)]
+        key = "b%d_%d" % (t, r)
+        lastw["fold"] = send([([T.cores[q] for q in far], m_far, key, srcs, [c4(Mb, r)] * len(far), 2),
+                              ([hc] + [T.cores[q] for q in near], m_near, key, srcs, [hb] + [c4(Mb, r)] * len(near), 2)], ["LX", "%s.%d" % (X, r)])
+        for q in range(N):
+            arrive("b%d_%d" % (t, q), len(_bits(topo.mask(hc, core))) if q == r else nk(q), ["M%d.%d" % (t % 2, q)])
+
+    def send_g(t):
+        dma("sp", T.HT[:], T.G1[0::8, :], ch("G1"), ["HT"])
+        send([([T.cores[prev]], mk(prev), "g%d" % t, [T.HT[:]], [T.HN[:, 512 * t - 512:512 * t]], 0)], ["HT"])
+        arrive("g%d" % t, nk(nxt), ["HN%d" % t])
+
+    for c in others:
+        send_x(c, "XA", 0, 0)
+    fold_x("XA", 0, 0)
+
+    def emat(k, a, b):
+        ts(T.EE[:, 144 * k:144 * k + 144], T.CI[:, 0:144], col(a), col(b), A.is_equal, A.mult, ["CI", "c%d" % a, "c%d" % b], ["E%d" % k])
+
+    def weight(k, a):
+        ts(col(k), T.OH[:, a:a + 1], 64.0, T.OH[:, a + 8:a + 9], A.mult, A.add, ["OH"], ["c%d" % k])
+
+    def consts2():
+        ts(T.T2[:, 0:160], T.CG[:], col(9), T.OH[:, 0:1], A.is_equal, A.mult, ["CG", "c9", "OH"], ["T2"])
+        ts(col(11), col(1), 4096.0, None, A.add, None, ["c1"], ["c11"])
+        tt(T.T1[:, 0:160], T.T1[:, 0:160], T.T2[:, 0:160], A.subtract, ["T1", "T2"], ["T1"])
+        ts(T.BC[:], T.BC[:], T.OH[:, 0:1], None, A.mult, None, ["BC", "OH"], ["BC"])
+        for z in range(2):
+            ts(T.LZ[:, 160 * z:160 + 160 * z], T.T1[:, 0:160], col(7 - z), None, A.mult, None, ["T1", "c6", "c7"], ["LZ%d" % z])
+        ts(T.DUMP[:], T.CI[:, 0:16], 16.0, col(11), A.mult, A.add, ["CI", "c11"], ["DUMP"])
+        ts(col(12), T.OH[:, 0:1], 255.0, 1.0, A.mult, A.add, ["OH"], ["c12"])
+        ts(T.NK[:, 3072:3584], T.SW[:, 0:512], col(5), -1.0, A.add, A.mult, ["SW0", "c5"], ["NKb"])
+
+    def consts3():
+        ts(col(3), col(2), 15.0, None, A.add, None, ["c2"], ["c3"])
+        ts(T.PI[:, 3:4], T.PI[:, 0:1], 112.0, None, A.add, None, ["PI0"], ["PI3"])
+        ts(col(14), T.OH[:, 0:1], -17.0, 1.0, A.mult, A.add, ["OH"], ["c14"])
+        ts(T.PI[:, 3:4], T.PI[:, 3:4], 127, None, A.bitwise_and, None, ["PI3"], ["PI3"])
+        emat(4, 3, 14)
+        cp(col(13), T.PI[:, 3:4], ["PI3"], ["c13"])
+        cp(T.ID[:], T.IDF[:], ["IDF"], ["ID"])
+        ts(T.NSH[:], T.CI[:, 0:128], col(13), -1.0, A.is_equal, A.mult, ["CI", "c13"], ["NSH"])
+
+    def places():
+        op("pool", lambda: g.iota(T.WG[:], [[0, 64], [1, 64]], 0, 1, allow_small_or_imprecise_dtypes=True), [], ["WGg"])
+        op("pool", lambda: g.iota(T.G2[:], [[1, 64], [0, 64]], 0, 0, allow_small_or_imprecise_dtypes=True), [], ch("G2"))
+        for row in (4, 5):
+            dma("sp", T.WG[row::16, :], T.G2[row::16, :], ch("G2") + ["WGg"], ["WGr%d" % row])
+
+    def own_rows():
+        ts(T.TI[:], T.P4[:, 0:8, :, :], 2048.0, None, A.add, None, ["P4"], ["TI"])
+        weight(15, 0)
+        ts(T.TJ[:], T.TI[:], 6, None, A.logical_shift_right, None, ["TI"], ["TJ"])
+        ts(T.KI[:], T.TI[:], 63, None, A.bitwise_and, None, ["TI"], ["KI"])
+        cp(T.HL[:, 0:256], T.TJ[:], ["TJ"], ["HL0"])
+        cp(T.HL[:, 256:512], T.KI[:], ["KI"], ["HL1"])
+        for row, k in ((0, 0), (8, 1)):
+            dma("sp", T.WG[row::16, :], T.HL[:, 256 * k:256 * k + 256], ["HL%d" % k, "WGg"], ["WGr%d" % row])
+        ts(T.B16[:], T.DUMP[:], -4096.0, 1.0 / 256, A.add, A.mult, ["DUMP"], ["B16"])
+        emat(0, 3, 15)
+        ts(T.LW[:, 0:256], T.CI[:], 16.0, col(1), A.mult, A.add, ["CI", "c1"], ["LW.0"])
+
+    def consts5():
+        ts(T.QI[:], T.IDF[:], 0.25, None, A.mult, None, ["IDF"], ["QI"])
+        ms(T.CM[:], -0.375, ["CM"])
+        ts(col(4), col(13), col(1), 15.0, A.subtract, A.add, ["c13", "c1"], ["c4"])
+        weight(16, 4)
+        weight(17, 5)
+        weight(21, 2)
+        ts(col(19), col(2), 12.0, None, A.add, None, ["c2"], ["c19"])
+        ts(col(20), col(0), -1.0, None, A.add, None, ["c0"], ["c20"])
+        ts(col(18), col(17), col(16), 6.0, A.subtract, A.mult, ["c16", "c17"], ["c18"])
+        emat(1, 4, 21)
+        emat(2, 3, 16)
+        emat(3, 3, 18)
+        ts(T.T1[:, 0:128], T.CI[:, 0:128], col(20), col(5), A.is_equal, A.mult, ["CI", "c20", "c5"], ["T1"])
+        ts(T.S2[:], T.CI[:, 0:128], col(3), T.OH[:, 0:1], A.is_equal, A.mult, ["CI", "c3", "OH"], ["S2"])
+        tt(T.S1[:], T.T1[:, 0:128], T.IDF[:], A.subtract, ["T1", "IDF"], ["S1"])
+        ts(T.MH[:, 256:257], col(0), 0.0, -8192.0, A.mult, A.add, ["c0"], ["MHe"])
+        ts(T.I16[:], T.IDF[:], 1.0 / 64, None, A.mult, None, ["IDF"], ["I16"])
+        ts(T.I8[:], T.IDF[:], 1.0 / 32, None, A.mult, None, ["IDF"], ["I8"])
+        cp(T.RB[:, 1:6], T.RHO[:, 0:5], ["RHO"], ["RBa"])
+        cp(T.RB[:, 0:1], T.RHO[:, 1:2], ["RHO"], ["RBb"])
+        rt = ["RT1.%d" % a for a in range(9)]
+        for a in range(9):
+            s = abs(a - 4)
+            ts(T.RT[:, 64 + 6 * a:70 + 6 * a], T.RB[:, 0:6], T.RHO[:, s:s + 1], None, A.mult, None, ["RBa", "RBb", "RHO"], [rt[a]])
+        ts(T.RT[:, 0:54], T.RT[:, 64:118], 128.0, None, A.mult, None, rt, ["RT0"])
+        ts(T.RT[:, 128:182], T.RT[:, 64:118], 1.0 / 128, None, A.mult, None, rt, ["RT2", "RT1"])
+
+    def KK(u):
+        return 2.0 ** (20 * u - 50)
+
+    def chain(Wa, Wr, wkey, u, gap=(None, None, None)):
+        op("dve", lambda: V_.tensor_tensor_scan(T.TOP[:, 1:257], Wa, T.ZR[:], 0.0, A.max, A.max), [wkey, "ZR"], ["TOP"])
+        ts(T.R16[:, 0:16], T.OH[:], T.TOP[:, 256:257], None, A.mult, None, ["OH", "TOP"], ["Ra"])
+        mm(T.PD[:, 0:16], T.GL[:], T.R16[:, 0:16], True, True, ["GL", "Ra"], ["PD"])
+        if gap[0]:
+            gap[0]()
+        red(T.CA[:, 0:1], T.PD[:, 0:16], A.max, ["PD"], ["CA0"])
+        ts(T.EX[:], T.TOP[:, 0:256], T.CA[:, 0:1], None, A.max, None, ["TOP", "TOP0", "CA0"], ["EX"])
+        tt(T.MM[:], T.EX[:], Wa, A.is_ge, ["EX", wkey], ["MM"])
+        op("dve", lambda: V_.tensor_tensor_scan(T.NN[:, 255::-1], T.MM[:, ::-1], Wr, 4096.0, A.mult, A.max), ["MM", wkey], ["NN"])
+        ts(T.R16[:, 16:32], T.OH[:], T.NN[:, 0:1], None, A.mult, None, ["OH", "NN"], ["Rb"])
+        mm(T.PD[:, 0:16], T.IDF[:], T.BIGM[:], True, False, ["IDF", "BIGM"], ["PD"])
+        mm(T.PD[:, 0:16], T.GU[:], T.R16[:, 16:32], False, True, ["GU", "Rb"], ["PD"])
+        ts(T.NN[:, 0:1], T.NN[:, 0:1], col(5), None, A.mult, None, ["NN", "c5"], ["NN"])
+        if gap[1]:
+            gap[1]()
+        red(T.CA[:, 1:2], T.PD[:, 0:16], A.min, ["PD"], ["CA1"])
+        ts(T.NH[:], T.NN[:, 0:256], T.CA[:, 1:2], -2048.0, A.min, A.add, ["NN", "CA1"], ["NH"])
+        ts(T.FF[:, 0:17], T.NN[:, 0:257:16], T.CA[:, 1:2], None, A.min, None, ["NN", "NNe", "CA1"], ["FF"])
+        op("dve", lambda: V_.transpose(T.TR[:], T.NH[:]), ["NH"], ["TR"])
+        regroup(0, "LZ")
+        tt(T.FA[:, 0:16], T.FF[:, 0:16], T.FF[:, 1:17], A.is_ge, ["FF"], ["FA0"])
+        tt(T.FA[:, 16:32], T.FA[:, 0:16], T.DUMP[:], A.mult, ["FA0", "DUMP"], ["FA1"])
+        tt(T.FA[:, 32:48], T.FA[:, 16:32], T.FF[:, 0:16], A.max, ["FA1", "FF"], ["FA2"])
+        cp(T.SO[:], T.FA[:, 32:48], ["FA2"], ["SO"])
+        tt(T.SRC[:], T.BC[:], T.P4[:, 0:8, :, :], A.add, ["BC", "P4"], ["SRC"])
+        if gap[2]:
+            gap[2]()
+        ts(T.SW[:].indirect(T.SO[:]), T.SRC[:], KK(u), 0.0, A.mult, A.add, ["SO", "SRC"], ["SW", "SW0", "SW1", "SW2", "SW3"])
+
+    def wr_pass(bank, e, src, skey, c):
+        for i in range(16):
+            mm(o4(T[bank], c), T.EE[:, 144 * e + 15 - i:144 * e + 143 - i], src[:, 1024 * c + i:1024 * c + 1024:16], i == 0, i == 15,
+               ["E%d" % e] + skey, [bank])
+
+    def b_pass(e, src, skey, c):
+        for i in range(4 * c, 4 * c + 4):
+            mm(T.PA[:, 0:256], T.EE[:, 144 * e + 15 - i:144 * e + 143 - i], src[:, 256 * i:256 * i + 256], i == 0, i == 15,
+               ["E%d" % e, "%s.%d" % (skey, c)], ["PA"])
+
+    def sweep(u, evac, pe_more=None):
+        for s in range(8):
+            a = slice(512 * s, 512 * s + 512)
+            ini = 0.0 if s == 0 else T.ST[:, 512 * s - 1:512 * s]
+            op("dve", lambda: V_.tensor_tensor_scan(T.ST[:, a], T.NK[:, 512 * u:512 * u + 512], T.SW[:, a], ini, A.add, A.max),
+               ["SW", "NK%d" % u] + (["ST.%d" % (s - 1)] if s else []), ["ST.%d" % s])
+            op("act", lambda: S_.activation(T.RR[:, a], T.ST[:, a], AF.Relu, bias=col(12), scale=-1.0 / KK(u)), ["ST.%d" % s, "c12"], ["RR.%d" % s])
+            if s % 2:
+                c = s // 2
+                wr_pass("PB" if c < 2 else "P1", 4, T.RR, ["RR.%d" % (s - 1), "RR.%d" % s], c)
+                if pe_more:
+                    pe_more(c)
+            if s == 5:
+                evac(0)
+        evac(1)
+
+    def evac_i(h):
+        a = slice(128 * h, 128 * h + 128)
+        b = "PB" if h == 0 else "P1"
+        ts(T.IN[:, a], T[b][:, a], MAG + 4096, MAG, A.add, A.subtract, [b], ["IN.%d" % h])
+
+    def evac_m(t):
+        def f(h):
+            a = slice(128 * h, 128 * h + 128)
+            b = "PB" if h == 0 else "P1"
+            ts(T.MO[:, a], T[b][:, a], MAG + 2048, MAG, A.add, A.subtract, [b], ["MO.%d" % h])
+            trs = []
+            for q in others:
+                o = 768 * t + 256 * ((r - q) % N - 1) + 128 * h
+                trs.append(([T.cores[q]], m_near if q in near else m_half[far.index(q)], "m%d_%d" % (t, h), [T.MO[:, a]], [T.ML[:, o:o + 128]], 0))
+            send(trs, ["MO.%d" % h], ["fold"])
+            arrive("m%d_%d" % (t, h), n_near * len(near) + n_far, ["ML%d.%d" % (t, h)])
+        return f
+
+    ring, jk = [0], [0]
+
+    def score(q, t, tr, j, n):
+        if n == 2:
+            ring[0] += ring[0] % 2
+        k = ring[0] % 4
+        ring[0] += n
+        B, o, keys = T["P%d" % (k // 2)], 512 * (k % 2), ["P0", "P5", "P1", "P6"][k:k + n]
+        base = (0 if t % 2 == 0 else 4 * W) if tr == 0 else tr * W
+        key = ("XA" if t % 2 == 0 else "XB") if tr == 0 else "T%d" % tr
+        for i in range(n):
+            a = 512 * (j + i)
+            out = B[:, o + 512 * i:o + 512 * i + 512]
+            mm(out, T.ID[:], T.GX[:, base + a:base + a + 512], True, False, ["ID", "%s.%d" % (key, j // 2)], [keys[i]])
+            mm(out, T.NSH[:], T["M%d" % (t % 2)][:, a:a + 512], False, True, ["NSH", "M%d.%d" % (t % 2, j // 2)], [keys[i]])
+        acc = T.ACC[:, 8 * tr + j:8 * tr + j + 1]
+        if q == "act":
+            jk[0] += 1
+            z = 1024 * (jk[0] % 2)
+            op("act", lambda: S_.activation(T.JK[:, z:z + 512 * n], B[:, o:o + 512 * n], AF.Abs, accum_out=acc), keys, ["JK%d" % z, "A%d.%d" % (tr, j)])
+        else:
+            red(acc, B[:, o:o + 512 * n], A.add, keys, ["A%d.%d" % (tr, j)], apply_absolute_value=True)
+
+    def trial(q, t, tr, c):
+        xb, X = (0, "XA") if t % 2 == 0 else (4 * W, "XB")
+        off, k = ((T.EU, "EU"), (T.GN, "GN"), (T.IN, "IN.%d" % (c // 2)))[tr - 1]
+        gat(q, c4(T.GX, c, tr * W), T.GX[:, xb:xb + W], o4(off, c), ch(X) + [k], ["T%d.%d" % (tr, c)])
+
+    def tsum(tr):
+        red(T.SC[:, tr:tr + 1], T.ACC[:, 8 * tr:8 * tr + 8], A.add, ["A%d.%d" % (tr, j) for j in range(8)], ["SC%d" % tr])
+
+    def scores(t, extra, pre, na, nd):
+        left = [(tr, c) for tr in (1, 2, 3) for c in range(4)][pre:]
+        for tr, c in left[:na]:
+            trial("act", t, tr, c)
+        for k, (tr, c) in enumerate(left[na:]):
+            if k < len(extra):
+                extra[k]()
+            trial("dve", t, tr, c)
+        cp(T.LW[:, 768:1024], T.IN[:], ["IN.0", "IN.1"], ["LW.3"])
+        todo = [(1, c) for c in others] + [(0, c) for c in order] + [(1, r)] + [(tr, c) for tr in (2, 3) for c in range(4)]
+        nw = 16 - nd
+        for tr, c in todo[:nw]:
+            score("act", t, tr, 2 * c, 2)
+        tsum(0)
+        tsum(1)
+        for tr, c in todo[nw:]:
+            score("dve", t, tr, 2 * c, 1)
+            score("act", t, tr, 2 * c + 1, 1)
+        tsum(2)
+        tsum(3)
+
+    def elect(t):
+        mm(T.PD[:, 0:4], T.GM4[:], T.SC[:], True, True, ["GM4"] + ["SC%d" % k for k in range(4)], ["PD"])
+        tt(T.KY[:], T.CI[:, 0:4], T.PD[:, 0:4], A.add, ["CI", "PD"], ["KY"])
+        red(T.EL[:, 0:1], T.PD[:, 0:4], A.min, ["PD"], ["EL0"])
+        red(T.EL[:, 1:2], T.KY[:], A.min, ["KY"], ["EL1"])
+        tt(T.EL[:, 2:3], T.EL[:, 1:2], T.EL[:, 0:1], A.subtract, ["EL0", "EL1"], ["EL2"])
+        ts(T.CS[:], T.B16[:], T.EL[:, 2:3], 256.0, A.add, A.mult, ["B16", "EL2"], ["CS"])
+        gat("dve", T.CU[:], T.LW[:], T.CS[:], ch("LW") + ["CS"], ["CU"])
+        wk = ["WGg"] + ["WGr%d" % k for k in (0, 8, 4, 5)]
+        for c in range(4):
+            gat("dve" if c % 2 == 0 else "act", c4(T.G1, c), T.WG[:], o4(T.CU, c), wk + ["CU"], ["G1.%d" % c])
+            b_pass(0, T.G1, "G1", c)
+        if t < 2:
+            send_g(t + 1)
+        dma("sp", T.G1[5::8, 0:W - 1], T.G1[4::8, 1:W], [], ch("G1"))
+        if t < 2:
+            dma("sp", T.G1[2::8, :], T.HN[:, 512 * t:512 * t + 512], ["HN%d" % (t + 1)], ch("G1"))
+            dma("sp", T.LW[:, 256:512], T.ew[:, 256 * t + 256:256 * t + 512], [], ["LW.1"])
+
+    def clear_sums():
+        ms(T.ACC[:], 0.0, ["A%d.%d" % (tr, j) for tr in range(4) for j in range(8)])
+
+    def window_base(t):
+        clear_sums()
+        if t % 2 == 0:
+            ts(T.EL[:, 4:5], T.EL[:, 2:3], -4096.0, MAG, A.mult, A.add, ["EL2"], ["EL4"])
+        else:
+            ts(T.EL[:, 3:4], T.EL[:, 2:3], 0.0, 4.0, A.is_equal, A.mult, ["EL2"], ["EL3"])
+            ts(T.EL[:, 3:4], T.EL[:, 3:4], T.EL[:, 2:3], -4096.0, A.add, A.mult, ["EL2", "EL3"], ["EL3"])
+            ts(T.EL[:, 4:5], T.EL[:, 3:4], MAG + 4096, None, A.add, None, ["EL3"], ["EL4"])
+
+    def mean(t, h):
+        a = slice(128 * h, 128 * h + 128)
+        b = "PD" if h == 0 else "P0"
+        mm(T[b][:, a], T.ID[:], T.CM[:], True, False, ["ID", "CM"], [b])
+        mm(T[b][:, a], T.QI[:], T.MO[:, a], False, False, ["QI", "MO.%d" % h], [b])
+        for k in range(3):
+            o = 768 * t + 256 * k + 128 * h
+            mm(T[b][:, a], T.QI[:], T.ML[:, o:o + 128], False, k == 2, ["QI", "ML%d.%d" % (t, h)], [b])
+        ts(T.MU[:, a], T[b][:, a], MAG + 2048, MAG, A.add, A.subtract, [b], ["MU.%d" % h])
+        ts(T.MX[:, a], T[b][:, a], MAG + 2048, T.EL[:, 4:5], A.add, A.subtract, [b, "EL4"], ["MX.%d" % h])
+
+    def gamma_mu(q, c):
+        gat(q, c4(T.G2, c), T.G1[:], o4(T.MU, c), ch("G1") + ["MU.%d" % (c // 2)], ["G2.%d" % c])
+
+    def x_new(t, c, q="act"):
+        wb, xb, X, Xo = (0, 4 * W, "XB", "XA") if t % 2 == 0 else (W, 0, "XA", "XB")
+        gat(q, c4(T.GX, c, xb), T.GX[:, wb:wb + 4 * W], o4(T.MX, c), ch(Xo) + ch("T1") + ch("T2") + ch("T3") + ["MX.%d" % (c // 2)], ["%s.%d" % (X, c)])
+        if c != r:
+            send_x(c, X, xb, t + 1)
+
+    def fold_new(t):
+        fold_x("XB" if t % 2 == 0 else "XA", 4 * W if t % 2 == 0 else 0, t + 1)
+
+    def full_pass(bank, e):
+        for c in range(4):
+            wr_pass(bank, e, T.G2, ["G2.%d" % c], c)
+
+    def slope_mu(bm):
+        ts(T.MH[:, 0:256], T.MU[:], -2048.0, None, A.add, None, ["MU.0", "MU.1"], ["MH"])
+        mm(T[bm][:, 0:256], T.S1[:], T.MH[:, 0:256], True, False, ["S1", "MH"], [bm])
+        mm(T[bm][:, 0:256], T.S2[:], T.MH[:, 1:257], False, True, ["S2", "MH", "MHe"], [bm])
+
+    def slopes(bd, bs, bm):
+        ts(T.DU[:], T[bd][:, 0:256], col(19), None, A.subtract, None, [bd, "c19"], ["DU"])
+        ts(T.T1[:], T[bs][:, 0:256], -24.0, 24.0, A.max, A.min, [bs], ["T1"])
+        ts(T.T2[:], T[bm][:, 0:256], -1.0, 4.0, A.max, A.min, [bm], ["T2"])
+        tt(T.T1[:], T.T1[:], T.T2[:], A.add, ["T1", "T2"], ["T1"])
+        ts(T.IX[:], T.T1[:], 25.0, None, A.add, None, ["T1"], ["IX"])
+
+    def v_gather(t, c):
+        win, k = (T.PAY, ["PAY"]) if t == 0 else (T.V, ch("V"))
+        gat("act", c4(T.VD, c), win[:], o4(T.DU, c), k + ["DU"], ["VD.%d" % c])
+
+    def v_mult(t, c):
+        out, k = (T.V, "V") if t < 2 else (T.VD, "VD")
+        tt(c4(out, c), T.RT[:, 64 * t:64 * t + 54].indirect(o4(T.IX, c)), c4(T.VD, c), A.mult, ["RT%d" % t, "IX", "VD.%d" % c], ["%s.%d" % (k, c)])
+        if t < 2:
+            dma("pool", c4(T.V, c), c4(T["M%d" % ((t + 1) % 2)], c), ["M%d.%d" % ((t + 1) % 2, c)], ["V.%d" % c], accum_op=A.add)
+
+    def nk_tiles(us):
+        for u in us:
+            op("act", lambda: S_.activation(T.NK[:, 512 * u:512 * u + 512], T.NK[:, 3072:3584], AF.Copy, scale=KK(u)), ["NKb"], ["NK%d" % u])
+
+    clear_sums()
+    cp(T.EU[:], T.LW[:, 256:512], ["LW.1"], ["EU"])
+    consts2()
+    nk_tiles([0])
+    for c in range(4):
+        trial("act", 0, 1, c)
+    to_blocks(T.LW[:, 512:768], "LW.2")
+    cp(T.GN[:], T.LW[:, 512:768], ["LW.2"], ["GN"])
+    for c in range(PRE0 - 4):
+        trial("act", 0, 2, c)
+    ts(T.WB[:], T.P4[:, 0:8, :, :], 2048.0, None, A.add, None, ["P4"], ["WB"])
+    chain(T.WB[:], T.WB[:, ::-1], "WB", 0, (consts3, None, None))
+    places()
+    dma("sp", T.RHO[:, 0:5], T.rho[:], [], ["RHO"])
+    dma("act", T.PAY[:], T.pay[:], ["SO"], ["PAY"])
+    sweep(0, evac_i)
+
+    for t in range(3):
+        if t == 0:
+            scores(t, [lambda: to_blocks(T.GA[:], "GA"), own_rows], PRE0, NA0, ND0)
+        else:
+            scores(t, [lambda: None, lambda: slopes("PA", "PD", "PB")], PRE, NA, ND)
+            v_gather(t - 1, 0)
+        elect(t)
+        if t > 0:
+            for c in range(1, 4):
+                v_gather(t - 1, c)
+        else:
+            nk_tiles(range(1, 6))
+            op("act", lambda: S_.activation(T.PAY[:], T.PAY[:], AF.Copy, scale=0.25), ["PAY"], ["PAY"])
+        chain(T.PA[:, 0:256], T.PA[:, 255::-1], "PA", 2 * t + 1, (lambda: window_base(t), None, None))
+        sweep(2 * t + 1, evac_m(t))
+        if t == 0:
+            consts5()
+        else:
+            v_mult(t - 1, 0)
+            v_mult(t - 1, 1)
+        if t == 2:
+            break
+        first = [c for c in others if c < 2] + [c for c in others if c >= 2]
+        mean(t, 0)
+        gamma_mu("dve", 0)
+        x_new(t, first[0])
+        gamma_mu("dve", 1)
+        mean(t, 1)
+        gamma_mu("dve", 2)
+        for k in range(1, 5):
+            if k == GA3:
+                gamma_mu("act", 3)
+            if k < 4:
+                x_new(t, (first + [r])[k])
+        if not GA3:
+            gamma_mu("dve", 3)
+        fold_new(t)
+        for c in range(4):
+            b_pass(1, T.G2, "G2", c)
+            if c < 2:
+                wr_pass("PB", 1, T.G2, ["G2.%d" % c], c)
+        dma("sp", T.WG[0::8, :], T.G2[0::8, :], ch("G2"), ["WGr0", "WGr8"])
+
+        def gap0():
+            wr_pass("PB", 1, T.G2, ["G2.2"], 2)
+            wr_pass("PB", 1, T.G2, ["G2.3"], 3)
+            cp(T.EU[:], T.LW[:, 256:512], ["LW.1"], ["EU"])
+            for c in range(min(PRE, 4)):
+                trial("act", t + 1, 1, c)
+
+        def gap1():
+            cp(T.GN[:], T.PB[:, 0:256], ["PB"], ["GN"])
+            for c in range(PRE - 4):
+                trial("act", t + 1, 2, c)
+
+        def gap2():
+            full_pass("PA", 2)
+        chain(T.PA[:, 0:256], T.PA[:, 255::-1], "PA", 2 * t + 2, (gap0, gap1, gap2))
+        cp(T.LW[:, 512:768], T.GN[:], ["GN"], ["LW.2"])
+        sweep(2 * t + 2, evac_i, lambda c: wr_pass("PD", 3, T.G2, ["G2.%d" % c], c))
+        slope_mu("PB")
+        if t > 0:
+            v_mult(t - 1, 2)
+            v_mult(t - 1, 3)
+
+    mean(2, 0)
+    gamma_mu("act", 0)
+    gamma_mu("act", 1)
+    v_mult(1, 2)
+    mean(2, 1)
+    gamma_mu("act", 2)
+    gamma_mu("act", 3)
+    v_mult(1, 3)
+    for c in range(4):
+        wr_pass("PA", 2, T.G2, ["G2.%d" % c], c)
+        wr_pass("PB", 3, T.G2, ["G2.%d" % c], c)
+        wr_pass("PD", 0, T.G2, ["G2.%d" % c], c)
+    x_new(2, far[0], "dve")
+    slope_mu("P1")
+    x_new(2, far[1], "dve")
+    x_new(2, near[0])
+    x_new(2, r)
+    slopes("PA", "PB", "P1")
+    cp(T.GO[:], T.PD[:, 0:256], ["PD"], ["GO"])
+    last = far + near + [r]
+    fold_new(2)
+    for c in last:
+        v_gather(2, c)
+    for k, c in enumerate(near + [r]):
+        gat("act", c4(T.RR, k), T.PAY[:], o4(T.GO, c), ["PAY", "GO"], ["RR.%d" % (2 * k), "RR.%d" % (2 * k + 1)])
+    for c in last:
+        v_mult(2, c)
+        slot = c4(T.LU, (r - c) % N - 1)
+        if c in far:
+            keys = ["ST.%d" % (2 * c), "ST.%d" % (2 * c + 1)]
+            tt(c4(T.ST, c), T.PAY[:].indirect(o4(T.GO, c)), c4(T.VD, c), A.add, ["PAY", "GO", "VD.%d" % c], keys)
+            send([([T.cores[c]], m_far, "u%d" % r, [c4(T.ST, c)], [slot], 0)], keys)
+        elif c in near:
+            send([([T.cores[c]], m_near, "u%d" % r, [c4(T.VD, c)], [slot], 0)], ["VD.%d" % c])
+            send([([T.cores[c]], m_near, "p", [c4(T.RR, 0)], [T.HN[:]], 0)], ["RR.0", "RR.1"])
+    arrive("p", n_near, ["HP"])
+    for q in others:
+        arrive("u%d" % q, nk(q), ["LU.%d" % ((q - r) % N - 1)])
+    late = [q for q in far if [c for c in [(q + k) % N for k in range(1, N)] if topo.chip(T.cores[c]) != topo.chip(T.cores[q])][1] == r]
+    tail = (late + far)[0]
+    lu = [(q - r) % N - 1 for q in [c for c in far if c != tail] + near + [tail]]
+    parts = [(T.I16, T.GX, 4 * W + 1024 * r, ["I16", "XB.%d" % r])] + [(T.I16, T.LX, 1024 * k, ["I16", "LX"]) for k in range(3)]
+    parts += [(T.ID, T.RR, 1024, ["ID", "RR.2", "RR.3"]), (T.IDF, T.VD, 1024 * r, ["IDF", "VD.%d" % r]), (T.I8, T.LX, 3072, ["I8", "MF"]),
+              (T.IDF, T.LU, 1024 * lu[0], ["IDF", "LU.%d" % lu[0]]), (T.ID, T.HN, 0, ["ID", "HP"]), (T.IDF, T.LU, 1024 * lu[1], ["IDF", "LU.%d" % lu[1]])]
+    for k, (l, src, o, keys) in enumerate(parts):
+        for h in range(2):
+            mm(T.P0[:, 512 * h:512 * h + 512], l[:], src[:, o + 512 * h:o + 512 * h + 512], k == 0, k == len(parts) - 1, keys, [("P0", "P5")[h]])
+    for h in range(2):
+        a = slice(512 * h, 512 * h + 512)
+        o = 1024 * lu[2] + 512 * h
+        tt(T.SW[:, a], T.LU[:, o:o + 512], T.P0[:, a], A.add, ["LU.%d" % lu[2], ("P0", "P5")[h]], [("SW", "Y1")[h]])
+        dma(("sp", "act")[h], T.y[:, a], T.SW[:, a], [("SW", "Y1")[h]], ["y%d" % h])
+    for s in cnt:
+        wait("pool", (s, cnt[s]))

@@ -2,9 +2,11 @@ from concourse.bass import DstId, RemoteDMATransfer
 from concourse.mybir import AluOpType as A, AxisListType, ActivationFunctionType as AF
 
 W = 4096
-PRE0, NA0, ND0, PRE, NA, ND, GA3 = 6, 0, 3, 3, 1, 2, 0
 MAG = 12582912.0
 F32, BF, F16, I32, U16 = "float32", "bfloat16", "float16", "int32", "uint16"
+NKW = 1024
+XD, MK, RAW, DA, RAW0, DA0, PZ0 = 1, 1, 3, 3, 2, 4, 2
+FOLDED = ()
 
 
 def _sb(n, d):
@@ -12,31 +14,34 @@ def _sb(n, d):
 
 
 SCRATCH = {
-    "GX": _sb(5 * W, BF), "M0": _sb(W, BF), "M1": _sb(W, BF), "LX": _sb(W, BF),
-    "V": _sb(W, F32), "VD": _sb(W, F32), "PAY": _sb(W, BF),
+    "X": _sb(W, BF), "XP": _sb(W, BF), "MP": _sb(W, BF), "MS": _sb(W, BF), "MR": _sb(W, BF), "LX": _sb(6144, BF), "D": _sb(2 * W, BF),
+    "V": _sb(W, F32), "VD": _sb(W, F32), "PZ": _sb(W, F32), "PAY": _sb(W, BF),
     "WG": _sb(W, BF), "G1": _sb(W, BF), "G2": _sb(W, BF),
-    "SW": _sb(W + 256, F32), "ST": _sb(W, F32), "RR": _sb(W, BF), "JK": _sb(2048, BF),
-    "LU": _sb(3072, F32), "NK": _sb(7 * 512, BF),
+    "SW": _sb(W + 256, F32), "ST": _sb(W, F32), "RR": _sb(W, BF),
+    "NK": _sb(2 * NKW, BF),
     "PI": _sb(4, I32), "KI": _sb(256, I32), "TI": _sb(256, I32), "TJ": _sb(256, I32), "GS": _sb(256, I32), "GA": _sb(256, I32),
+    "EI": _sb(256, I32), "LO": _sb(256, U16),
     "CI": _sb(256, F32), "CG": _sb(160, F32), "CO": _sb(32, F32), "OH": _sb(16, F32), "T1": _sb(256, F32), "T2": _sb(256, F32),
-    "EE": _sb(5 * 144, BF), "ID": _sb(128, BF), "NSH": _sb(128, BF), "I16": _sb(128, BF), "I8": _sb(128, BF), "CM": _sb(128, BF),
-    "IDF": _sb(128, F32), "GM4": _sb(128, F32), "GL": _sb(128, F32), "GU": _sb(128, F32), "BIGM": _sb(16, F32),
+    "EE": _sb(6 * 144, BF), "ID": _sb(128, BF), "NID": _sb(128, BF), "ID2": _sb(128, BF), "I32": _sb(128, BF), "CM": _sb(128, BF),
+    "IDF": _sb(128, F32), "GM4": _sb(128, F32), "KC": _sb(8, F32),
     "QI": _sb(128, F16), "LZ": _sb(4 * 160, F16), "S1": _sb(128, F16), "S2": _sb(128, F16),
-    "BC": _sb(256, F32), "DUMP": _sb(16, F32), "B16": _sb(16, F32), "ZR": _sb(256, F32), "PO": _sb(16, U16),
-    "TOP": _sb(260, F32), "EX": _sb(256, F32), "MM": _sb(256, F32), "NN": _sb(260, F32), "R16": _sb(32, F32), "CA": _sb(8, F32),
+    "BC": _sb(256, F32), "DUMP": _sb(16, F32), "B64": _sb(16, F32), "ZR": _sb(256, F32), "PO": _sb(16, U16),
+    "TOP": _sb(260, F32), "EX": _sb(256, F32), "MM": _sb(256, F32), "NN": _sb(260, F32),
+    "TA": _sb(72, F32), "TB": _sb(64, F32), "TC": _sb(64, F32), "MK": _sb(64, F32),
     "NH": _sb(256, F16), "TR": ("sbuf", [128, 8, 2, 16], F16), "FF": _sb(20, F32), "FA": _sb(48, F32), "SO": _sb(16, U16), "SRC": _sb(256, F32),
-    "WB": _sb(256, F32), "HL": _sb(512, BF),
+    "HL": _sb(512, BF),
     "LW": _sb(1024, I32), "EU": _sb(256, U16), "GO": _sb(256, U16), "GN": _sb(256, U16), "IN": _sb(256, U16), "HT": _sb(512, BF), "HN": _sb(1024, BF),
-    "MO": _sb(256, F16), "ML": _sb(9 * 256, F16), "MU": _sb(256, U16), "MX": _sb(256, U16), "MH": _sb(264, F16),
-    "ACC": _sb(32, F32), "SC": _sb(4, F32), "KY": _sb(4, F32), "EL": _sb(8, F32), "CS": _sb(16, U16), "CU": _sb(256, U16),
+    "MO": _sb(256, F16), "ML": _sb(9 * 256, F16), "MU": _sb(256, U16), "MV": _sb(128, U16), "MH": _sb(264, F16),
+    "ACC": _sb(32, F32), "EL": _sb(8, F32), "CS": _sb(16, U16), "CU": _sb(256, U16),
     "DU": _sb(256, U16), "IX": _sb(256, U16), "RHO": _sb(8, F32), "RB": _sb(8, F32), "RT": _sb(192, F32),
     "PA": ("psum", [128, 512], F32), "PB": ("psum", [128, 512], F32), "PD": ("psum", [128, 512], F32),
     "P0": ("psum", [128, 1024], F32), "P1": ("psum", [128, 1024], F32),
     "P4": ("psum", [128, 16, 2, 16], F32),
 }
-REMOTE = (["g%d" % t for t in range(3)]
+REMOTE = (["g%d" % t for t in range(3)] + ["i"]
           + ["m%d_%d" % (t, h) for t in range(3) for h in range(2)] + ["x%d" % t for t in range(4)]
-          + ["b%d_%d" % (t, q) for t in range(4) for q in range(4)] + ["u%d" % q for q in range(4)] + ["p"])
+          + ["b%d_%d" % (t, q) for t in range(4) for q in range(4)] + ["u%d" % q for q in range(4)]
+          + ["s%d" % t for t in range(2)] + ["f%d_%d" % (e, tr) for e in (1, 2) for tr in range(2)])
 SEMAPHORES = ["pe", "dve", "act", "pool"] + ["r" + k for k in REMOTE] + ["q%d" % i for i in range(100)]
 
 
@@ -48,17 +53,31 @@ def _helper(core, T, topo):
     return [c for c in topo.cores_of(core) if topo.die(c) == topo.die(core) and T.rank_of(c) is None][0]
 
 
+def _folded(T, tr):
+    return T.MP[:] if tr == 0 else T.D[:, W:2 * W]
+
+
+def _parked(T, e, tr):
+    return (T.G1, T.G2, T.WG, T.XP)[2 * e - 2 + tr][:]
+
+
 def helper_program(g, core, owner, T, topo):
     rid, pid, _ = topo.addr(owner)
     r = T.rank_of(owner)
     m = topo.mask(core, owner)
     n = len(_bits(m))
     far = [c for c in T.cores if topo.chip(c) != topo.chip(owner)][0]
-    for t in range(4):
-        g.wait_ge(T.sem["rb%d_%d" % (t, r)], len(_bits(topo.mask(owner, core) & ~topo.mask(owner, far))))
-        dst = T.LX[:, 3072:4096] if t == 3 else T["M%d" % (t % 2)][:, 1024 * r:1024 * r + 1024]
-        g.remote_dma(dst, T.GX[:, 1024 * t:1024 * t + 1024], T.sem["rb%d_%d" % (t, r)], T.sem.q0, pid, rid, m)
-    g.wait_ge(T.sem.q0, 4 * n)
+    k = 0
+    for e in range(4):
+        g.wait_ge(T.sem["rb%d_%d" % (e, r)], len(_bits(topo.mask(owner, core) & ~topo.mask(owner, far))))
+        dst = (T.MP if e else T.MS)[:, 1024 * r:1024 * r + 1024]
+        g.remote_dma(dst, T.X[:, 1024 * e:1024 * e + 1024], T.sem["rb%d_%d" % (e, r)], T.sem.q0, pid, rid, m)
+        k += 1
+        for tr in (FOLDED if e in (1, 2) else ()):
+            g.wait_ge(T.sem["rf%d_%d" % (e, tr)], len(_bits(topo.mask(owner, core))))
+            g.remote_dma(_folded(T, tr), _parked(T, e, tr), T.sem["rf%d_%d" % (e, tr)], T.sem.q0, pid, rid, m)
+            k += 1
+    g.wait_ge(T.sem.q0, k * n)
 
 
 def rank_program(g, core, T, topo):
@@ -120,6 +139,17 @@ def rank_program(g, core, T, topo):
         cnt[s] = 16
         done((s, 16), rd, wr)
 
+    def dma2(q, pairs, rd, wr):
+        deps(q, rd, wr, False)
+        s = fresh()
+        for out, in_ in pairs:
+            Q[q].dma_start(out, in_).then_inc(T.sem[s], 16)
+        cnt[s] = 16 * len(pairs)
+        done((s, cnt[s]), rd, wr)
+
+    def back(out, in_):
+        return [(out[0:112], in_[16:128]), (out[112:128], in_[0:16])]
+
     def arrive(key, n, wr):
         cnt["r" + key] = n
         done(("r" + key, n), [], wr)
@@ -158,14 +188,23 @@ def rank_program(g, core, T, topo):
     def red(out, a, o, rd, wr, **kw):
         op("dve", lambda: V_.tensor_reduce(out, a, AxisListType.X, o, **kw), rd, wr)
 
+    def scan(out, d0, d1, ini, o0, o1, rd, wr):
+        op("dve", lambda: V_.tensor_tensor_scan(out, d0, d1, ini, o0, o1), rd, wr)
+
+    def turn(out, a, rd, wr):
+        op("dve", lambda: V_.transpose(out, a), rd, wr)
+
+    def act(out, a, f, rd, wr, **kw):
+        op("act", lambda: S_.activation(out, a, f, **kw), rd, wr)
+
     def mm(out, l, rhs, st, sp, rd, wr):
         op("pe", lambda: P_.matmul(out, l, rhs, st, sp), rd, wr)
 
     def gat(q, out, win, off, rd, wr):
         if q == "dve":
-            op(q, lambda: V_.tensor_copy(out, win.indirect(off)), rd, wr)
+            cp(out, win.indirect(off), rd, wr)
         else:
-            op(q, lambda: S_.activation(out, win.indirect(off), AF.Copy), rd, wr)
+            act(out, win.indirect(off), AF.Copy, rd, wr)
 
     def ch(name, cs=range(4)):
         return ["%s.%d" % (name, c) for c in cs]
@@ -176,16 +215,27 @@ def rank_program(g, core, T, topo):
     def o4(t, c, base=0):
         return t[:, base + 64 * c:base + 64 * c + 64]
 
+    def rows(t, a, b, c):
+        return t[a:b, 1024 * c:1024 * c + 1024]
+
+    BANK = {"PA": (T.PA, 0), "PB": (T.PB, 0), "PD": (T.PD, 0), "P0": (T.P0, 0), "P5": (T.P0, 512), "P1": (T.P1, 0), "P6": (T.P1, 512)}
+
+    def pb(b, a, n):
+        return BANK[b][0][:, BANK[b][1] + a:BANK[b][1] + a + n]
+
     others = [(r + k) % N for k in range(1, N)]
-    order = others + [r]
     far = [q for q in others if topo.chip(T.cores[q]) != topo.chip(core)]
     near = [q for q in others if q not in far]
+    last = far + near + [r]
+    side = int(r > near[0])
+    mine, theirs = [2 * side, 2 * side + 1], [2 - 2 * side, 3 - 2 * side]
     hc = _helper(core, T, topo)
     m_far = topo.mask(core, T.cores[far[0]])
     m_near = topo.mask(core, T.cores[near[0]]) & ~m_far
     fb = _bits(m_far)
     m_half = [sum(1 << e for e in fb[:len(fb) // 2]), sum(1 << e for e in fb[len(fb) // 2:])]
     n_far, n_near = len(fb), len(_bits(m_near))
+    N_X = 2 * n_far + n_near
     prev, nxt = (r - 1) % N, (r + 1) % N
 
     def mk(q):
@@ -194,12 +244,14 @@ def rank_program(g, core, T, topo):
     def nk(q):
         return n_far if q in far else n_near
 
-    dma("act", T.GS[0:112, :], T.gam[16:128, :], [], ["GSa"])
-    dma("sp", T.GS[112:128, :], T.gam[0:16, :], [], ["GSb"])
-    for c in order:
-        dma("sp", c4(T.GX, c), c4(T.xs, c), [], ["XA.%d" % c])
-    dma("act", T.LW[:, 256:512], T.ew[:, 0:256], [], ["LW.1"])
-    dma("act", T.GA[:], T.gam[:], [], ["GA"])
+    dma2("sp", back(T.GS, T.gam), [], ["GS"])
+    for c in last:
+        dma2("sp" if c in far else "act", [(rows(T.D, 0, 112, c), rows(T.xs, 16, 128, c)), (rows(T.D, 112, 128, c), rows(T.xs, 0, 16, c))], [], ["D.%d" % c])
+    dma("act", T.EI[:], T.ew[:, 0:256], [], ["EI"])
+    dma("sp", T.X[:], T.xs[:], [], ch("X"))
+    dma("sp", T.PAY[:], T.pay[:], ["X.0"], ["pay"])
+    dma("sp", T.GA[:], T.gam[:], [], ["GA"])
+    dma("sp", T.RHO[:, 0:5], T.rho[:], [], ["RHO"])
 
     op("pool", lambda: g.iota(T.PI[:, 0:1], [[0, 1]], 0, 1), [], ["PI0"])
     op("pool", lambda: g.iota(T.KI[:], [[1, 256]], 0, 0), [], ["KI"])
@@ -208,10 +260,17 @@ def rank_program(g, core, T, topo):
 
     def col(i):
         return CO[:, i:i + 1]
-    ms(T.SW[:, 0:1088], 0.0, ["SW0"])
-    for k in range(1, 4):
-        op("act", lambda: S_.activation(T.SW[:, 1088 * k:1088 * k + 1088], T.SW[:, 0:1088], AF.Copy), ["SW0"], ["SW%d" % k])
+    ms(T.SW[:, 0:272], 0.0, ["SW0"])
+    for k in range(4):
+        act(T.SW[:, 272 << k:544 << k], T.SW[:, 0:272 << k], AF.Copy, ["SW%d" % i for i in range(k + 1)], ["SW%d" % (k + 1)])
     ms(T.ZR[:], 0.0, ["ZR"])
+    ms(T.MK[:, 0:32], 1.0, ["MK"])
+    ms(T.MK[:, 32:64], 0.0, ["MK2"])
+    ms(T.TA[:], 0.0, ["TA0", "TA1"])
+    ms(T.MK[:, 0:32:16], 0.0, ["MK"])
+    ms(T.MK[:, 47:64:16], 4096.0, ["MK2"])
+    ms(T.TOP[:, 0:1], 0.0, ["TOP0"])
+    ms(T.NN[:, 256:257], 4096.0, ["NNe"])
     ts(T.PI[:, 1:2], T.PI[:, 0:1], 15, None, A.bitwise_and, None, ["PI0"], ["PI1"])
     ts(T.PI[:, 2:3], T.PI[:, 0:1], 16, None, A.bitwise_and, None, ["PI0"], ["PI2"])
     cp(T.CI[:], T.KI[:], ["KI"], ["CI"])
@@ -227,7 +286,7 @@ def rank_program(g, core, T, topo):
     ts(col(5), T.OH[:, 0:1], -1.0, 1.0, A.mult, A.add, ["OH"], ["c5"])
     ts(col(7), col(6), -1.0, 1.0, A.mult, A.add, ["c6"], ["c7"])
     ts(T.T1[:, 0:160], T.CI[:, 0:160], col(8), None, A.is_equal, None, ["CI", "c8"], ["T1"])
-    ts(T.PO[:], T.CI[:, 0:16], col(10), None, A.add, None, ["CI", "c10"], ["PO"])
+    ts(T.PO[:], T.CI[:, 0:16], col(10), None, A.add, None, ["CI", "c10"], ["po"])
     for z in range(2):
         ts(T.LZ[:, 320 + 160 * z:480 + 160 * z], T.T1[:, 0:160], col(7 - z), None, A.mult, None, ["T1", "c6", "c7"], ["LP%d" % z])
 
@@ -238,55 +297,55 @@ def rank_program(g, core, T, topo):
                 mm(T.P4[:, 0:8, z, :], T.LZ[:, o:o + 128], T.TR[:, :, gb, :], gb == 0, gb == 1, ["TR", key + str(z)], ["P4"])
 
     def to_blocks(src, key):
-        ts(T.NH[:], src.indirect(T.PO[:]), -2048.0, None, A.add, None, [key, "PO"], ["NH"])
-        op("dve", lambda: V_.transpose(T.TR[:], T.NH[:]), ["NH"], ["TR"])
+        ts(T.NH[:], src.indirect(T.PO[:]), -2048.0, None, A.add, None, [key, "po"], ["NH"])
+        turn(T.TR[:], T.NH[:], ["NH"], ["TR"])
         regroup(320, "LP")
 
-    send([([T.cores[prev]], mk(prev), "g0", [T.GS[:]], [T.LW[:, 512:768]], 0)], ["GSa", "GSb"])
-    arrive("g0", nk(nxt), ["LW.2"])
-    ts(T.T2[:, 0:128], T.CG[:, 0:128], col(2), None, A.is_equal, None, ["CG", "c2"], ["T2"])
-    ts(T.GL[:], T.CI[:, 0:128], col(0), None, A.is_gt, None, ["CI", "c0"], ["GL"])
-    ts(T.GU[:], T.CI[:, 0:128], col(0), None, A.is_lt, None, ["CI", "c0"], ["GU"])
-    tt(T.GL[:], T.GL[:], T.T2[:, 0:128], A.mult, ["GL", "T2"], ["GL"])
-    tt(T.GU[:], T.GU[:], T.T2[:, 0:128], A.mult, ["GU", "T2"], ["GU"])
-    ts(T.GM4[:], T.T2[:, 0:128], 4.0, None, A.mult, None, ["T2"], ["GM4"])
-    ts(T.IDF[:], T.CI[:, 0:128], col(0), None, A.is_equal, None, ["CI", "c0"], ["IDF"])
-    ts(T.BIGM[:], T.CI[:, 0:16], col(1), 4096.0, A.is_le, A.mult, ["CI", "c1"], ["BIGM"])
-    ms(T.TOP[:, 0:1], 0.0, ["TOP0"])
-    ms(T.NN[:, 256:257], 4096.0, ["NNe"])
+    def x_src(e, c):
+        return (c4(T.D, c), "D.%d" % c) if e < 3 else (c4(T.XP, c), "XP.%d" % c)
 
-    def send_x(c, X, xb, t):
-        send([([T.cores[c]], mk(c), "x%d" % t, [c4(T.GX, c, xb)], [c4(T.LX, (r - c) % N - 1)], 0)], ["%s.%d" % (X, c)])
+    def send_x(e, cs):
+        trs = []
+        for c in cs:
+            m = m_half[far.index(c)] if c in far and len(cs) > 1 else mk(c)
+            trs.append(([T.cores[c]], m, "x%d" % e, [x_src(e, c)[0]], [c4(T.LX, (r - c) % N - 1, 3072 * (e % 2))], 0))
+        send(trs, [x_src(e, c)[1] for c in cs], ["fold", "MR"])
 
-    def fold_x(X, xb, t):
-        arrive("x%d" % t, sum(nk(q) for q in others), ["LX"])
-        srcs = [c4(T.GX, r, xb)] + [c4(T.LX, k) for k in range(3)]
-        hb = T.GX[:, 1024 * t:1024 * t + 1024]
-        if t == 3:
-            send([([hc], m_near, "b3_%d" % r, srcs, [hb], 2)], ["LX", "%s.%d" % (X, r)])
-            arrive("b3_%d" % r, len(_bits(topo.mask(hc, core))), ["MF"])
-            return
-        Mb = T["M%d" % (t % 2)]
-        key = "b%d_%d" % (t, r)
+    def fold_x(e, n):
+        arrive("x%d" % e, n, ["LX"])
+        srcs = [x_src(e, r)[0]] + [c4(T.LX, k, 3072 * (e % 2)) for k in range(3)]
+        Mb, mkey = (T.MP, "MP") if e else (T.MS, "MS")
+        key = "b%d_%d" % (e, r)
         lastw["fold"] = send([([T.cores[q] for q in far], m_far, key, srcs, [c4(Mb, r)] * len(far), 2),
-                              ([hc] + [T.cores[q] for q in near], m_near, key, srcs, [hb] + [c4(Mb, r)] * len(near), 2)], ["LX", "%s.%d" % (X, r)])
+                              ([hc] + [T.cores[q] for q in near], m_near, key, srcs, [c4(T.X, e)] + [c4(Mb, r)] * len(near), 2)], ["LX", x_src(e, r)[1]])
         for q in range(N):
-            arrive("b%d_%d" % (t, q), len(_bits(topo.mask(hc, core))) if q == r else nk(q), ["M%d.%d" % (t % 2, q)])
+            arrive("b%d_%d" % (e, q), len(_bits(topo.mask(hc, core))) if q == r else nk(q), ["%s.%d" % (mkey, q)])
 
     def send_g(t):
         dma("sp", T.HT[:], T.G1[0::8, :], ch("G1"), ["HT"])
         send([([T.cores[prev]], mk(prev), "g%d" % t, [T.HT[:]], [T.HN[:, 512 * t - 512:512 * t]], 0)], ["HT"])
         arrive("g%d" % t, nk(nxt), ["HN%d" % t])
 
-    for c in others:
-        send_x(c, "XA", 0, 0)
-    fold_x("XA", 0, 0)
+    send([([T.cores[prev]], mk(prev), "g0", [T.GS[:]], [T.TJ[:]], 0)], ["GS"])
+    arrive("g0", nk(nxt), ["TJ"])
+    send_x(0, far + near)
 
     def emat(k, a, b):
         ts(T.EE[:, 144 * k:144 * k + 144], T.CI[:, 0:144], col(a), col(b), A.is_equal, A.mult, ["CI", "c%d" % a, "c%d" % b], ["E%d" % k])
 
     def weight(k, a):
         ts(col(k), T.OH[:, a:a + 1], 64.0, T.OH[:, a + 8:a + 9], A.mult, A.add, ["OH"], ["c%d" % k])
+
+    def KK(u):
+        return 2.0 ** (20 * u - 50)
+
+    def nk_ap(u):
+        return T.NK[:, NKW * (u % 2):NKW * (u % 2) + NKW]
+
+    def nk_tile(u):
+        a, b, k = NKW * (u % 2), NKW * ((u - 1) % 2), "NK%d" % (u % 2)
+        act(T.NK[:, a:a + 256], T.NK[:, b:b + 256], AF.Copy, ["NKa%d" % ((u - 1) % 2)], [k, "NKa%d" % (u % 2)], scale=KK(u) / KK(u - 1))
+        dma2("sp", [(T.NK[:, a + 256 * i:a + 256 * i + 256], T.NK[:, a:a + 256]) for i in range(1, NKW // 256)], [], [k])
 
     def consts2():
         ts(T.T2[:, 0:160], T.CG[:], col(9), T.OH[:, 0:1], A.is_equal, A.mult, ["CG", "c9", "OH"], ["T2"])
@@ -297,224 +356,221 @@ def rank_program(g, core, T, topo):
             ts(T.LZ[:, 160 * z:160 + 160 * z], T.T1[:, 0:160], col(7 - z), None, A.mult, None, ["T1", "c6", "c7"], ["LZ%d" % z])
         ts(T.DUMP[:], T.CI[:, 0:16], 16.0, col(11), A.mult, A.add, ["CI", "c11"], ["DUMP"])
         ts(col(12), T.OH[:, 0:1], 255.0, 1.0, A.mult, A.add, ["OH"], ["c12"])
-        ts(T.NK[:, 3072:3584], T.SW[:, 0:512], col(5), -1.0, A.add, A.mult, ["SW0", "c5"], ["NKb"])
+        ts(col(24), col(5), -KK(0), None, A.mult, None, ["c5"], ["c24"])
+        act(nk_ap(0), T.SW[:, 0:NKW], AF.Identity, ["SW0", "SW1", "SW2", "c24"], ["NK0", "NKa0"], bias=col(24))
 
     def consts3():
         ts(col(3), col(2), 15.0, None, A.add, None, ["c2"], ["c3"])
-        ts(T.PI[:, 3:4], T.PI[:, 0:1], 112.0, None, A.add, None, ["PI0"], ["PI3"])
         ts(col(14), T.OH[:, 0:1], -17.0, 1.0, A.mult, A.add, ["OH"], ["c14"])
-        ts(T.PI[:, 3:4], T.PI[:, 3:4], 127, None, A.bitwise_and, None, ["PI3"], ["PI3"])
         emat(4, 3, 14)
-        cp(col(13), T.PI[:, 3:4], ["PI3"], ["c13"])
+
+    def consts4():
+        ts(T.IDF[:], T.CI[:, 0:128], col(0), None, A.is_equal, None, ["CI", "c0"], ["IDF"])
         cp(T.ID[:], T.IDF[:], ["IDF"], ["ID"])
-        ts(T.NSH[:], T.CI[:, 0:128], col(13), -1.0, A.is_equal, A.mult, ["CI", "c13"], ["NSH"])
+        ts(T.NID[:], T.IDF[:], -1.0, None, A.mult, None, ["IDF"], ["NID"])
+        ts(T.ID2[:], T.IDF[:], 2.0, None, A.mult, None, ["IDF"], ["ID2"])
+        ts(T.GM4[:], T.CG[:, 0:128], col(2), 4.0, A.is_equal, A.mult, ["CG", "c2"], ["GM4"])
+        ts(T.KC[:], T.CI[:, 0:8], -4.0, 0.0, A.add, A.max, ["CI"], ["KC"])
+        ts(T.B64[:], T.DUMP[:], -4096.0, 4.0, A.add, A.mult, ["DUMP"], ["B64"])
+        ts(T.LW[:, 0::4], T.CI[:], 16.0, col(1), A.mult, A.add, ["CI", "c1"], ["LW.0"])
+        weight(15, 0)
+        emat(0, 3, 15)
 
     def places():
-        op("pool", lambda: g.iota(T.WG[:], [[0, 64], [1, 64]], 0, 1, allow_small_or_imprecise_dtypes=True), [], ["WGg"])
-        op("pool", lambda: g.iota(T.G2[:], [[1, 64], [0, 64]], 0, 0, allow_small_or_imprecise_dtypes=True), [], ch("G2"))
-        for row in (4, 5):
-            dma("sp", T.WG[row::16, :], T.G2[row::16, :], ch("G2") + ["WGg"], ["WGr%d" % row])
+        for k, (pat, base) in enumerate((([[1, 4], [0, 64]], 0), ([[0, 4], [1, 64]], 0), ([[0, 4], [1, 64]], 1))):
+            op("pool", lambda: g.iota(T.G2[:, 256 * k:256 * k + 256], pat, base, 0, allow_small_or_imprecise_dtypes=True), [], ["PL%d." % k])
+        ts(col(25), col(1), 4.0, None, A.mult, None, ["c1"], ["c25"])
+        ts(T.G2[:, 0:256], T.G2[:, 0:256], col(25), None, A.add, None, ["PL0.", "c25"], ["PL0."])
+        dma2("sp", [(T.WG[row::16, :], T.G2[:, 256 * k:256 * k + 256]) for row, k in ((1, 0), (2, 0), (4, 0), (9, 1), (12, 1), (10, 2))],
+             ["PL0.", "PL1.", "PL2.", "G2.0"], ["WGp"])
+        dma2("sp", [(T.WG[a::b, :], T.xs[a::b, :]) for a, b in ((3, 4), (5, 8), (6, 8))], [], ["WGg"])
 
     def own_rows():
-        ts(T.TI[:], T.P4[:, 0:8, :, :], 2048.0, None, A.add, None, ["P4"], ["TI"])
-        weight(15, 0)
         ts(T.TJ[:], T.TI[:], 6, None, A.logical_shift_right, None, ["TI"], ["TJ"])
         ts(T.KI[:], T.TI[:], 63, None, A.bitwise_and, None, ["TI"], ["KI"])
         cp(T.HL[:, 0:256], T.TJ[:], ["TJ"], ["HL0"])
         cp(T.HL[:, 256:512], T.KI[:], ["KI"], ["HL1"])
-        for row, k in ((0, 0), (8, 1)):
-            dma("sp", T.WG[row::16, :], T.HL[:, 256 * k:256 * k + 256], ["HL%d" % k, "WGg"], ["WGr%d" % row])
-        ts(T.B16[:], T.DUMP[:], -4096.0, 1.0 / 256, A.add, A.mult, ["DUMP"], ["B16"])
-        emat(0, 3, 15)
-        ts(T.LW[:, 0:256], T.CI[:], 16.0, col(1), A.mult, A.add, ["CI", "c1"], ["LW.0"])
+        dma2("sp", [(T.WG[8 * k + 16::16, :], T.HL[0:112, 256 * k:256 * k + 256]) for k in range(2)]
+             + [(T.WG[8 * k:8 * k + 1, :], T.HL[112:128, 256 * k:256 * k + 256]) for k in range(2)], ["HL0", "HL1", "WGg"], ["WGr"])
 
     def consts5():
         ts(T.QI[:], T.IDF[:], 0.25, None, A.mult, None, ["IDF"], ["QI"])
         ms(T.CM[:], -0.375, ["CM"])
+        ts(T.PI[:, 3:4], T.PI[:, 0:1], 112.0, None, A.add, None, ["PI0"], ["PI3"])
+        weight(16, 1)
+        ts(T.PI[:, 3:4], T.PI[:, 3:4], 127, None, A.bitwise_and, None, ["PI3"], ["PI3"])
+        weight(17, 2)
+        cp(col(13), T.PI[:, 3:4], ["PI3"], ["c13"])
+        weight(21, 5)
         ts(col(4), col(13), col(1), 15.0, A.subtract, A.add, ["c13", "c1"], ["c4"])
-        weight(16, 4)
-        weight(17, 5)
-        weight(21, 2)
-        ts(col(19), col(2), 12.0, None, A.add, None, ["c2"], ["c19"])
+        weight(22, 4)
         ts(col(20), col(0), -1.0, None, A.add, None, ["c0"], ["c20"])
         ts(col(18), col(17), col(16), 6.0, A.subtract, A.mult, ["c16", "c17"], ["c18"])
         emat(1, 4, 21)
         emat(2, 3, 16)
         emat(3, 3, 18)
+        emat(5, 3, 22)
+
+    def consts6():
         ts(T.T1[:, 0:128], T.CI[:, 0:128], col(20), col(5), A.is_equal, A.mult, ["CI", "c20", "c5"], ["T1"])
         ts(T.S2[:], T.CI[:, 0:128], col(3), T.OH[:, 0:1], A.is_equal, A.mult, ["CI", "c3", "OH"], ["S2"])
         tt(T.S1[:], T.T1[:, 0:128], T.IDF[:], A.subtract, ["T1", "IDF"], ["S1"])
         ts(T.MH[:, 256:257], col(0), 0.0, -8192.0, A.mult, A.add, ["c0"], ["MHe"])
-        ts(T.I16[:], T.IDF[:], 1.0 / 64, None, A.mult, None, ["IDF"], ["I16"])
-        ts(T.I8[:], T.IDF[:], 1.0 / 32, None, A.mult, None, ["IDF"], ["I8"])
+        ts(T.I32[:], T.IDF[:], 1.0 / 32, None, A.mult, None, ["IDF"], ["I32"])
         cp(T.RB[:, 1:6], T.RHO[:, 0:5], ["RHO"], ["RBa"])
         cp(T.RB[:, 0:1], T.RHO[:, 1:2], ["RHO"], ["RBb"])
         rt = ["RT1.%d" % a for a in range(9)]
         for a in range(9):
             s = abs(a - 4)
             ts(T.RT[:, 64 + 6 * a:70 + 6 * a], T.RB[:, 0:6], T.RHO[:, s:s + 1], None, A.mult, None, ["RBa", "RBb", "RHO"], [rt[a]])
-        ts(T.RT[:, 0:54], T.RT[:, 64:118], 128.0, None, A.mult, None, rt, ["RT0"])
+        ts(T.RT[:, 0:54], T.RT[:, 64:118], 32.0, None, A.mult, None, rt, ["RT0"])
         ts(T.RT[:, 128:182], T.RT[:, 64:118], 1.0 / 128, None, A.mult, None, rt, ["RT2", "RT1"])
 
-    def KK(u):
-        return 2.0 ** (20 * u - 50)
-
-    def chain(Wa, Wr, wkey, u, gap=(None, None, None)):
-        op("dve", lambda: V_.tensor_tensor_scan(T.TOP[:, 1:257], Wa, T.ZR[:], 0.0, A.max, A.max), [wkey, "ZR"], ["TOP"])
-        ts(T.R16[:, 0:16], T.OH[:], T.TOP[:, 256:257], None, A.mult, None, ["OH", "TOP"], ["Ra"])
-        mm(T.PD[:, 0:16], T.GL[:], T.R16[:, 0:16], True, True, ["GL", "Ra"], ["PD"])
-        if gap[0]:
-            gap[0]()
-        red(T.CA[:, 0:1], T.PD[:, 0:16], A.max, ["PD"], ["CA0"])
-        ts(T.EX[:], T.TOP[:, 0:256], T.CA[:, 0:1], None, A.max, None, ["TOP", "TOP0", "CA0"], ["EX"])
+    def chain(Wa, Wr, wkey, u):
+        scan(T.TOP[:, 1:257], Wa, T.ZR[:], 0.0, A.max, A.max, [wkey, "ZR"], ["TOP"])
+        turn(T.TA[:, 1:33], T.TOP[:, 225:257], ["TOP"], ["TA0"])
+        scan(T.TB[:, 0:32], T.TA[:, 0:32], T.MK[:, 0:32], 0.0, A.max, A.mult, ["TA0", "MK"], ["TB0"])
+        turn(T.TC[:, 0:32], T.TB[:, 0:32], ["TB0"], ["TC0"])
+        ts(T.EX[:], T.TOP[:, 0:256], T.TC[:, 31:32], None, A.max, None, ["TOP", "TOP0", "TC0"], ["EX"])
         tt(T.MM[:], T.EX[:], Wa, A.is_ge, ["EX", wkey], ["MM"])
-        op("dve", lambda: V_.tensor_tensor_scan(T.NN[:, 255::-1], T.MM[:, ::-1], Wr, 4096.0, A.mult, A.max), ["MM", wkey], ["NN"])
-        ts(T.R16[:, 16:32], T.OH[:], T.NN[:, 0:1], None, A.mult, None, ["OH", "NN"], ["Rb"])
-        mm(T.PD[:, 0:16], T.IDF[:], T.BIGM[:], True, False, ["IDF", "BIGM"], ["PD"])
-        mm(T.PD[:, 0:16], T.GU[:], T.R16[:, 16:32], False, True, ["GU", "Rb"], ["PD"])
+        scan(T.NN[:, 255::-1], T.MM[:, ::-1], Wr, 4096.0, A.mult, A.max, ["MM", wkey], ["NN"])
+        turn(T.TA[:, 36:68], T.NN[:, 0:32], ["NN"], ["TA1"])
         ts(T.NN[:, 0:1], T.NN[:, 0:1], col(5), None, A.mult, None, ["NN", "c5"], ["NN"])
-        if gap[1]:
-            gap[1]()
-        red(T.CA[:, 1:2], T.PD[:, 0:16], A.min, ["PD"], ["CA1"])
-        ts(T.NH[:], T.NN[:, 0:256], T.CA[:, 1:2], -2048.0, A.min, A.add, ["NN", "CA1"], ["NH"])
-        ts(T.FF[:, 0:17], T.NN[:, 0:257:16], T.CA[:, 1:2], None, A.min, None, ["NN", "NNe", "CA1"], ["FF"])
-        op("dve", lambda: V_.transpose(T.TR[:], T.NH[:]), ["NH"], ["TR"])
+        scan(T.TB[:, 63:31:-1], T.TA[:, 68:36:-1], T.MK[:, 63:31:-1], 4096.0, A.min, A.max, ["TA1", "MK2"], ["TB1"])
+        turn(T.TC[:, 32:64], T.TB[:, 32:64], ["TB1"], ["TC1"])
+        ts(T.NH[:], T.NN[:, 0:256], T.TC[:, 32:33], -2048.0, A.min, A.add, ["NN", "TC1"], ["NH"])
+        ts(T.FF[:, 0:17], T.NN[:, 0:257:16], T.TC[:, 32:33], None, A.min, None, ["NN", "NNe", "TC1"], ["FF"])
+        turn(T.TR[:], T.NH[:], ["NH"], ["TR"])
         regroup(0, "LZ")
         tt(T.FA[:, 0:16], T.FF[:, 0:16], T.FF[:, 1:17], A.is_ge, ["FF"], ["FA0"])
         tt(T.FA[:, 16:32], T.FA[:, 0:16], T.DUMP[:], A.mult, ["FA0", "DUMP"], ["FA1"])
         tt(T.FA[:, 32:48], T.FA[:, 16:32], T.FF[:, 0:16], A.max, ["FA1", "FF"], ["FA2"])
         cp(T.SO[:], T.FA[:, 32:48], ["FA2"], ["SO"])
         tt(T.SRC[:], T.BC[:], T.P4[:, 0:8, :, :], A.add, ["BC", "P4"], ["SRC"])
-        if gap[2]:
-            gap[2]()
-        ts(T.SW[:].indirect(T.SO[:]), T.SRC[:], KK(u), 0.0, A.mult, A.add, ["SO", "SRC"], ["SW", "SW0", "SW1", "SW2", "SW3"])
+        ts(T.SW[:].indirect(T.SO[:]), T.SRC[:], KK(u), 0.0, A.mult, A.add, ["SO", "SRC"], ["SW", "SW0", "SW1", "SW2", "SW3", "SW4"])
 
-    def wr_pass(bank, e, src, skey, c):
+    def wr_pass(bank, o, e, src, skey, c, n=1):
         for i in range(16):
-            mm(o4(T[bank], c), T.EE[:, 144 * e + 15 - i:144 * e + 143 - i], src[:, 1024 * c + i:1024 * c + 1024:16], i == 0, i == 15,
-               ["E%d" % e] + skey, [bank])
+            mm(pb(bank, o + 64 * c, 64 * n), T.EE[:, 144 * e + 15 - i:144 * e + 143 - i], src[:, 1024 * c + i:1024 * (c + n):16], i == 0, i == 15,
+               ["E%d" % e] + ch(skey, range(c, c + n)), [bank])
 
-    def b_pass(e, src, skey, c):
+    def b_pass(e, src, skey, c, first, end):
         for i in range(4 * c, 4 * c + 4):
-            mm(T.PA[:, 0:256], T.EE[:, 144 * e + 15 - i:144 * e + 143 - i], src[:, 256 * i:256 * i + 256], i == 0, i == 15,
+            mm(T.PA[:, 0:256], T.EE[:, 144 * e + 15 - i:144 * e + 143 - i], src[:, 256 * i:256 * i + 256], first and i % 4 == 0, end and i % 4 == 3,
                ["E%d" % e, "%s.%d" % (skey, c)], ["PA"])
 
-    def sweep(u, evac, pe_more=None):
-        for s in range(8):
-            a = slice(512 * s, 512 * s + 512)
-            ini = 0.0 if s == 0 else T.ST[:, 512 * s - 1:512 * s]
-            op("dve", lambda: V_.tensor_tensor_scan(T.ST[:, a], T.NK[:, 512 * u:512 * u + 512], T.SW[:, a], ini, A.add, A.max),
-               ["SW", "NK%d" % u] + (["ST.%d" % (s - 1)] if s else []), ["ST.%d" % s])
-            op("act", lambda: S_.activation(T.RR[:, a], T.ST[:, a], AF.Relu, bias=col(12), scale=-1.0 / KK(u)), ["ST.%d" % s, "c12"], ["RR.%d" % s])
-            if s % 2:
-                c = s // 2
-                wr_pass("PB" if c < 2 else "P1", 4, T.RR, ["RR.%d" % (s - 1), "RR.%d" % s], c)
-                if pe_more:
-                    pe_more(c)
-            if s == 5:
-                evac(0)
-        evac(1)
+    def count_down(u, c):
+        ini = 0.0 if c == 0 else T.ST[:, 1024 * c - 1:1024 * c]
+        scan(c4(T.ST, c), nk_ap(u), c4(T.SW, c), ini, A.add, A.max,
+             ["SW", "NK%d" % (u % 2)] + (["ST.%d" % (c - 1)] if c else []), ["ST.%d" % c])
 
-    def evac_i(h):
+    def run_out(u, c):
+        act(c4(T.RR, c), c4(T.ST, c), AF.Relu, ["ST.%d" % c, "c12"], ["RR.%d" % c], bias=col(12), scale=-1.0 / KK(u))
+
+    def evac_i(out, key):
+        ts(out, pb("PB", 0, 256), MAG + 4096, MAG, A.add, A.subtract, ["PB"], [key])
+
+    def evac_m(t, h):
         a = slice(128 * h, 128 * h + 128)
         b = "PB" if h == 0 else "P1"
-        ts(T.IN[:, a], T[b][:, a], MAG + 4096, MAG, A.add, A.subtract, [b], ["IN.%d" % h])
-
-    def evac_m(t):
-        def f(h):
-            a = slice(128 * h, 128 * h + 128)
-            b = "PB" if h == 0 else "P1"
-            ts(T.MO[:, a], T[b][:, a], MAG + 2048, MAG, A.add, A.subtract, [b], ["MO.%d" % h])
-            trs = []
-            for q in others:
-                o = 768 * t + 256 * ((r - q) % N - 1) + 128 * h
-                trs.append(([T.cores[q]], m_near if q in near else m_half[far.index(q)], "m%d_%d" % (t, h), [T.MO[:, a]], [T.ML[:, o:o + 128]], 0))
-            send(trs, ["MO.%d" % h], ["fold"])
-            arrive("m%d_%d" % (t, h), n_near * len(near) + n_far, ["ML%d.%d" % (t, h)])
-        return f
+        ts(T.MO[:, a], pb(b, 128 * h, 128), MAG + 2048, MAG, A.add, A.subtract, [b], ["MO.%d" % h])
+        trs = []
+        for q in others:
+            o = 768 * t + 256 * ((r - q) % N - 1) + 128 * h
+            trs.append(([T.cores[q]], m_near if q in near else m_half[far.index(q)], "m%d_%d" % (t, h), [T.MO[:, a]], [T.ML[:, o:o + 128]], 0))
+        send(trs, ["MO.%d" % h])
+        arrive("m%d_%d" % (t, h), n_near * len(near) + n_far, ["ML%d.%d" % (t, h)])
 
     ring, jk = [0], [0]
+    LIST = {1: (T.EU, "EU"), 2: (T.GN, "GN"), 3: (T.IN, "IN")}
 
-    def score(q, t, tr, j, n):
-        if n == 2:
-            ring[0] += ring[0] % 2
-        k = ring[0] % 4
-        ring[0] += n
-        B, o, keys = T["P%d" % (k // 2)], 512 * (k % 2), ["P0", "P5", "P1", "P6"][k:k + n]
-        base = (0 if t % 2 == 0 else 4 * W) if tr == 0 else tr * W
-        key = ("XA" if t % 2 == 0 else "XB") if tr == 0 else "T%d" % tr
-        for i in range(n):
-            a = 512 * (j + i)
-            out = B[:, o + 512 * i:o + 512 * i + 512]
-            mm(out, T.ID[:], T.GX[:, base + a:base + a + 512], True, False, ["ID", "%s.%d" % (key, j // 2)], [keys[i]])
-            mm(out, T.NSH[:], T["M%d" % (t % 2)][:, a:a + 512], False, True, ["NSH", "M%d.%d" % (t % 2, j // 2)], [keys[i]])
-        acc = T.ACC[:, 8 * tr + j:8 * tr + j + 1]
+    def slot(tr, c):
+        return (c4(T.XP, c), "XP.%d" % c) if tr == 3 else (c4(T.D, c, W * (2 - tr)), "D.%d" % (c + 4 * (2 - tr)))
+
+    def acc(tr, j):
+        return T.ACC[:, 4 * j + tr:4 * j + tr + 1], "A%d.%d" % (tr, j)
+
+    def diff(tr, c):
+        d, dk = slot(tr, c)
+        tt(d, T.X[:].indirect(o4(LIST[tr][0], c)), c4(T.MS, c), A.subtract, ch("X") + [LIST[tr][1], "MS.%d" % c], [dk])
+
+    def size(q, tr, c):
+        d, dk = slot(tr, c)
+        a, ak = acc(tr, 2 * c)
+        if q == "act":
+            act(d, d, AF.Abs, [dk], [dk, ak], accum_out=a)
+        else:
+            red(a, d, A.add, [dk], [ak], apply_absolute_value=True)
+
+    def raw(tr, c):
+        d, dk = slot(tr, c)
+        gat("act", d, T.X[:], o4(LIST[tr][0], c), ch("X") + [LIST[tr][1]], [dk])
+
+    def size_pe(q, tr, c):
+        d, dk = (c4(T.X, c), "X.%d" % c) if tr == 0 else slot(tr, c)
+        ring[0] += 1
+        B, keys = (T.P0, ["P0", "P5"]) if ring[0] % 2 else (T.P1, ["P1", "P6"])
+        src = T.X if tr == 0 else (T.XP if tr == 3 else T.D)
+        base = 1024 * c + (0 if tr in (0, 3) else W * (2 - tr))
+        for i in range(2):
+            out = B[:, 512 * i:512 * i + 512]
+            mm(out, T.ID[:], src[:, base + 512 * i:base + 512 * i + 512], True, False, ["ID", dk], [keys[i]])
+            mm(out, T.NID[:], T.MS[:, 1024 * c + 512 * i:1024 * c + 512 * i + 512], False, True, ["NID", "MS.%d" % c], [keys[i]])
+        a, ak = acc(tr, 2 * c)
         if q == "act":
             jk[0] += 1
-            z = 1024 * (jk[0] % 2)
-            op("act", lambda: S_.activation(T.JK[:, z:z + 512 * n], B[:, o:o + 512 * n], AF.Abs, accum_out=acc), keys, ["JK%d" % z, "A%d.%d" % (tr, j)])
+            act(c4(T.MP, jk[0] % 4), B[:], AF.Abs, keys, ["MP.%d" % (jk[0] % 4), ak], accum_out=a)
         else:
-            red(acc, B[:, o:o + 512 * n], A.add, keys, ["A%d.%d" % (tr, j)], apply_absolute_value=True)
+            red(a, B[:], A.add, keys, [ak], apply_absolute_value=True)
 
-    def trial(q, t, tr, c):
-        xb, X = (0, "XA") if t % 2 == 0 else (4 * W, "XB")
-        off, k = ((T.EU, "EU"), (T.GN, "GN"), (T.IN, "IN.%d" % (c // 2)))[tr - 1]
-        gat(q, c4(T.GX, c, tr * W), T.GX[:, xb:xb + W], o4(off, c), ch(X) + [k], ["T%d.%d" % (tr, c)])
+    def sum_pe(tr, l, lkey, src, base, keys, first=False, end=False):
+        b = ("P0", "P5")[tr]
+        for i in range(8):
+            mm(pb(b, 0, 512), l[:], src[:, base + 512 * i:base + 512 * i + 512], first and i == 0, end and i == 7, [lkey, keys[i // 2]], [b])
 
-    def tsum(tr):
-        red(T.SC[:, tr:tr + 1], T.ACC[:, 8 * tr:8 * tr + 8], A.add, ["A%d.%d" % (tr, j) for j in range(8)], ["SC%d" % tr])
+    def trial_of(tr):
+        return (T.X, 0, ch("X")) if tr == 0 else (T.D, W, ch("D", range(4, 8)))
 
-    def scores(t, extra, pre, na, nd):
-        left = [(tr, c) for tr in (1, 2, 3) for c in range(4)][pre:]
-        for tr, c in left[:na]:
-            trial("act", t, tr, c)
-        for k, (tr, c) in enumerate(left[na:]):
-            if k < len(extra):
-                extra[k]()
-            trial("dve", t, tr, c)
-        cp(T.LW[:, 768:1024], T.IN[:], ["IN.0", "IN.1"], ["LW.3"])
-        todo = [(1, c) for c in others] + [(0, c) for c in order] + [(1, r)] + [(tr, c) for tr in (2, 3) for c in range(4)]
-        nw = 16 - nd
-        for tr, c in todo[:nw]:
-            score("act", t, tr, 2 * c, 2)
-        tsum(0)
-        tsum(1)
-        for tr, c in todo[nw:]:
-            score("dve", t, tr, 2 * c, 1)
-            score("act", t, tr, 2 * c + 1, 1)
-        tsum(2)
-        tsum(3)
+    def fold_max(e, tr):
+        src, base, keys = trial_of(tr)
+        back_keys = ch("MP") if tr == 0 else keys
+        deps("pool", [], back_keys, False)
+        key = "f%d_%d" % (e, tr)
+        send([([hc], topo.mask(core, hc), key, [src[:, base:base + W], T.MS[:]], [_parked(T, e, tr)], 2)], keys + ch("MS"))
+        arrive(key, len(_bits(topo.mask(hc, core))), back_keys)
 
-    def elect(t):
-        mm(T.PD[:, 0:4], T.GM4[:], T.SC[:], True, True, ["GM4"] + ["SC%d" % k for k in range(4)], ["PD"])
-        tt(T.KY[:], T.CI[:, 0:4], T.PD[:, 0:4], A.add, ["CI", "PD"], ["KY"])
-        red(T.EL[:, 0:1], T.PD[:, 0:4], A.min, ["PD"], ["EL0"])
-        red(T.EL[:, 1:2], T.KY[:], A.min, ["KY"], ["EL1"])
-        tt(T.EL[:, 2:3], T.EL[:, 1:2], T.EL[:, 0:1], A.subtract, ["EL0", "EL1"], ["EL2"])
-        ts(T.CS[:], T.B16[:], T.EL[:, 2:3], 256.0, A.add, A.mult, ["B16", "EL2"], ["CS"])
-        gat("dve", T.CU[:], T.LW[:], T.CS[:], ch("LW") + ["CS"], ["CU"])
-        wk = ["WGg"] + ["WGr%d" % k for k in (0, 8, 4, 5)]
-        for c in range(4):
-            gat("dve" if c % 2 == 0 else "act", c4(T.G1, c), T.WG[:], o4(T.CU, c), wk + ["CU"], ["G1.%d" % c])
-            b_pass(0, T.G1, "G1", c)
-        if t < 2:
-            send_g(t + 1)
-        dma("sp", T.G1[5::8, 0:W - 1], T.G1[4::8, 1:W], [], ch("G1"))
-        if t < 2:
-            dma("sp", T.G1[2::8, :], T.HN[:, 512 * t:512 * t + 512], ["HN%d" % (t + 1)], ch("G1"))
-            dma("sp", T.LW[:, 256:512], T.ew[:, 256 * t + 256:256 * t + 512], [], ["LW.1"])
+    def sum_max(tr):
+        src, base, keys = (T.MP, 0, ch("MP")) if tr == 0 else trial_of(tr)
+        sum_pe(tr, T.ID2, "ID2", src, base, keys, end=True)
+
+    def size_sum(q, tr):
+        b = ("P0", "P5")[tr]
+        a, ak = acc(tr, 0)
+        if q == "act":
+            act(T.HL[:], pb(b, 0, 512), AF.Copy, [b], ["HL0", "HL1", ak], accum_out=a)
+        else:
+            red(a, pb(b, 0, 512), A.add, [b], [ak])
 
     def clear_sums():
         ms(T.ACC[:], 0.0, ["A%d.%d" % (tr, j) for tr in range(4) for j in range(8)])
 
-    def window_base(t):
-        clear_sums()
-        if t % 2 == 0:
-            ts(T.EL[:, 4:5], T.EL[:, 2:3], -4096.0, MAG, A.mult, A.add, ["EL2"], ["EL4"])
-        else:
-            ts(T.EL[:, 3:4], T.EL[:, 2:3], 0.0, 4.0, A.is_equal, A.mult, ["EL2"], ["EL3"])
-            ts(T.EL[:, 3:4], T.EL[:, 3:4], T.EL[:, 2:3], -4096.0, A.add, A.mult, ["EL2", "EL3"], ["EL3"])
-            ts(T.EL[:, 4:5], T.EL[:, 3:4], MAG + 4096, None, A.add, None, ["EL3"], ["EL4"])
+    def elect(t, cs):
+        mm(T.P4[:, 8, 0, 0:8], T.IDF[:], T.KC[:], True, False, ["IDF", "KC"], ["P4"])
+        for k, c in enumerate(cs):
+            for z in range(2):
+                mm(T.P4[:, 8, 0, 4 * z:4 * z + 4], T.GM4[:], T.ACC[:, 8 * c:8 * c + 4], False, k == 3 and z == 1, ["GM4"] + ["A%d.%d" % (tr, 2 * c) for tr in range(4)], ["P4"])
+        red(T.EL[:, 0:1], T.P4[:, 8, 0, 0:4], A.min, ["P4"], ["EL0"])
+        red(T.EL[:, 1:2], T.P4[:, 8, 0, 4:8], A.min, ["P4"], ["EL1"])
+        ts(T.CS[:], T.B64[:], T.EL[:, 1:2], T.EL[:, 0:1], A.add, A.subtract, ["B64", "EL0", "EL1"], ["CS"])
+        gat("dve", T.CU[:], T.LW[:], T.CS[:], ch("LW") + ["CS"], ["CU"])
+
+    def gamma_c(q, c):
+        gat(q, c4(T.G1, c), T.WG[:], o4(T.CU, c), ["WGg", "WGp", "WGr", "CU"], ["G1.%d" % c])
+
+    def x_c(t, c, q="act"):
+        gat(q, c4(T.XP, c), T.X[:], o4(T.CU, c), ch("X") + ["CU"], ["XP.%d" % c])
+        if t < 2:
+            dma2("sp", [(rows(T.D, 0, 112, c), rows(T.XP, 16, 128, c)), (rows(T.D, 112, 128, c), rows(T.XP, 0, 16, c))], ["XP.%d" % c], ["D.%d" % c])
 
     def mean(t, h):
         a = slice(128 * h, 128 * h + 128)
@@ -525,183 +581,275 @@ def rank_program(g, core, T, topo):
             o = 768 * t + 256 * k + 128 * h
             mm(T[b][:, a], T.QI[:], T.ML[:, o:o + 128], False, k == 2, ["QI", "ML%d.%d" % (t, h)], [b])
         ts(T.MU[:, a], T[b][:, a], MAG + 2048, MAG, A.add, A.subtract, [b], ["MU.%d" % h])
-        ts(T.MX[:, a], T[b][:, a], MAG + 2048, T.EL[:, 4:5], A.add, A.subtract, [b, "EL4"], ["MX.%d" % h])
 
     def gamma_mu(q, c):
-        gat(q, c4(T.G2, c), T.G1[:], o4(T.MU, c), ch("G1") + ["MU.%d" % (c // 2)], ["G2.%d" % c])
+        gat(q, c4(T.G2, c), T.G1[:], o4(T.MU, c), ch("G1") + ["G1n", "G1x", "MU.%d" % (c // 2)], ["G2.%d" % c])
 
-    def x_new(t, c, q="act"):
-        wb, xb, X, Xo = (0, 4 * W, "XB", "XA") if t % 2 == 0 else (W, 0, "XA", "XB")
-        gat(q, c4(T.GX, c, xb), T.GX[:, wb:wb + 4 * W], o4(T.MX, c), ch(Xo) + ch("T1") + ch("T2") + ch("T3") + ["MX.%d" % (c // 2)], ["%s.%d" % (X, c)])
-        if c != r:
-            send_x(c, X, xb, t + 1)
+    def x_mu(q, c):
+        gat(q, c4(T.X, c), T.XP[:], o4(T.MU, c), ch("XP") + ["MU.%d" % (c // 2)], ["X.%d" % c])
 
-    def fold_new(t):
-        fold_x("XB" if t % 2 == 0 else "XA", 4 * W if t % 2 == 0 else 0, t + 1)
+    def m_mu(t):
+        for k, c in enumerate(mine):
+            gat("act", c4(T.MS, c), T.MP[:], o4(T.MV, k), ch("MP") + ["MV"], ["MS.%d" % c])
+        half = T.MS[:, 2048 * side:2048 * side + 2048]
+        send([([T.cores[near[0]]], topo.mask(core, T.cores[near[0]]), "s%d" % t, [half], [half], 0)], ch("MS", mine))
+        arrive("s%d" % t, len(_bits(topo.mask(T.cores[near[0]], core))), ch("MS", theirs))
 
-    def full_pass(bank, e):
-        for c in range(4):
-            wr_pass(bank, e, T.G2, ["G2.%d" % c], c)
-
-    def slope_mu(bm):
+    def slope_mu(bm, o=0):
         ts(T.MH[:, 0:256], T.MU[:], -2048.0, None, A.add, None, ["MU.0", "MU.1"], ["MH"])
-        mm(T[bm][:, 0:256], T.S1[:], T.MH[:, 0:256], True, False, ["S1", "MH"], [bm])
-        mm(T[bm][:, 0:256], T.S2[:], T.MH[:, 1:257], False, True, ["S2", "MH", "MHe"], [bm])
+        mm(pb(bm, o, 256), T.S1[:], T.MH[:, 0:256], True, False, ["S1", "MH"], [bm])
+        mm(pb(bm, o, 256), T.S2[:], T.MH[:, 1:257], False, True, ["S2", "MH", "MHe"], [bm])
 
-    def slopes(bd, bs, bm):
-        ts(T.DU[:], T[bd][:, 0:256], col(19), None, A.subtract, None, [bd, "c19"], ["DU"])
-        ts(T.T1[:], T[bs][:, 0:256], -24.0, 24.0, A.max, A.min, [bs], ["T1"])
-        ts(T.T2[:], T[bm][:, 0:256], -1.0, 4.0, A.max, A.min, [bm], ["T2"])
-        tt(T.T1[:], T.T1[:], T.T2[:], A.add, ["T1", "T2"], ["T1"])
-        ts(T.IX[:], T.T1[:], 25.0, None, A.add, None, ["T1"], ["IX"])
+    def composed(bd, a=0, n=256):
+        cp(T.DU[:, a:a + n], pb(bd, a, n), [bd], ch("DU", range(a // 64, (a + n) // 64)))
+
+    def slope_m(bm, o=0):
+        ts(T.T2[:], pb(bm, o, 256), -1.0, 4.0, A.max, A.min, [bm], ["T2"])
+
+    def slopes(bs, o, a=0, n=256):
+        k = "T1.%d" % a
+        ts(T.T1[:, a:a + n], pb(bs, o + a, n), -24.0, 24.0, A.max, A.min, [bs], [k, "T1"])
+        tt(T.T1[:, a:a + n], T.T1[:, a:a + n], T.T2[:, a:a + n], A.add, [k, "T2"], [k])
+        ts(T.IX[:, a:a + n], T.T1[:, a:a + n], 25.0, None, A.add, None, [k], ch("IX", range(a // 64, (a + n) // 64)))
+
+    VB = ("VD", "V", "VD")
 
     def v_gather(t, c):
-        win, k = (T.PAY, ["PAY"]) if t == 0 else (T.V, ch("V"))
-        gat("act", c4(T.VD, c), win[:], o4(T.DU, c), k + ["DU"], ["VD.%d" % c])
+        win, k = (T.PAY, ["pay"]) if t == 0 else (T[VB[t - 1]], ch(VB[t - 1]))
+        gat("act", c4(T[VB[t]], c), win[:], o4(T.DU, c), k + ["DU.%d" % c], ["%s.%d" % (VB[t], c)])
 
     def v_mult(t, c):
-        out, k = (T.V, "V") if t < 2 else (T.VD, "VD")
-        tt(c4(out, c), T.RT[:, 64 * t:64 * t + 54].indirect(o4(T.IX, c)), c4(T.VD, c), A.mult, ["RT%d" % t, "IX", "VD.%d" % c], ["%s.%d" % (k, c)])
-        if t < 2:
-            dma("pool", c4(T.V, c), c4(T["M%d" % ((t + 1) % 2)], c), ["M%d.%d" % ((t + 1) % 2, c)], ["V.%d" % c], accum_op=A.add)
+        v, k = c4(T[VB[t]], c), "%s.%d" % (VB[t], c)
+        tt(v, T.RT[:, 64 * t:64 * t + 54].indirect(o4(T.IX, c)), v, A.mult, ["RT%d" % t, "IX.%d" % c, k], [k])
 
-    def nk_tiles(us):
-        for u in us:
-            op("act", lambda: S_.activation(T.NK[:, 512 * u:512 * u + 512], T.NK[:, 3072:3584], AF.Copy, scale=KK(u)), ["NKb"], ["NK%d" % u])
+    def v_add(t, c, n):
+        a = slice(1024 * c, 1024 * (c + n))
+        dma("pool", T[VB[t]][:, a], T.MR[:, a], ["MR"], ch(VB[t], range(c, c + n)), accum_op=A.add, max_dma_last_dim=4096)
 
-    clear_sums()
-    cp(T.EU[:], T.LW[:, 256:512], ["LW.1"], ["EU"])
+    def p_zero(c):
+        act(c4(T.PZ, c), T.PAY[:].indirect(o4(T.GO, c)), AF.Copy, ["pay", "GO"], ["pz.%d" % c], scale=16.0)
+
+    def p_gather(q, c):
+        if q == "act":
+            act(c4(T.SW, c), T.PZ[:].indirect(o4(T.GO, c)), AF.Copy, ch("pz") + ["GO.%d" % (c // 2), "SW"], ["pp%d" % c], scale=1.0 / 64)
+        else:
+            ts(c4(T.SW, c), T.PZ[:].indirect(o4(T.GO, c)), 1.0 / 64, None, A.mult, None, ch("pz") + ["GO.%d" % (c // 2), "SW"], ["pp%d" % c])
+
+    order = near + far + [r]
+    to_blocks(T.GS[:], "GS")
+    cp(T.EU[:], T.EI[:], ["EI"], ["EU"])
     consts2()
-    nk_tiles([0])
-    for c in range(4):
-        trial("act", 0, 1, c)
-    to_blocks(T.LW[:, 512:768], "LW.2")
-    cp(T.GN[:], T.LW[:, 512:768], ["LW.2"], ["GN"])
-    for c in range(PRE0 - 4):
-        trial("act", 0, 2, c)
-    ts(T.WB[:], T.P4[:, 0:8, :, :], 2048.0, None, A.add, None, ["P4"], ["WB"])
-    chain(T.WB[:], T.WB[:, ::-1], "WB", 0, (consts3, None, None))
+    ts(T.T2[:], T.P4[:, 0:8, :, :], 2048.0, None, A.add, None, ["P4"], ["T2"])
+    for c in order:
+        raw(1, c)
+    chain(T.T2[:], T.T2[:, ::-1], "T2", 0)
+    cp(T.GN[:], T.TJ[:], ["TJ"], ["GN"])
+    consts3()
     places()
-    dma("sp", T.RHO[:, 0:5], T.rho[:], [], ["RHO"])
-    dma("act", T.PAY[:], T.pay[:], ["SO"], ["PAY"])
-    sweep(0, evac_i)
+    fold_x(0, n_far + n_near)
+    for c in range(4):
+        count_down(0, c)
+        run_out(0, c)
+        wr_pass("PB", 0, 4, T.RR, "RR", c)
+    cp(T.LW[:, 2::4], T.TJ[:], ["TJ"], ["LW.2"])
+    cp(T.TI[:], T.T2[:], ["T2"], ["TI"])
+    own_rows()
+    evac_i(T.LO[:], "LO")
+    send([([T.cores[prev]], mk(prev), "i", [T.LO[:]], [T.IN[:]], 0)], ["LO"])
+    arrive("i", nk(nxt), ["IN"])
+    for c in order[:RAW0]:
+        raw(2, c)
+    clear_sums()
+    consts4()
+    cp(T.LW[:, 1::4], T.EI[:], ["EI"], ["LW.1"])
+    cp(T.GO[:], T.GA[:], ["GA"], ["GO"])
+    for c in range(PZ0):
+        p_zero(c)
+    for c in order[RAW0:]:
+        if c != r:
+            diff(2, c)
+    cp(T.LW[:, 3::4], T.IN[:], ["IN"], ["LW.3"])
+    for c in order:
+        diff(3, c)
+    if RAW0 < 4:
+        diff(2, r)
+    todo = [(tr, c) for c in order for tr in (1, 0, 2) if tr < 2 or c in order[:RAW0]]
+    made = [(2, c) for c in order[RAW0:3]] + [(3, c) for c in order] + [(2, r)] * (RAW0 < 4)
+    for k, tc in enumerate(todo):
+        size_pe("act", *tc)
+        if k < len(made) - DA0:
+            size("act", *made[k])
+    for tc in made[len(made) - DA0:]:
+        size("dve", *tc)
 
     for t in range(3):
-        if t == 0:
-            scores(t, [lambda: to_blocks(T.GA[:], "GA"), own_rows], PRE0, NA0, ND0)
-        else:
-            scores(t, [lambda: None, lambda: slopes("PA", "PD", "PB")], PRE, NA, ND)
-            v_gather(t - 1, 0)
-        elect(t)
+        for u in range(2 * t + 1, min(2 * t + 3, 6)):
+            nk_tile(u)
+        elect(t, order)
+        for c in range(4):
+            gamma_c("dve" if c % 2 == 0 else "act", c)
+            b_pass(0, T.G1, "G1", c, c == 0, c == 3)
         if t > 0:
+            composed("PD")
+            slope_m("PD", 256)
+            slopes("PB", 256)
+        if t < 2:
+            send_g(t + 1)
+        wait("sp", lastw["PA"])
+        dma("sp", T.G1[2::8, 0:W - 1], T.G1[1::8, 1:W], ch("G1"), ["G1x"])
+        for c in (far + near if t else last):
+            x_c(t, c)
+            if c != r:
+                send_x(t + 1, [c])
+        if t < 2:
+            dma("sp", T.G1[5::8, :], T.HN[:, 512 * t:512 * t + 512], ["HN%d" % (t + 1)] + ch("G1"), ["G1n"])
+            dma("sp", T.EI[:], T.ew[:, 256 * t + 256:256 * t + 512], [], ["EI"])
+        if t:
+            v_gather(t - 1, 0)
+        chain(T.PA[:, 0:256], T.PA[:, 255::-1], "PA", 2 * t + 1)
+        for c in range(4):
+            count_down(2 * t + 1, c)
+            run_out(2 * t + 1, c)
+            wr_pass("PB" if c < 2 else "P1", 0, 4, T.RR, "RR", c)
+        if t == 0:
+            evac_m(t, 0)
+            consts5()
+            evac_m(t, 1)
+            fold_x(t + 1, N_X)
+            consts6()
+            for c in range(PZ0, 4):
+                p_zero(c)
+        else:
+            evac_m(t, 0)
+            x_c(t, r, "dve")
             for c in range(1, 4):
                 v_gather(t - 1, c)
-        else:
-            nk_tiles(range(1, 6))
-            op("act", lambda: S_.activation(T.PAY[:], T.PAY[:], AF.Copy, scale=0.25), ["PAY"], ["PAY"])
-        chain(T.PA[:, 0:256], T.PA[:, 255::-1], "PA", 2 * t + 1, (lambda: window_base(t), None, None))
-        sweep(2 * t + 1, evac_m(t))
-        if t == 0:
-            consts5()
-        else:
-            v_mult(t - 1, 0)
-            v_mult(t - 1, 1)
-        if t == 2:
-            break
-        first = [c for c in others if c < 2] + [c for c in others if c >= 2]
+            evac_m(t, 1)
+            if t == 1:
+                fold_x(t + 1, N_X)
+            for c in range(3):
+                v_mult(t - 1, c)
+                if t == 2:
+                    v_add(t - 1, c, 1)
+            if t == 2:
+                break
+        clear_sums()
         mean(t, 0)
         gamma_mu("dve", 0)
-        x_new(t, first[0])
-        gamma_mu("dve", 1)
+        gamma_mu("act", 1)
         mean(t, 1)
+        a = slice(128 * side, 128 * side + 128)
+        dma2("sp", [(T.MV[0:112], T.MU[16:128, a]), (T.MV[112:128], T.MU[0:16, a])], ["MU.%d" % side], ["MV"])
         gamma_mu("dve", 2)
-        for k in range(1, 5):
-            if k == GA3:
-                gamma_mu("act", 3)
-            if k < 4:
-                x_new(t, (first + [r])[k])
-        if not GA3:
-            gamma_mu("dve", 3)
-        fold_new(t)
+        x_mu("act", 0)
+        gamma_mu("act", 3)
         for c in range(4):
-            b_pass(1, T.G2, "G2", c)
-            if c < 2:
-                wr_pass("PB", 1, T.G2, ["G2.%d" % c], c)
-        dma("sp", T.WG[0::8, :], T.G2[0::8, :], ch("G2"), ["WGr0", "WGr8"])
-
-        def gap0():
-            wr_pass("PB", 1, T.G2, ["G2.2"], 2)
-            wr_pass("PB", 1, T.G2, ["G2.3"], 3)
-            cp(T.EU[:], T.LW[:, 256:512], ["LW.1"], ["EU"])
-            for c in range(min(PRE, 4)):
-                trial("act", t + 1, 1, c)
-
-        def gap1():
-            cp(T.GN[:], T.PB[:, 0:256], ["PB"], ["GN"])
-            for c in range(PRE - 4):
-                trial("act", t + 1, 2, c)
-
-        def gap2():
-            full_pass("PA", 2)
-        chain(T.PA[:, 0:256], T.PA[:, 255::-1], "PA", 2 * t + 2, (gap0, gap1, gap2))
-        cp(T.LW[:, 512:768], T.GN[:], ["GN"], ["LW.2"])
-        sweep(2 * t + 2, evac_i, lambda c: wr_pass("PD", 3, T.G2, ["G2.%d" % c], c))
-        slope_mu("PB")
-        if t > 0:
-            v_mult(t - 1, 2)
+            b_pass(1, T.G2, "G2", c, c == 0, c == 3)
+        dma("sp", T.WG[0::4, :], T.G2[0::4, :], ch("G2"), ["WGr"])
+        cp(T.EU[:], T.EI[:], ["EI"], ["EU"])
+        for c in range(1, 4):
+            x_mu("act" if c < 4 - XD else "dve", c)
+        wr_pass("P1", 0, 1, T.G2, "G2", 0, 4)
+        order = mine + theirs
+        for c in order[:MK]:
+            raw(1, c)
+        m_mu(t)
+        for c in order[MK:RAW]:
+            raw(1, c)
+        chain(T.PA[:, 0:256], T.PA[:, 255::-1], "PA", 2 * t + 2)
+        cp(T.GN[:], pb("P1", 0, 256), ["P1"], ["GN"])
+        wr_pass("PD", 0, 2, T.G2, "G2", 0, 4)
+        wr_pass("PB", 256, 3, T.G2, "G2", 0, 4)
+        for c in range(4):
+            count_down(2 * t + 2, c)
+            run_out(2 * t + 2, c)
+        cp(T.LW[:, 1::4], T.EI[:], ["EI"], ["LW.1"])
+        cp(T.LW[:, 2::4], T.GN[:], ["GN"], ["LW.2"])
+        slope_mu("PD", 256)
+        if t == 1:
             v_mult(t - 1, 3)
+            wait("pool", lastw["MS.%d" % theirs[0]])
+            v_add(0, 0, 4)
+        else:
+            wait("pool", lastw["MS.%d" % theirs[0]])
+            dma("pool", T.PZ[:], T.xs[:], [], ch("pz"), accum_op=A.add, max_dma_last_dim=4096)
+        dma2("sp", [(T.MR[16:128], T.MS[0:112]), (T.MR[0:16], T.MS[112:128])], ch("MS"), ["MR"])
+        for c in order:
+            diff(2, c)
+        for c in order[RAW:]:
+            diff(1, c)
+        todo = [(0, c) for c in order] + [(1, c) for c in order[:RAW]]
+        made = [(2, c) for c in order] + [(1, c) for c in order[RAW:]] + [(3, c) for c in order]
+        for k in range(len(made) - DA):
+            if k < len(todo):
+                size_pe("act", *todo[k])
+            if k == 1:
+                wr_pass("PB", 0, 4, T.RR, "RR", 0, 4)
+                evac_i(T.IN[:], "IN")
+                cp(T.LW[:, 3::4], T.IN[:], ["IN"], ["LW.3"])
+                for c in order:
+                    diff(3, c)
+            size("act", *made[k])
+        for tc in todo[len(made) - DA:]:
+            size_pe("act", *tc)
+        for tc in made[len(made) - DA:]:
+            size("dve", *tc)
 
     mean(2, 0)
-    gamma_mu("act", 0)
-    gamma_mu("act", 1)
-    v_mult(1, 2)
     mean(2, 1)
-    gamma_mu("act", 2)
-    gamma_mu("act", 3)
     v_mult(1, 3)
-    for c in range(4):
-        wr_pass("PA", 2, T.G2, ["G2.%d" % c], c)
-        wr_pass("PB", 3, T.G2, ["G2.%d" % c], c)
-        wr_pass("PD", 0, T.G2, ["G2.%d" % c], c)
-    x_new(2, far[0], "dve")
-    slope_mu("P1")
-    x_new(2, far[1], "dve")
-    x_new(2, near[0])
-    x_new(2, r)
-    slopes("PA", "PB", "P1")
-    cp(T.GO[:], T.PD[:, 0:256], ["PD"], ["GO"])
-    last = far + near + [r]
-    fold_new(2)
+    v_add(1, 3, 1)
+    fold_x(3, N_X)
     for c in last:
-        v_gather(2, c)
-    for k, c in enumerate(near + [r]):
-        gat("act", c4(T.RR, k), T.PAY[:], o4(T.GO, c), ["PAY", "GO"], ["RR.%d" % (2 * k), "RR.%d" % (2 * k + 1)])
-    for c in last:
-        v_mult(2, c)
-        slot = c4(T.LU, (r - c) % N - 1)
-        if c in far:
-            keys = ["ST.%d" % (2 * c), "ST.%d" % (2 * c + 1)]
-            tt(c4(T.ST, c), T.PAY[:].indirect(o4(T.GO, c)), c4(T.VD, c), A.add, ["PAY", "GO", "VD.%d" % c], keys)
-            send([([T.cores[c]], m_far, "u%d" % r, [c4(T.ST, c)], [slot], 0)], keys)
-        elif c in near:
-            send([([T.cores[c]], m_near, "u%d" % r, [c4(T.VD, c)], [slot], 0)], ["VD.%d" % c])
-            send([([T.cores[c]], m_near, "p", [c4(T.RR, 0)], [T.HN[:]], 0)], ["RR.0", "RR.1"])
-    arrive("p", n_near, ["HP"])
+        gamma_mu("act" if c != far[1] else "dve", c)
+    slope_mu("P5")
+    hf = far[0] // 2
+    banks = {hf: ("PA", "PB", "PD"), 1 - hf: ("P1", "P6", "P0")}
+    for h in (hf, 1 - hf):
+        for k in (0, 2, 1):
+            wr_pass(banks[h][k], 0, (2, 3, 5)[k], T.G2, "G2", 2 * h, 2)
+    slope_m("P5")
+
+    def lists(h):
+        composed(banks[h][0], 128 * h, 128)
+        cp(T.GO[:, 128 * h:128 * h + 128], pb(banks[h][2], 128 * h, 128), [banks[h][2]], ["GO.%d" % h, "GO"])
+
+    def send_u(c):
+        send([([T.cores[c]], mk(c), "u%d" % r, [c4(T.VD, c), c4(T.SW, c)], [c4(T.ST, (r - c) % N - 1)], 1)], ["VD.%d" % c, "pp%d" % c])
+    lists(hf)
+    v_gather(2, far[0])
+    v_gather(2, far[1])
+    p_gather("dve", far[0])
+    p_gather("act", far[1])
+    slopes(banks[hf][1], 0, 128 * hf, 128)
+    v_mult(2, far[0])
+    send_u(far[0])
+    lists(1 - hf)
+    v_mult(2, far[1])
+    send_u(far[1])
+    v_gather(2, near[0])
+    v_gather(2, r)
+    slopes(banks[1 - hf][1], 0, 128 * (1 - hf), 128)
+    p_gather("dve", near[0])
+    v_mult(2, near[0])
+    send_u(near[0])
+    p_gather("act", r)
+    v_mult(2, r)
+    gat("act", c4(T.RR, 0), T.MP[:], o4(T.MU, r), ch("MP") + ["MU.%d" % (r // 2)], ["RR.0"])
     for q in others:
         arrive("u%d" % q, nk(q), ["LU.%d" % ((q - r) % N - 1)])
     late = [q for q in far if [c for c in [(q + k) % N for k in range(1, N)] if topo.chip(T.cores[c]) != topo.chip(T.cores[q])][1] == r]
     tail = (late + far)[0]
     lu = [(q - r) % N - 1 for q in [c for c in far if c != tail] + near + [tail]]
-    parts = [(T.I16, T.GX, 4 * W + 1024 * r, ["I16", "XB.%d" % r])] + [(T.I16, T.LX, 1024 * k, ["I16", "LX"]) for k in range(3)]
-    parts += [(T.ID, T.RR, 1024, ["ID", "RR.2", "RR.3"]), (T.IDF, T.VD, 1024 * r, ["IDF", "VD.%d" % r]), (T.I8, T.LX, 3072, ["I8", "MF"]),
-              (T.IDF, T.LU, 1024 * lu[0], ["IDF", "LU.%d" % lu[0]]), (T.ID, T.HN, 0, ["ID", "HP"]), (T.IDF, T.LU, 1024 * lu[1], ["IDF", "LU.%d" % lu[1]])]
+    parts = [(T.IDF, T.SW, 1024 * r, ["IDF", "pp%d" % r]), (T.IDF, T.VD, 1024 * r, ["IDF", "VD.%d" % r]), (T.I32, T.RR, 0, ["I32", "RR.0"]),
+             (T.IDF, T.ST, 1024 * lu[0], ["IDF", "LU.%d" % lu[0]]), (T.IDF, T.ST, 1024 * lu[1], ["IDF", "LU.%d" % lu[1]])]
     for k, (l, src, o, keys) in enumerate(parts):
         for h in range(2):
             mm(T.P0[:, 512 * h:512 * h + 512], l[:], src[:, o + 512 * h:o + 512 * h + 512], k == 0, k == len(parts) - 1, keys, [("P0", "P5")[h]])
     for h in range(2):
         a = slice(512 * h, 512 * h + 512)
         o = 1024 * lu[2] + 512 * h
-        tt(T.SW[:, a], T.LU[:, o:o + 512], T.P0[:, a], A.add, ["LU.%d" % lu[2], ("P0", "P5")[h]], [("SW", "Y1")[h]])
-        dma(("sp", "act")[h], T.y[:, a], T.SW[:, a], [("SW", "Y1")[h]], ["y%d" % h])
+        tt(T.ST[:, 3072 + 512 * h:3584 + 512 * h], T.ST[:, o:o + 512], T.P0[:, a], A.add, ["LU.%d" % lu[2], ("P0", "P5")[h]], ["Y%d" % h, "ST.3"])
+        dma(("sp", "act")[h], T.y[:, a], T.ST[:, 3072 + 512 * h:3584 + 512 * h], ["Y%d" % h], ["y%d" % h])
     for s in cnt:
         wait("pool", (s, cnt[s]))

@@ -5,8 +5,7 @@ W = 4096
 MAG = 12582912.0
 F32, BF, F16, I32, U16 = "float32", "bfloat16", "float16", "int32", "uint16"
 NKW = 1024
-XD, MK, RAW, DA, RAW0, DA0, PZ0 = 1, 1, 3, 3, 2, 4, 2
-FOLDED = ()
+G1P = (768, 768, 768, 768, 512, 512)
 
 
 def _sb(n, d):
@@ -20,29 +19,30 @@ SCRATCH = {
     "SW": _sb(W + 256, F32), "ST": _sb(W, F32), "RR": _sb(W, BF),
     "NK": _sb(2 * NKW, BF),
     "PI": _sb(4, I32), "KI": _sb(256, I32), "TI": _sb(256, I32), "TJ": _sb(256, I32), "GS": _sb(256, I32), "GA": _sb(256, I32),
-    "EI": _sb(256, I32), "LO": _sb(256, U16),
+    "EI": _sb(256, I32),
     "CI": _sb(256, F32), "CG": _sb(160, F32), "CO": _sb(32, F32), "OH": _sb(16, F32), "T1": _sb(256, F32), "T2": _sb(256, F32),
-    "EE": _sb(6 * 144, BF), "ID": _sb(128, BF), "NID": _sb(128, BF), "ID2": _sb(128, BF), "I32": _sb(128, BF), "CM": _sb(128, BF),
-    "IDF": _sb(128, F32), "GM4": _sb(128, F32), "KC": _sb(8, F32),
+    "EE": _sb(7 * 144, BF), "ID": _sb(128, BF), "NID": _sb(128, BF), "ID2": _sb(128, BF), "I32": _sb(128, BF), "CM": _sb(128, BF),
+    "IDF": _sb(128, F32), "GM4": _sb(128, F32), "GN4": _sb(128, F32), "KC": _sb(4, F32),
     "QI": _sb(128, F16), "LZ": _sb(4 * 160, F16), "S1": _sb(128, F16), "S2": _sb(128, F16),
     "BC": _sb(256, F32), "DUMP": _sb(16, F32), "B64": _sb(16, F32), "ZR": _sb(256, F32), "PO": _sb(16, U16),
     "TOP": _sb(260, F32), "EX": _sb(256, F32), "MM": _sb(256, F32), "NN": _sb(260, F32),
     "TA": _sb(72, F32), "TB": _sb(64, F32), "TC": _sb(64, F32), "MK": _sb(64, F32),
-    "NH": _sb(256, F16), "TR": ("sbuf", [128, 8, 2, 16], F16), "FF": _sb(20, F32), "FA": _sb(48, F32), "SO": _sb(16, U16), "SRC": _sb(256, F32),
+    "NH": _sb(264, F16), "TR": ("sbuf", [128, 8, 2, 16], F16), "FF": _sb(20, F32), "FA": _sb(48, F32), "SO": _sb(16, U16), "SRC": _sb(256, F32),
     "HL": _sb(512, BF),
-    "LW": _sb(1024, I32), "EU": _sb(256, U16), "GO": _sb(256, U16), "GN": _sb(256, U16), "IN": _sb(256, U16), "HT": _sb(512, BF), "HN": _sb(1024, BF),
+    "LW": _sb(1024, F32), "EU": _sb(256, U16), "GO": _sb(256, U16), "GN": _sb(256, U16), "IN": _sb(256, U16), "HT": _sb(512, BF), "HN": _sb(1024, BF),
     "MO": _sb(256, F16), "ML": _sb(9 * 256, F16), "MU": _sb(256, U16), "MV": _sb(128, U16), "MH": _sb(264, F16),
-    "ACC": _sb(32, F32), "EL": _sb(8, F32), "CS": _sb(16, U16), "CU": _sb(256, U16),
+    "ACC": _sb(72, F32), "EL": _sb(8, F32), "CS": _sb(16, U16), "CU": _sb(256, U16),
     "DU": _sb(256, U16), "IX": _sb(256, U16), "RHO": _sb(8, F32), "RB": _sb(8, F32), "RT": _sb(192, F32),
+    "LENT": ("dram", [2, 128, 2048], BF),
     "PA": ("psum", [128, 512], F32), "PB": ("psum", [128, 512], F32), "PD": ("psum", [128, 512], F32),
     "P0": ("psum", [128, 1024], F32), "P1": ("psum", [128, 1024], F32),
     "P4": ("psum", [128, 16, 2, 16], F32),
 }
-REMOTE = (["g%d" % t for t in range(3)] + ["i"]
-          + ["m%d_%d" % (t, h) for t in range(3) for h in range(2)] + ["x%d" % t for t in range(4)]
-          + ["b%d_%d" % (t, q) for t in range(4) for q in range(4)] + ["u%d" % q for q in range(4)]
-          + ["s%d" % t for t in range(2)] + ["f%d_%d" % (e, tr) for e in (1, 2) for tr in range(2)])
-SEMAPHORES = ["pe", "dve", "act", "pool"] + ["r" + k for k in REMOTE] + ["q%d" % i for i in range(100)]
+REMOTE = (["g%d" % t for t in range(3)] + ["a0", "a1"] + ["c_%d" % q for q in range(4)]
+          + ["m%d_%d" % (t, h) for t in range(3) for h in range(2)] + ["x%d" % t for t in range(1, 4)]
+          + ["b%d_%d" % (t, q) for t in range(4) for q in range(4)] + ["u%d_%d" % (q, h) for q in range(4) for h in range(2)]
+          + ["s%d" % t for t in range(2)] + ["n%d" % t for t in range(2)] + ["%s%d" % (k, t) for t in range(2) for k in "fhl"])
+SEMAPHORES = ["pe", "dve", "act", "pool"] + ["r" + k for k in REMOTE] + ["q%d" % i for i in range(90)]
 
 
 def _bits(m):
@@ -53,31 +53,23 @@ def _helper(core, T, topo):
     return [c for c in topo.cores_of(core) if topo.die(c) == topo.die(core) and T.rank_of(c) is None][0]
 
 
-def _folded(T, tr):
-    return T.MP[:] if tr == 0 else T.D[:, W:2 * W]
-
-
-def _parked(T, e, tr):
-    return (T.G1, T.G2, T.WG, T.XP)[2 * e - 2 + tr][:]
-
-
 def helper_program(g, core, owner, T, topo):
     rid, pid, _ = topo.addr(owner)
     r = T.rank_of(owner)
+    side = int(r > [T.rank_of(c) for c in T.cores if c != owner and topo.chip(c) == topo.chip(owner)][0])
     m = topo.mask(core, owner)
-    n = len(_bits(m))
     far = [c for c in T.cores if topo.chip(c) != topo.chip(owner)][0]
-    k = 0
-    for e in range(4):
-        g.wait_ge(T.sem["rb%d_%d" % (e, r)], len(_bits(topo.mask(owner, core) & ~topo.mask(owner, far))))
-        dst = (T.MP if e else T.MS)[:, 1024 * r:1024 * r + 1024]
-        g.remote_dma(dst, T.X[:, 1024 * e:1024 * e + 1024], T.sem["rb%d_%d" % (e, r)], T.sem.q0, pid, rid, m)
-        k += 1
-        for tr in (FOLDED if e in (1, 2) else ()):
-            g.wait_ge(T.sem["rf%d_%d" % (e, tr)], len(_bits(topo.mask(owner, core))))
-            g.remote_dma(_folded(T, tr), _parked(T, e, tr), T.sem["rf%d_%d" % (e, tr)], T.sem.q0, pid, rid, m)
-            k += 1
-    g.wait_ge(T.sem.q0, k * n)
+    n_in = len(_bits(topo.mask(owner, core) & ~topo.mask(owner, far)))
+    g.wait_ge(T.sem["rc_%d" % r], n_in)
+    g.remote_dma(T.MS[:, 2048 + 512 * r:2560 + 512 * r], T.X[:, 0:512], T.sem["rc_%d" % r], T.sem.q0, pid, rid, m)
+    for t in range(3):
+        s = T.sem["rb%d_%d" % (t + 1, r)]
+        g.wait_ge(s, n_in)
+        g.remote_dma(T.MP[:, 1024 * r:1024 * r + 1024], T.X[:, 1024 * t + 1024:1024 * t + 2048], s, T.sem.q0, pid, rid, m)
+        if t < 2:
+            g.wait_ge(T.sem["rf%d" % t], len(_bits(topo.mask(owner, core))))
+            g.remote_dma(T.G1[:, 2048 * side:2048 * side + 2048], T.G1[:, 2048 * t:2048 * t + 2048], T.sem["rf%d" % t], T.sem.q0, pid, rid, m)
+    g.wait_ge(T.sem.q0, 6 * len(_bits(m)))
 
 
 def rank_program(g, core, T, topo):
@@ -103,21 +95,32 @@ def rank_program(g, core, T, topo):
 
     def deps(q, rd, wr, inorder):
         for k in rd:
-            if k in lastw and not (q == "pe" and lastw[k][0] == "pe"):
-                wait(q, lastw[k])
+            for tok in lastw.get(k, []):
+                if not (q == "pe" and tok[0] == "pe"):
+                    wait(q, tok)
         for k in wr:
-            for tok in ([lastw[k]] if k in lastw else []) + readers.get(k, []):
+            for tok in lastw.get(k, []) + readers.get(k, []):
                 if not (inorder and tok[0] == q):
                     wait(q, tok)
 
-    def done(tok, rd, wr):
+    def done(tok, rd, wr, more=False):
         for k in rd:
             readers.setdefault(k, []).append(tok)
         for k in wr:
-            lastw[k] = tok
+            lastw[k] = lastw[k] + [tok] if more else [tok]
             readers[k] = []
 
+    held = []
+
+    def later(*fns):
+        held.append([])
+        for f in fns:
+            f()
+        return held.pop()
+
     def op(q, fn, rd, wr):
+        if held:
+            return held[0].append(lambda: op(q, fn, rd, wr))
         ps = [k for k in rd if k[0] == "P" and len(k) == 2]
         deps(q, rd, wr, q == "pe")
         for k in ps:
@@ -140,6 +143,8 @@ def rank_program(g, core, T, topo):
         done((s, 16), rd, wr)
 
     def dma2(q, pairs, rd, wr):
+        if held:
+            return held[0].append(lambda: dma2(q, pairs, rd, wr))
         deps(q, rd, wr, False)
         s = fresh()
         for out, in_ in pairs:
@@ -150,9 +155,9 @@ def rank_program(g, core, T, topo):
     def back(out, in_):
         return [(out[0:112], in_[16:128]), (out[112:128], in_[0:16])]
 
-    def arrive(key, n, wr):
-        cnt["r" + key] = n
-        done(("r" + key, n), [], wr)
+    def arrive(key, n, wr, more=False):
+        cnt["r" + key] = cnt.get("r" + key, 0) + n
+        done(("r" + key, cnt["r" + key]), [], wr, more)
 
     def send(trs, rd, extra=()):
         deps("pool", list(rd) + list(extra), [], False)
@@ -226,8 +231,9 @@ def rank_program(g, core, T, topo):
     others = [(r + k) % N for k in range(1, N)]
     far = [q for q in others if topo.chip(T.cores[q]) != topo.chip(core)]
     near = [q for q in others if q not in far]
-    last = far + near + [r]
     side = int(r > near[0])
+    far = sorted(far, reverse=bool(side))
+    last = far + near + [r]
     mine, theirs = [2 * side, 2 * side + 1], [2 - 2 * side, 3 - 2 * side]
     hc = _helper(core, T, topo)
     m_far = topo.mask(core, T.cores[far[0]])
@@ -235,7 +241,6 @@ def rank_program(g, core, T, topo):
     fb = _bits(m_far)
     m_half = [sum(1 << e for e in fb[:len(fb) // 2]), sum(1 << e for e in fb[len(fb) // 2:])]
     n_far, n_near = len(fb), len(_bits(m_near))
-    N_X = 2 * n_far + n_near
     prev, nxt = (r - 1) % N, (r + 1) % N
 
     def mk(q):
@@ -245,12 +250,13 @@ def rank_program(g, core, T, topo):
         return n_far if q in far else n_near
 
     dma2("sp", back(T.GS, T.gam), [], ["GS"])
-    for c in last:
-        dma2("sp" if c in far else "act", [(rows(T.D, 0, 112, c), rows(T.xs, 16, 128, c)), (rows(T.D, 112, 128, c), rows(T.xs, 0, 16, c))], [], ["D.%d" % c])
-    dma("act", T.EI[:], T.ew[:, 0:256], [], ["EI"])
+    for p in range(2):
+        a = slice(2048 * p, 2048 * p + 2048)
+        dma2("sp", [(T.D[0:112, a], T.xs[16:128, a]), (T.D[112:128, a], T.xs[0:16, a])], [], ch("D", (2 * p, 2 * p + 1)))
+    dma("sp", T.GA[:], T.gam[:], [], ["GA"])
+    dma("sp", T.EI[:], T.ew[:, 0:256], [], ["EI"])
     dma("sp", T.X[:], T.xs[:], [], ch("X"))
     dma("sp", T.PAY[:], T.pay[:], ["X.0"], ["pay"])
-    dma("sp", T.GA[:], T.gam[:], [], ["GA"])
     dma("sp", T.RHO[:, 0:5], T.rho[:], [], ["RHO"])
 
     op("pool", lambda: g.iota(T.PI[:, 0:1], [[0, 1]], 0, 1), [], ["PI0"])
@@ -297,38 +303,59 @@ def rank_program(g, core, T, topo):
                 mm(T.P4[:, 0:8, z, :], T.LZ[:, o:o + 128], T.TR[:, :, gb, :], gb == 0, gb == 1, ["TR", key + str(z)], ["P4"])
 
     def to_blocks(src, key):
-        ts(T.NH[:], src.indirect(T.PO[:]), -2048.0, None, A.add, None, [key, "po"], ["NH"])
-        turn(T.TR[:], T.NH[:], ["NH"], ["TR"])
+        ts(T.NH[:, 0:256], src.indirect(T.PO[:]), -2048.0, None, A.add, None, [key, "po"], ["NH"])
+        turn(T.TR[:], T.NH[:, 0:256], ["NH"], ["TR"])
         regroup(320, "LP")
 
     def x_src(e, c):
         return (c4(T.D, c), "D.%d" % c) if e < 3 else (c4(T.XP, c), "XP.%d" % c)
 
-    def send_x(e, cs):
-        trs = []
-        for c in cs:
-            m = m_half[far.index(c)] if c in far and len(cs) > 1 else mk(c)
-            trs.append(([T.cores[c]], m, "x%d" % e, [x_src(e, c)[0]], [c4(T.LX, (r - c) % N - 1, 3072 * (e % 2))], 0))
-        send(trs, [x_src(e, c)[1] for c in cs], ["fold", "MR"])
+    def send_x(e, c):
+        send([([T.cores[c]], mk(c), "x%d" % e, [x_src(e, c)[0]], [c4(T.LX, (r - c) % N - 1, 3072 * (e % 2))], 0)],
+             [x_src(e, c)[1]], ["fold", "MR"])
 
-    def fold_x(e, n):
-        arrive("x%d" % e, n, ["LX"])
+    def fold_x(e):
+        arrive("x%d" % e, sum(nk(q) for q in others), ["LX"])
         srcs = [x_src(e, r)[0]] + [c4(T.LX, k, 3072 * (e % 2)) for k in range(3)]
-        Mb, mkey = (T.MP, "MP") if e else (T.MS, "MS")
         key = "b%d_%d" % (e, r)
-        lastw["fold"] = send([([T.cores[q] for q in far], m_far, key, srcs, [c4(Mb, r)] * len(far), 2),
-                              ([hc] + [T.cores[q] for q in near], m_near, key, srcs, [c4(T.X, e)] + [c4(Mb, r)] * len(near), 2)], ["LX", x_src(e, r)[1]])
+        lastw["fold"] = [send([([T.cores[q] for q in far], m_far, key, srcs, [c4(T.MP, r)] * len(far), 2),
+                               ([hc, T.cores[near[0]]], m_near, key, srcs, [c4(T.X, e), c4(T.MP, r)], 2)], ["LX", x_src(e, r)[1]])]
         for q in range(N):
-            arrive("b%d_%d" % (e, q), len(_bits(topo.mask(hc, core))) if q == r else nk(q), ["%s.%d" % (mkey, q)])
+            arrive("b%d_%d" % (e, q), len(_bits(topo.mask(hc, core))) if q == r else nk(q), ["MP.%d" % q])
 
     def send_g(t):
         dma("sp", T.HT[:], T.G1[0::8, :], ch("G1"), ["HT"])
         send([([T.cores[prev]], mk(prev), "g%d" % t, [T.HT[:]], [T.HN[:, 512 * t - 512:512 * t]], 0)], ["HT"])
         arrive("g%d" % t, nk(nxt), ["HN%d" % t])
 
+    def piece(t, p, q):
+        return t[:, 2048 * p + 512 * q:2048 * p + 512 * q + 512]
+
+    def send_first(p):
+        send([([T.cores[q]], m_near if q in near else m_half[far.index(q)], "a%d" % p, [piece(T.D, p, q)], [piece(T.LX, 0, 3 * p + (r - q) % N - 1)], 0)
+              for q in others], ch("D", (2 * p, 2 * p + 1)))
+
+    def fold_first(p):
+        arrive("a%d" % p, n_far + n_near, ["LX%d" % p])
+        srcs = [piece(T.D, p, r)] + [piece(T.LX, 0, 3 * p + k) for k in range(3)]
+        key, to = "%s_%d" % (("b0", "c")[p], r), piece(T.MS, p, r)
+        lastw["fold"] = lastw.get("fold", []) + [send([([T.cores[q] for q in far], m_far, key, srcs, [to] * len(far), 2),
+                                                       ([hc] * p + [T.cores[near[0]]], m_near, key, srcs, [piece(T.X, 0, 0)] * p + [to], 2)],
+                                                      ["LX%d" % p] + ch("D", (2 * p, 2 * p + 1)))]
+        for q in range(N):
+            arrive("%s_%d" % (("b0", "c")[p], q), len(_bits(topo.mask(hc, core))) if p and q == r else nk(q), ["MS.%d" % (2 * p + q // 2)], q % 2)
+
+    def hand_back(key, part, pk):
+        key = "%s_%d" % (key, near[0])
+        wait("pool", ("r" + key, n_near))
+        tok = send([([T.cores[near[0]]], m_near, key, [part], [part], 0)], [])
+        lastw["fold"].append(tok)
+        done(tok, [pk], [])
+
     send([([T.cores[prev]], mk(prev), "g0", [T.GS[:]], [T.TJ[:]], 0)], ["GS"])
     arrive("g0", nk(nxt), ["TJ"])
-    send_x(0, far + near)
+    send_first(0)
+    send_first(1)
 
     def emat(k, a, b):
         ts(T.EE[:, 144 * k:144 * k + 144], T.CI[:, 0:144], col(a), col(b), A.is_equal, A.mult, ["CI", "c%d" % a, "c%d" % b], ["E%d" % k])
@@ -363,22 +390,25 @@ def rank_program(g, core, T, topo):
         ts(col(3), col(2), 15.0, None, A.add, None, ["c2"], ["c3"])
         ts(col(14), T.OH[:, 0:1], -17.0, 1.0, A.mult, A.add, ["OH"], ["c14"])
         emat(4, 3, 14)
+        ts(T.EE[:, 864:1008], T.CI[:, 0:144], col(3), None, A.is_equal, None, ["CI", "c3"], ["E6"])
+
+        ts(T.IDF[:], T.CI[:, 0:128], col(0), None, A.is_equal, None, ["CI", "c0"], ["IDF"])
+
+    def identities():
+        for k, v in (("ID", 1.0), ("NID", -1.0), ("ID2", 2.0), ("I32", 1.0 / 32)):
+            act(T[k][:], T.IDF[:], AF.Copy, ["IDF"], [k], scale=v)
 
     def consts4():
-        ts(T.IDF[:], T.CI[:, 0:128], col(0), None, A.is_equal, None, ["CI", "c0"], ["IDF"])
-        cp(T.ID[:], T.IDF[:], ["IDF"], ["ID"])
-        ts(T.NID[:], T.IDF[:], -1.0, None, A.mult, None, ["IDF"], ["NID"])
-        ts(T.ID2[:], T.IDF[:], 2.0, None, A.mult, None, ["IDF"], ["ID2"])
         ts(T.GM4[:], T.CG[:, 0:128], col(2), 4.0, A.is_equal, A.mult, ["CG", "c2"], ["GM4"])
-        ts(T.KC[:], T.CI[:, 0:8], -4.0, 0.0, A.add, A.max, ["CI"], ["KC"])
-        ts(T.B64[:], T.DUMP[:], -4096.0, 4.0, A.add, A.mult, ["DUMP"], ["B64"])
+        ts(T.KC[:], T.CI[:, 0:4], -1.5, None, A.add, None, ["CI"], ["KC"])
+        ts(T.B64[:], T.DUMP[:], -4095.625, 4.0, A.add, A.mult, ["DUMP"], ["B64"])
         ts(T.LW[:, 0::4], T.CI[:], 16.0, col(1), A.mult, A.add, ["CI", "c1"], ["LW.0"])
         weight(15, 0)
         emat(0, 3, 15)
 
     def places():
         for k, (pat, base) in enumerate((([[1, 4], [0, 64]], 0), ([[0, 4], [1, 64]], 0), ([[0, 4], [1, 64]], 1))):
-            op("pool", lambda: g.iota(T.G2[:, 256 * k:256 * k + 256], pat, base, 0, allow_small_or_imprecise_dtypes=True), [], ["PL%d." % k])
+            op("pool", lambda k=k, pat=pat, base=base: g.iota(T.G2[:, 256 * k:256 * k + 256], pat, base, 0, allow_small_or_imprecise_dtypes=True), [], ["PL%d." % k])
         ts(col(25), col(1), 4.0, None, A.mult, None, ["c1"], ["c25"])
         ts(T.G2[:, 0:256], T.G2[:, 0:256], col(25), None, A.add, None, ["PL0.", "c25"], ["PL0."])
         dma2("sp", [(T.WG[row::16, :], T.G2[:, 256 * k:256 * k + 256]) for row, k in ((1, 0), (2, 0), (4, 0), (9, 1), (12, 1), (10, 2))],
@@ -386,16 +416,17 @@ def rank_program(g, core, T, topo):
         dma2("sp", [(T.WG[a::b, :], T.xs[a::b, :]) for a, b in ((3, 4), (5, 8), (6, 8))], [], ["WGg"])
 
     def own_rows():
-        ts(T.TJ[:], T.TI[:], 6, None, A.logical_shift_right, None, ["TI"], ["TJ"])
-        ts(T.KI[:], T.TI[:], 63, None, A.bitwise_and, None, ["TI"], ["KI"])
-        cp(T.HL[:, 0:256], T.TJ[:], ["TJ"], ["HL0"])
-        cp(T.HL[:, 256:512], T.KI[:], ["KI"], ["HL1"])
-        dma2("sp", [(T.WG[8 * k + 16::16, :], T.HL[0:112, 256 * k:256 * k + 256]) for k in range(2)]
-             + [(T.WG[8 * k:8 * k + 1, :], T.HL[112:128, 256 * k:256 * k + 256]) for k in range(2)], ["HL0", "HL1", "WGg"], ["WGr"])
+        ts(T.TI[:], T.P4[:, 0:8, :, :], 2048.0, None, A.add, None, ["P4"], ["TI"])
+        ts(T.KI[:], T.TI[:], 6, None, A.logical_shift_right, None, ["TI"], ["KI"])
+        ts(T.TI[:], T.TI[:], 63, None, A.bitwise_and, None, ["TI"], ["TI"])
+        cp(T.HL[:, 0:256], T.KI[:], ["KI"], ["HL0"])
+        cp(T.HL[:, 256:512], T.TI[:], ["TI"], ["HL1"])
+        dma2("sp", [(T.WG[8 * k::16, :], T.HL[:, 256 * k:256 * k + 256]) for k in range(2)], ["HL0", "HL1"], ["WGr"])
 
     def consts5():
         ts(T.QI[:], T.IDF[:], 0.25, None, A.mult, None, ["IDF"], ["QI"])
         ms(T.CM[:], -0.375, ["CM"])
+        act(T.GN4[:], T.GM4[:], AF.Copy, ["GM4"], ["GN4"], scale=-1.0)
         ts(T.PI[:, 3:4], T.PI[:, 0:1], 112.0, None, A.add, None, ["PI0"], ["PI3"])
         weight(16, 1)
         ts(T.PI[:, 3:4], T.PI[:, 3:4], 127, None, A.bitwise_and, None, ["PI3"], ["PI3"])
@@ -416,7 +447,6 @@ def rank_program(g, core, T, topo):
         ts(T.S2[:], T.CI[:, 0:128], col(3), T.OH[:, 0:1], A.is_equal, A.mult, ["CI", "c3", "OH"], ["S2"])
         tt(T.S1[:], T.T1[:, 0:128], T.IDF[:], A.subtract, ["T1", "IDF"], ["S1"])
         ts(T.MH[:, 256:257], col(0), 0.0, -8192.0, A.mult, A.add, ["c0"], ["MHe"])
-        ts(T.I32[:], T.IDF[:], 1.0 / 32, None, A.mult, None, ["IDF"], ["I32"])
         cp(T.RB[:, 1:6], T.RHO[:, 0:5], ["RHO"], ["RBa"])
         cp(T.RB[:, 0:1], T.RHO[:, 1:2], ["RHO"], ["RBb"])
         rt = ["RT1.%d" % a for a in range(9)]
@@ -426,28 +456,57 @@ def rank_program(g, core, T, topo):
         ts(T.RT[:, 0:54], T.RT[:, 64:118], 32.0, None, A.mult, None, rt, ["RT0"])
         ts(T.RT[:, 128:182], T.RT[:, 64:118], 1.0 / 128, None, A.mult, None, rt, ["RT2", "RT1"])
 
-    def chain(Wa, Wr, wkey, u):
+    def bits_of(out, win, off, c, rd, key, n, mult=None):
+        def one(i):
+            a, b = 1024 * c + 1024 // n * i, 1024 * c + 1024 // n * (i + 1)
+            wr = [key] if i == 0 else []
+            if mult:
+                tt(out[:, a:b], win.indirect(off[:, a // 16:b // 16]), out[:, a:b], A.mult, rd + [key] * (i == 0), wr)
+            else:
+                cp(out[:, a:b], win.indirect(off[:, a // 16:b // 16]), rd, wr)
+            lastw[key] = [("dve", cnt["dve"])]
+        return [lambda i=i: one(i) for i in range(n)]
+
+    def chain(Wa, Wr, wkey, u, fill=()):
+        fill = list(fill)
+
+        def gap():
+            if fill:
+                fill.pop(0)()
         scan(T.TOP[:, 1:257], Wa, T.ZR[:], 0.0, A.max, A.max, [wkey, "ZR"], ["TOP"])
+        gap()
         turn(T.TA[:, 1:33], T.TOP[:, 225:257], ["TOP"], ["TA0"])
+        gap()
         scan(T.TB[:, 0:32], T.TA[:, 0:32], T.MK[:, 0:32], 0.0, A.max, A.mult, ["TA0", "MK"], ["TB0"])
+        gap()
         turn(T.TC[:, 0:32], T.TB[:, 0:32], ["TB0"], ["TC0"])
+        gap()
         ts(T.EX[:], T.TOP[:, 0:256], T.TC[:, 31:32], None, A.max, None, ["TOP", "TOP0", "TC0"], ["EX"])
+        gap()
         tt(T.MM[:], T.EX[:], Wa, A.is_ge, ["EX", wkey], ["MM"])
+        gap()
         scan(T.NN[:, 255::-1], T.MM[:, ::-1], Wr, 4096.0, A.mult, A.max, ["MM", wkey], ["NN"])
+        gap()
         turn(T.TA[:, 36:68], T.NN[:, 0:32], ["NN"], ["TA1"])
         ts(T.NN[:, 0:1], T.NN[:, 0:1], col(5), None, A.mult, None, ["NN", "c5"], ["NN"])
         scan(T.TB[:, 63:31:-1], T.TA[:, 68:36:-1], T.MK[:, 63:31:-1], 4096.0, A.min, A.max, ["TA1", "MK2"], ["TB1"])
+        gap()
         turn(T.TC[:, 32:64], T.TB[:, 32:64], ["TB1"], ["TC1"])
-        ts(T.NH[:], T.NN[:, 0:256], T.TC[:, 32:33], -2048.0, A.min, A.add, ["NN", "TC1"], ["NH"])
+        gap()
+        ts(T.NH[:, 0:257], T.NN[:, 0:257], T.TC[:, 32:33], -2048.0, A.min, A.add, ["NN", "NNe", "TC1"], ["NH"])
         ts(T.FF[:, 0:17], T.NN[:, 0:257:16], T.TC[:, 32:33], None, A.min, None, ["NN", "NNe", "TC1"], ["FF"])
-        turn(T.TR[:], T.NH[:], ["NH"], ["TR"])
+        turn(T.TR[:], T.NH[:, 0:256], ["NH"], ["TR"])
         regroup(0, "LZ")
         tt(T.FA[:, 0:16], T.FF[:, 0:16], T.FF[:, 1:17], A.is_ge, ["FF"], ["FA0"])
+        gap()
         tt(T.FA[:, 16:32], T.FA[:, 0:16], T.DUMP[:], A.mult, ["FA0", "DUMP"], ["FA1"])
+        gap()
         tt(T.FA[:, 32:48], T.FA[:, 16:32], T.FF[:, 0:16], A.max, ["FA1", "FF"], ["FA2"])
-        cp(T.SO[:], T.FA[:, 32:48], ["FA2"], ["SO"])
         tt(T.SRC[:], T.BC[:], T.P4[:, 0:8, :, :], A.add, ["BC", "P4"], ["SRC"])
+        cp(T.SO[:], T.FA[:, 32:48], ["FA2"], ["SO"])
+        gap()
         ts(T.SW[:].indirect(T.SO[:]), T.SRC[:], KK(u), 0.0, A.mult, A.add, ["SO", "SRC"], ["SW", "SW0", "SW1", "SW2", "SW3", "SW4"])
+        return fill
 
     def wr_pass(bank, o, e, src, skey, c, n=1):
         for i in range(16):
@@ -467,8 +526,8 @@ def rank_program(g, core, T, topo):
     def run_out(u, c):
         act(c4(T.RR, c), c4(T.ST, c), AF.Relu, ["ST.%d" % c, "c12"], ["RR.%d" % c], bias=col(12), scale=-1.0 / KK(u))
 
-    def evac_i(out, key):
-        ts(out, pb("PB", 0, 256), MAG + 4096, MAG, A.add, A.subtract, ["PB"], [key])
+    def evac_i():
+        ts(T.IN[:], pb("PB", 0, 256), MAG + 4096, MAG, A.add, A.subtract, ["PB"], ["IN"])
 
     def evac_m(t, h):
         a = slice(128 * h, 128 * h + 128)
@@ -484,8 +543,12 @@ def rank_program(g, core, T, topo):
     ring, jk = [0], [0]
     LIST = {1: (T.EU, "EU"), 2: (T.GN, "GN"), 3: (T.IN, "IN")}
 
+    HOME = {0: ("X", 0), 1: ("D", 4), 2: ("G1", 0), 3: ("XP", 0)}
+    SUMS = {0: ("PB", "G1"), 3: ("PA", "XP")}
+
     def slot(tr, c):
-        return (c4(T.XP, c), "XP.%d" % c) if tr == 3 else (c4(T.D, c, W * (2 - tr)), "D.%d" % (c + 4 * (2 - tr)))
+        b, k = HOME[tr]
+        return c4(T[b], c + k), "%s.%d" % (b, c + k)
 
     def acc(tr, j):
         return T.ACC[:, 4 * j + tr:4 * j + tr + 1], "A%d.%d" % (tr, j)
@@ -506,71 +569,96 @@ def rank_program(g, core, T, topo):
         d, dk = slot(tr, c)
         gat("act", d, T.X[:], o4(LIST[tr][0], c), ch("X") + [LIST[tr][1]], [dk])
 
-    def size_pe(q, tr, c):
-        d, dk = (c4(T.X, c), "X.%d" % c) if tr == 0 else slot(tr, c)
+    def size_pe(tr, c, junk="MP"):
+        dk = slot(tr, c)[1]
         ring[0] += 1
         B, keys = (T.P0, ["P0", "P5"]) if ring[0] % 2 else (T.P1, ["P1", "P6"])
-        src = T.X if tr == 0 else (T.XP if tr == 3 else T.D)
-        base = 1024 * c + (0 if tr in (0, 3) else W * (2 - tr))
+        src, base = T[HOME[tr][0]], 1024 * (c + HOME[tr][1])
         for i in range(2):
             out = B[:, 512 * i:512 * i + 512]
             mm(out, T.ID[:], src[:, base + 512 * i:base + 512 * i + 512], True, False, ["ID", dk], [keys[i]])
             mm(out, T.NID[:], T.MS[:, 1024 * c + 512 * i:1024 * c + 512 * i + 512], False, True, ["NID", "MS.%d" % c], [keys[i]])
         a, ak = acc(tr, 2 * c)
-        if q == "act":
-            jk[0] += 1
-            act(c4(T.MP, jk[0] % 4), B[:], AF.Abs, keys, ["MP.%d" % (jk[0] % 4), ak], accum_out=a)
+        jk[0] += 1
+        act(c4(T[junk], jk[0] % 4), B[:], AF.Abs, keys, ["%s.%d" % (junk, jk[0] % 4), ak], accum_out=a)
+
+    def lend_x(t):
+        deps("pool", [], ch("G1") + ["G1x", "G1n"], False)
+        send([([T.cores[near[0]]], topo.mask(core, T.cores[near[0]]), "l%d" % t, [T.X[:, 1024 * theirs[0]:1024 * theirs[0] + 2048]],
+               [T.LENT[t]], 0)], ch("X", theirs))
+        arrive("l%d" % t, len(_bits(topo.mask(T.cores[near[0]], core))), ["lent"])
+
+    def fold_max(t, own):
+        a = slice(2048 * side, 2048 * side + 2048)
+        if own:
+            send([([hc], topo.mask(core, hc), "f%d" % t, [T.X[:, a], T.MS[:, a]], [T.G1[:, 2048 * t:2048 * t + 2048]], 2)], ch("X", mine) + ch("MS", mine))
+            return arrive("f%d" % t, len(_bits(topo.mask(hc, core))), ch("G1", mine))
+        send([([T.cores[near[0]]], topo.mask(core, T.cores[near[0]]), "h%d" % t, [T.LENT[t], T.MS[:, a]], [T.G1[:, a]], 2)], ch("MS", mine) + ["lent"])
+        arrive("h%d" % t, len(_bits(topo.mask(T.cores[near[0]], core))), ch("G1", theirs))
+
+    def add_up(tr, c, first=False, end=False):
+        b, sk = SUMS[tr]
+        for i in range(4):
+            a = 1024 * c + 256 * i
+            mm(pb(b, 0, 256), T.ID2[:], T[sk][:, a:a + 256], first and i == 0, end and i == 3,
+               ["ID2", "%s.%d" % (sk, c)] + ["XPz"] * (tr == 3 and end and i == 3), [b])
+
+    def inverse_sum(step):
+        if step == 0:
+            tt(T.EX[:], T.NH[:, 0:256], T.NH[:, 1:257], A.subtract, ["NH"], ["EX"])
+        elif step == 1:
+            tt(T.MM[:], T.EX[:], T.PA[:, 0:256], A.mult, ["EX", "PA"], ["MM"])
         else:
-            red(a, B[:], A.add, keys, [ak], apply_absolute_value=True)
+            red(acc(3, 1)[0], T.MM[:], A.add, ["MM"], [acc(3, 1)[1]])
 
-    def sum_pe(tr, l, lkey, src, base, keys, first=False, end=False):
-        b = ("P0", "P5")[tr]
-        for i in range(8):
-            mm(pb(b, 0, 512), l[:], src[:, base + 512 * i:base + 512 * i + 512], first and i == 0, end and i == 7, [lkey, keys[i // 2]], [b])
+    def greater(c, end=False):
+        a, b = 1024 * c, 1024 * c + (768 if end else 1024)
+        tt(T.XP[:, a:b], T.X[:].indirect(T.IN[:, a // 16:b // 16]), T.MS[:, a:b], A.max, ch("X") + ["IN", "MS.%d" % c], ["XP.%d" % c])
+        if end:
+            tt(T.XP[:, b:b + 256], T.X[:].indirect(T.IN[:, b // 16:b // 16 + 16]), T.MS[:, b:b + 256], A.max, ch("X") + ["IN", "MS.%d" % c], ["XPz"])
 
-    def trial_of(tr):
-        return (T.X, 0, ch("X")) if tr == 0 else (T.D, W, ch("D", range(4, 8)))
+    def size_sum(tr, j=3, b=None):
+        b = b or SUMS[tr][0]
+        red(acc(tr, j)[0], pb(b, 0, 256), A.add, [b], [acc(tr, j)[1]])
 
-    def fold_max(e, tr):
-        src, base, keys = trial_of(tr)
-        back_keys = ch("MP") if tr == 0 else keys
-        deps("pool", [], back_keys, False)
-        key = "f%d_%d" % (e, tr)
-        send([([hc], topo.mask(core, hc), key, [src[:, base:base + W], T.MS[:]], [_parked(T, e, tr)], 2)], keys + ch("MS"))
-        arrive(key, len(_bits(topo.mask(hc, core))), back_keys)
+    def clear_sums(n):
+        ms(T.ACC[:, 0:4 * n], 0.0, ["A%d.%d" % (tr, j) for tr in range(4) for j in range(n)])
 
-    def sum_max(tr):
-        src, base, keys = (T.MP, 0, ch("MP")) if tr == 0 else trial_of(tr)
-        sum_pe(tr, T.ID2, "ID2", src, base, keys, end=True)
+    def tally(js, first=False, end=False):
+        if first:
+            mm(T.P4[:, 8, 0, 0:4], T.IDF[:], T.KC[:], True, False, ["IDF", "KC"], ["P4"])
+        for j in js:
+            gm = "GM4" if j < 14 else "GN4"
+            for z in range(2 if j in (8, 11) else 1):
+                mm(T.P4[:, 8, 0, 0:4], T[gm][:], T.ACC[:, 4 * j + z:4 * j + z + 4], False, end and j == js[-1], [gm] + ["A%d.%d" % (tr, j) for tr in range(4)], ["P4"])
 
-    def size_sum(q, tr):
-        b = ("P0", "P5")[tr]
-        a, ak = acc(tr, 0)
-        if q == "act":
-            act(T.HL[:], pb(b, 0, 512), AF.Copy, [b], ["HL0", "HL1", ak], accum_out=a)
-        else:
-            red(a, pb(b, 0, 512), A.add, [b], [ak])
-
-    def clear_sums():
-        ms(T.ACC[:], 0.0, ["A%d.%d" % (tr, j) for tr in range(4) for j in range(8)])
-
-    def elect(t, cs):
-        mm(T.P4[:, 8, 0, 0:8], T.IDF[:], T.KC[:], True, False, ["IDF", "KC"], ["P4"])
-        for k, c in enumerate(cs):
-            for z in range(2):
-                mm(T.P4[:, 8, 0, 4 * z:4 * z + 4], T.GM4[:], T.ACC[:, 8 * c:8 * c + 4], False, k == 3 and z == 1, ["GM4"] + ["A%d.%d" % (tr, 2 * c) for tr in range(4)], ["P4"])
+    def elect():
         red(T.EL[:, 0:1], T.P4[:, 8, 0, 0:4], A.min, ["P4"], ["EL0"])
-        red(T.EL[:, 1:2], T.P4[:, 8, 0, 4:8], A.min, ["P4"], ["EL1"])
-        ts(T.CS[:], T.B64[:], T.EL[:, 1:2], T.EL[:, 0:1], A.add, A.subtract, ["B64", "EL0", "EL1"], ["CS"])
-        gat("dve", T.CU[:], T.LW[:], T.CS[:], ch("LW") + ["CS"], ["CU"])
+        ts(T.EL[:, 1:2], T.EL[:, 0:1], 0.25, MAG, A.mult, A.add, ["EL0"], ["EL1"])
+        ts(T.EL[:, 2:3], T.EL[:, 1:2], MAG, -4.0, A.subtract, A.mult, ["EL1"], ["EL2"])
+        ts(T.CS[:], T.B64[:], T.EL[:, 0:1], T.EL[:, 2:3], A.add, A.add, ["B64", "EL0", "EL2"], ["CS"])
+        ts(T.CU[:], T.LW[:].indirect(T.CS[:]), MAG, MAG, A.add, A.subtract, ch("LW") + ["CS"], ["CU"])
 
-    def gamma_c(q, c):
-        gat(q, c4(T.G1, c), T.WG[:], o4(T.CU, c), ["WGg", "WGp", "WGr", "CU"], ["G1.%d" % c])
+    def gamma_c():
+        deps("dve", [], ch("G1"), False)
+        deps("act", [], ch("G1"), False)
+        a, toks = 0, []
+        for k, n in enumerate(G1P):
+            q, key = ("dve", "act")[k % 2], "G1p%d" % k
+            gat(q, T.G1[:, a:a + n], T.WG[:], T.CU[:, a // 16:(a + n) // 16], ["WGg", "WGp", "WGr", "CU"], [key])
+            toks = toks[-1:] + lastw[key]
+            for i in range(a // 256, (a + n) // 256):
+                mm(T.PA[:, 0:256], T.EE[:, 15 - i:143 - i], T.G1[:, 256 * i:256 * i + 256], i == 0, i == 15, ["E0", key], ["PA"])
+            a += n
+        for k in ch("G1"):
+            lastw[k], readers[k] = toks, list(lastw["PA"])
 
-    def x_c(t, c, q="act"):
-        gat(q, c4(T.XP, c), T.X[:], o4(T.CU, c), ch("X") + ["CU"], ["XP.%d" % c])
+    def x_c(t, c):
+        gat("act", c4(T.XP, c), T.X[:], o4(T.CU, c), ch("X") + ["CU"], ["XP.%d" % c, "XPz"])
         if t < 2:
             dma2("sp", [(rows(T.D, 0, 112, c), rows(T.XP, 16, 128, c)), (rows(T.D, 112, 128, c), rows(T.XP, 0, 16, c))], ["XP.%d" % c], ["D.%d" % c])
+        if c != r:
+            send_x(t + 1, c)
 
     def mean(t, h):
         a = slice(128 * h, 128 * h + 128)
@@ -585,15 +673,18 @@ def rank_program(g, core, T, topo):
     def gamma_mu(q, c):
         gat(q, c4(T.G2, c), T.G1[:], o4(T.MU, c), ch("G1") + ["G1n", "G1x", "MU.%d" % (c // 2)], ["G2.%d" % c])
 
-    def x_mu(q, c):
-        gat(q, c4(T.X, c), T.XP[:], o4(T.MU, c), ch("XP") + ["MU.%d" % (c // 2)], ["X.%d" % c])
+    def x_mu(c):
+        gat("act", c4(T.X, c), T.XP[:], o4(T.MU, c), ch("XP") + ["MU.%d" % (c // 2)], ["X.%d" % c])
 
     def m_mu(t):
-        for k, c in enumerate(mine):
-            gat("act", c4(T.MS, c), T.MP[:], o4(T.MV, k), ch("MP") + ["MV"], ["MS.%d" % c])
         half = T.MS[:, 2048 * side:2048 * side + 2048]
+        act(half, T.MP[:].indirect(T.MV[:]), AF.Copy, ch("MP") + ["MV"], ch("MS", mine) + [acc(2, 8)[1]], accum_out=acc(2, 8)[0])
         send([([T.cores[near[0]]], topo.mask(core, T.cores[near[0]]), "s%d" % t, [half], [half], 0)], ch("MS", mine))
         arrive("s%d" % t, len(_bits(topo.mask(T.cores[near[0]], core))), ch("MS", theirs))
+
+    def m_sums(t):
+        send([([T.cores[near[0]]], m_near, "n%d" % t, [T.ACC[:, 32:36]], [T.ACC[:, 44:48]], 0)], ["A%d.8" % tr for tr in range(4)])
+        arrive("n%d" % t, n_near, ["A%d.11" % tr for tr in range(4)])
 
     def slope_mu(bm, o=0):
         ts(T.MH[:, 0:256], T.MU[:], -2048.0, None, A.add, None, ["MU.0", "MU.1"], ["MH"])
@@ -606,11 +697,14 @@ def rank_program(g, core, T, topo):
     def slope_m(bm, o=0):
         ts(T.T2[:], pb(bm, o, 256), -1.0, 4.0, A.max, A.min, [bm], ["T2"])
 
-    def slopes(bs, o, a=0, n=256):
+    def slopes(bs, o, a=0, n=256, steps=range(3)):
         k = "T1.%d" % a
-        ts(T.T1[:, a:a + n], pb(bs, o + a, n), -24.0, 24.0, A.max, A.min, [bs], [k, "T1"])
-        tt(T.T1[:, a:a + n], T.T1[:, a:a + n], T.T2[:, a:a + n], A.add, [k, "T2"], [k])
-        ts(T.IX[:, a:a + n], T.T1[:, a:a + n], 25.0, None, A.add, None, [k], ch("IX", range(a // 64, (a + n) // 64)))
+        if 0 in steps:
+            ts(T.T1[:, a:a + n], pb(bs, o + a, n), -24.0, 24.0, A.max, A.min, [bs], [k, "T1"])
+        if 1 in steps:
+            tt(T.T1[:, a:a + n], T.T1[:, a:a + n], T.T2[:, a:a + n], A.add, [k, "T2"], [k])
+        if 2 in steps:
+            ts(T.IX[:, a:a + n], T.T1[:, a:a + n], 25.0, None, A.add, None, [k], ch("IX", range(a // 64, (a + n) // 64)))
 
     VB = ("VD", "V", "VD")
 
@@ -626,230 +720,295 @@ def rank_program(g, core, T, topo):
         a = slice(1024 * c, 1024 * (c + n))
         dma("pool", T[VB[t]][:, a], T.MR[:, a], ["MR"], ch(VB[t], range(c, c + n)), accum_op=A.add, max_dma_last_dim=4096)
 
+    def v_add_pe(c):
+        B, keys = ((T.P0, ["P0", "P5"]), (T.P1, ["P1", "P6"]))[c % 2]
+        for i in range(2):
+            a = slice(1024 * c + 512 * i, 1024 * c + 512 * i + 512)
+            mm(B[:, 512 * i:512 * i + 512], T.ID[:], T.MR[:, a], True, False, ["ID", "MR"], [keys[i]])
+            mm(B[:, 512 * i:512 * i + 512], T.IDF[:], T.V[:, a], False, True, ["IDF", "V.%d" % c], [keys[i]])
+        act(c4(T.V, c), B[:], AF.Copy, keys, ["V.%d" % c])
+
     def p_zero(c):
         act(c4(T.PZ, c), T.PAY[:].indirect(o4(T.GO, c)), AF.Copy, ["pay", "GO"], ["pz.%d" % c], scale=16.0)
 
-    def p_gather(q, c):
-        if q == "act":
-            act(c4(T.SW, c), T.PZ[:].indirect(o4(T.GO, c)), AF.Copy, ch("pz") + ["GO.%d" % (c // 2), "SW"], ["pp%d" % c], scale=1.0 / 64)
-        else:
-            ts(c4(T.SW, c), T.PZ[:].indirect(o4(T.GO, c)), 1.0 / 64, None, A.mult, None, ch("pz") + ["GO.%d" % (c // 2), "SW"], ["pp%d" % c])
-
-    order = near + far + [r]
-    to_blocks(T.GS[:], "GS")
+    order = [1 - r // 2, r // 2, 3 - r // 2, 2 + r // 2]
     cp(T.EU[:], T.EI[:], ["EI"], ["EU"])
+    to_blocks(T.GA[:], "GA")
+    cp(T.GO[:], T.GA[:], ["GA"], ["GO"])
     consts2()
-    ts(T.T2[:], T.P4[:, 0:8, :, :], 2048.0, None, A.add, None, ["P4"], ["T2"])
+    rows_, places_ = later(own_rows), later(places)
+    for f in rows_[:1] + places_[:3]:
+        f()
+    fold_first(0)
+    fold_first(1)
+    hand_back("b0", piece(T.MS, 0, near[0]), "MS.%d" % (near[0] // 2))
     for c in order:
         raw(1, c)
-    chain(T.T2[:], T.T2[:, ::-1], "T2", 0)
-    cp(T.GN[:], T.TJ[:], ["TJ"], ["GN"])
     consts3()
-    places()
-    fold_x(0, n_far + n_near)
+    to_blocks(T.TJ[:], "TJ")
+    cp(T.GN[:], T.TJ[:], ["TJ"], ["GN"])
+    ts(T.T2[:], T.P4[:, 0:8, :, :], 2048.0, None, A.add, None, ["P4"], ["T2"])
+    identities()
+    for c in range(2):
+        p_zero(c)
+    fill = chain(T.T2[:], T.T2[:, ::-1], "T2", 0, rows_[1:] + places_[3:] + later(lambda: clear_sums(18), consts4))
+    early = [later(lambda: size_pe(tr, order[0])) for tr in (1, 0)]
     for c in range(4):
         count_down(0, c)
         run_out(0, c)
-        wr_pass("PB", 0, 4, T.RR, "RR", c)
-    cp(T.LW[:, 2::4], T.TJ[:], ["TJ"], ["LW.2"])
-    cp(T.TI[:], T.T2[:], ["T2"], ["TI"])
-    own_rows()
-    evac_i(T.LO[:], "LO")
-    send([([T.cores[prev]], mk(prev), "i", [T.LO[:]], [T.IN[:]], 0)], ["LO"])
-    arrive("i", nk(nxt), ["IN"])
-    for c in order[:RAW0]:
-        raw(2, c)
-    clear_sums()
-    consts4()
+        if c == 1:
+            for f in early[0][:4] + early[1][:4]:
+                f()
+        if c % 2:
+            wr_pass("PB", 0, 4, T.RR, "RR", c - 1, 2)
+        if fill:
+            fill.pop(0)()
+    for f in fill:
+        f()
     cp(T.LW[:, 1::4], T.EI[:], ["EI"], ["LW.1"])
-    cp(T.GO[:], T.GA[:], ["GA"], ["GO"])
-    for c in range(PZ0):
-        p_zero(c)
-    for c in order[RAW0:]:
-        if c != r:
-            diff(2, c)
+    cp(T.LW[:, 2::4], T.TJ[:], ["TJ"], ["LW.2"])
+    made = [(2, c) for c in order[:2]] + [(tr, c) for k, c in enumerate(order) for tr in (3, 2) if tr == 3 or k >= 2]
+    for k, tc in enumerate(made):
+        if k == 2:
+            evac_i()
+        diff(*tc)
     cp(T.LW[:, 3::4], T.IN[:], ["IN"], ["LW.3"])
-    for c in order:
-        diff(3, c)
-    if RAW0 < 4:
-        diff(2, r)
-    todo = [(tr, c) for c in order for tr in (1, 0, 2) if tr < 2 or c in order[:RAW0]]
-    made = [(2, c) for c in order[RAW0:3]] + [(3, c) for c in order] + [(2, r)] * (RAW0 < 4)
-    for k, tc in enumerate(todo):
-        size_pe("act", *tc)
-        if k < len(made) - DA0:
+    early[0][4]()
+    early[1][4]()
+    for k, tc in enumerate([(tr, c) for c in order[1:] for tr in (1, 0)]):
+        if k < 5:
             size("act", *made[k])
-    for tc in made[len(made) - DA0:]:
+        size_pe(*tc)
+    tally([2 * c for c in order[:2]], True)
+    for tc in made[5:]:
         size("dve", *tc)
+    tally([2 * c for c in order[2:]], end=True)
+    HOME[2] = ("D", 0)
 
     for t in range(3):
         for u in range(2 * t + 1, min(2 * t + 3, 6)):
             nk_tile(u)
-        elect(t, order)
-        for c in range(4):
-            gamma_c("dve" if c % 2 == 0 else "act", c)
-            b_pass(0, T.G1, "G1", c, c == 0, c == 3)
-        if t > 0:
-            composed("PD")
-            slope_m("PD", 256)
-            slopes("PB", 256)
+        if t:
+            v_gather(t - 1, 0)
+        elect()
+        gamma_c()
+        if t:
+            slopes("PB", 256, steps=[1, 2])
         if t < 2:
             send_g(t + 1)
-        wait("sp", lastw["PA"])
+        wait("sp", readers["G1.0"][0])
         dma("sp", T.G1[2::8, 0:W - 1], T.G1[1::8, 1:W], ch("G1"), ["G1x"])
-        for c in (far + near if t else last):
+        for c in last:
             x_c(t, c)
-            if c != r:
-                send_x(t + 1, [c])
         if t < 2:
             dma("sp", T.G1[5::8, :], T.HN[:, 512 * t:512 * t + 512], ["HN%d" % (t + 1)] + ch("G1"), ["G1n"])
             dma("sp", T.EI[:], T.ew[:, 256 * t + 256:256 * t + 512], [], ["EI"])
         if t:
-            v_gather(t - 1, 0)
-        chain(T.PA[:, 0:256], T.PA[:, 255::-1], "PA", 2 * t + 1)
+            v_gather(t - 1, 1)
+        fill = chain(T.PA[:, 0:256], T.PA[:, 255::-1], "PA", 2 * t + 1, [] if t else later(consts5))
         for c in range(4):
             count_down(2 * t + 1, c)
             run_out(2 * t + 1, c)
             wr_pass("PB" if c < 2 else "P1", 0, 4, T.RR, "RR", c)
         if t == 0:
             evac_m(t, 0)
-            consts5()
+            for f in fill:
+                f()
             evac_m(t, 1)
-            fold_x(t + 1, N_X)
-            consts6()
-            for c in range(PZ0, 4):
+            fold_x(t + 1)
+            for c in range(2, 4):
                 p_zero(c)
+            fill = later(consts6, lambda: clear_sums(8))
+            between = [fill[:8], fill[8:]]
         else:
             evac_m(t, 0)
-            x_c(t, r, "dve")
-            for c in range(1, 4):
+            v_mult(t - 1, 0)
+            for c in range(2, 4):
                 v_gather(t - 1, c)
             evac_m(t, 1)
-            if t == 1:
-                fold_x(t + 1, N_X)
-            for c in range(3):
-                v_mult(t - 1, c)
-                if t == 2:
-                    v_add(t - 1, c, 1)
             if t == 2:
+                v_add_pe(0)
+                for c in range(1, 4):
+                    if c == 3:
+                        mean(2, 0)
+                        gamma_mu("act", side)
+                        gamma_mu("act", 1 - side)
+                    v_mult(t - 1, c)
+                    if c < 3:
+                        v_add(t - 1, c, 1)
                 break
-        clear_sums()
+            fold_x(t + 1)
+            between = [[lambda: v_mult(0, 1)], [lambda: v_mult(0, 2)]]
+        for f in between[0]:
+            f()
         mean(t, 0)
-        gamma_mu("dve", 0)
+        gamma_mu("act", 0)
         gamma_mu("act", 1)
+        for f in between[1]:
+            f()
         mean(t, 1)
         a = slice(128 * side, 128 * side + 128)
         dma2("sp", [(T.MV[0:112], T.MU[16:128, a]), (T.MV[112:128], T.MU[0:16, a])], ["MU.%d" % side], ["MV"])
         gamma_mu("dve", 2)
-        x_mu("act", 0)
         gamma_mu("act", 3)
+        x_mu(0)
         for c in range(4):
             b_pass(1, T.G2, "G2", c, c == 0, c == 3)
         dma("sp", T.WG[0::4, :], T.G2[0::4, :], ch("G2"), ["WGr"])
         cp(T.EU[:], T.EI[:], ["EI"], ["EU"])
+        cp(T.LW[:, 1::4], T.EI[:], ["EI"], ["LW.1"])
         for c in range(1, 4):
-            x_mu("act" if c < 4 - XD else "dve", c)
+            if c != theirs[1]:
+                x_mu(c)
+        slope_mu("PD", 256)
         wr_pass("P1", 0, 1, T.G2, "G2", 0, 4)
-        order = mine + theirs
-        for c in order[:MK]:
-            raw(1, c)
-        m_mu(t)
-        for c in order[MK:RAW]:
-            raw(1, c)
-        chain(T.PA[:, 0:256], T.PA[:, 255::-1], "PA", 2 * t + 2)
+        fill = bits_of(T.X, T.XP[:], T.MU, theirs[1], ch("XP") + ["MU.1"], "X.%d" % theirs[1], 8)
+        if t == 1:
+            fill += bits_of(T.VD, T.RT[:, 0:54], T.IX, 3, ["RT0", "IX.3"], "VD.3", 4, True)
+        wr_pass("PD", 0, 2, T.G2, "G2", 0, 2)
+        for f in chain(T.PA[:, 0:256], T.PA[:, 255::-1], "PA", 2 * t + 2, fill):
+            f()
         cp(T.GN[:], pb("P1", 0, 256), ["P1"], ["GN"])
-        wr_pass("PD", 0, 2, T.G2, "G2", 0, 4)
-        wr_pass("PB", 256, 3, T.G2, "G2", 0, 4)
+        for c in range(4):
+            b_pass(6, T.X, "X", c, c == 0, c == 3)
+        wr_pass("PD", 0, 2, T.G2, "G2", 2, 2)
         for c in range(4):
             count_down(2 * t + 2, c)
-            run_out(2 * t + 2, c)
-        cp(T.LW[:, 1::4], T.EI[:], ["EI"], ["LW.1"])
+            if c < 3:
+                inverse_sum(c)
         cp(T.LW[:, 2::4], T.GN[:], ["GN"], ["LW.2"])
-        slope_mu("PD", 256)
+        size_sum(0, 14, "PA")
+        order = mine + theirs
+        raw(1, order[0])
+        lend_x(t)
+        m_mu(t)
+        for c in range(4):
+            run_out(2 * t + 2, c)
+        for c in order[1:]:
+            raw(1, c)
+        fold_max(t, True)
+        fold_max(t, False)
+        m_sums(t)
+        wr_pass("PB", 256, 3, T.G2, "G2", 0, 4)
+        tally([8, 1], first=True)
+        wr_pass("PB", 0, 4, T.RR, "RR", 0, 4)
+        for c in mine:
+            diff(2, c)
+        evac_i()
+        for c in theirs:
+            diff(2, c)
+        for c in mine:
+            greater(c)
+        cp(T.LW[:, 3::4], T.IN[:], ["IN"], ["LW.3"])
+        for c in theirs:
+            greater(c, c == theirs[1])
+        for k, c in enumerate(order):
+            size_pe(1, c, "RR")
+            size("act", 2, c)
+            if k == 1:
+                tally([14, 11])
+            if k >= 2:
+                add_up(0, c, k == 2)
+        add_up(3, mine[0], True)
+        add_up(3, mine[1])
+        for c in mine:
+            add_up(0, c, end=c == mine[1])
+        tally([2 * c for c in order[:3]])
+        add_up(3, theirs[0])
+        size_sum(0)
+        add_up(3, theirs[1], end=True)
+        composed("PD")
+        slope_m("PD", 256)
+        size_sum(3)
+        tally([2 * order[3], 3], end=True)
+        slopes("PB", 256, steps=[0])
         if t == 1:
-            v_mult(t - 1, 3)
-            wait("pool", lastw["MS.%d" % theirs[0]])
             v_add(0, 0, 4)
         else:
-            wait("pool", lastw["MS.%d" % theirs[0]])
             dma("pool", T.PZ[:], T.xs[:], [], ch("pz"), accum_op=A.add, max_dma_last_dim=4096)
         dma2("sp", [(T.MR[16:128], T.MS[0:112]), (T.MR[0:16], T.MS[112:128])], ch("MS"), ["MR"])
-        for c in order:
-            diff(2, c)
-        for c in order[RAW:]:
-            diff(1, c)
-        todo = [(0, c) for c in order] + [(1, c) for c in order[:RAW]]
-        made = [(2, c) for c in order] + [(1, c) for c in order[RAW:]] + [(3, c) for c in order]
-        for k in range(len(made) - DA):
-            if k < len(todo):
-                size_pe("act", *todo[k])
-            if k == 1:
-                wr_pass("PB", 0, 4, T.RR, "RR", 0, 4)
-                evac_i(T.IN[:], "IN")
-                cp(T.LW[:, 3::4], T.IN[:], ["IN"], ["LW.3"])
-                for c in order:
-                    diff(3, c)
-            size("act", *made[k])
-        for tc in todo[len(made) - DA:]:
-            size_pe("act", *tc)
-        for tc in made[len(made) - DA:]:
-            size("dve", *tc)
 
-    mean(2, 0)
+    fold_x(3)
     mean(2, 1)
-    v_mult(1, 3)
-    v_add(1, 3, 1)
-    fold_x(3, N_X)
-    for c in last:
-        gamma_mu("act" if c != far[1] else "dve", c)
+    blocks = [far[0], near[0], far[1], r]
+    first = [c for c in blocks if c >= 2][0]
+    gamma_mu("act", 5 - first)
+    gamma_mu("dve", first)
+    v_add_pe(3)
     slope_mu("P5")
-    hf = far[0] // 2
-    banks = {hf: ("PA", "PB", "PD"), 1 - hf: ("P1", "P6", "P0")}
-    for h in (hf, 1 - hf):
-        for k in (0, 2, 1):
-            wr_pass(banks[h][k], 0, (2, 3, 5)[k], T.G2, "G2", 2 * h, 2)
     slope_m("P5")
+    banks = (("PA", "PB", "PD"), ("P1", "P6", "P0"))
 
-    def lists(h):
-        composed(banks[h][0], 128 * h, 128)
-        cp(T.GO[:, 128 * h:128 * h + 128], pb(banks[h][2], 128 * h, 128), [banks[h][2]], ["GO.%d" % h, "GO"])
+    def passes(j):
+        for k in range(3):
+            wr_pass(banks[j % 2][k], 0, (2, 3, 5)[k], T.G2, "G2", blocks[j])
 
-    def send_u(c):
-        send([([T.cores[c]], mk(c), "u%d" % r, [c4(T.VD, c), c4(T.SW, c)], [c4(T.ST, (r - c) % N - 1)], 1)], ["VD.%d" % c, "pp%d" % c])
-    lists(hf)
-    v_gather(2, far[0])
-    v_gather(2, far[1])
-    p_gather("dve", far[0])
-    p_gather("act", far[1])
-    slopes(banks[hf][1], 0, 128 * hf, 128)
-    v_mult(2, far[0])
-    send_u(far[0])
-    lists(1 - hf)
-    v_mult(2, far[1])
-    send_u(far[1])
-    v_gather(2, near[0])
-    v_gather(2, r)
-    slopes(banks[1 - hf][1], 0, 128 * (1 - hf), 128)
-    p_gather("dve", near[0])
-    v_mult(2, near[0])
-    send_u(near[0])
-    p_gather("act", r)
-    v_mult(2, r)
+    def lists(j):
+        c, b = blocks[j], banks[j % 2]
+        return later(lambda: composed(b[0], 64 * c, 64), lambda: slopes(b[1], 0, 64 * c, 64),
+                     lambda: cp(o4(T.GO, c), pb(b[2], 64 * c, 64), [b[2]], ["GO.%d" % c, "GO"]))
+
+    def span(t, k, base=0, unit=1):
+        return t[:, (base + k[0]) // unit:(base + k[0] + k[1]) // unit]
+
+    def u_v(k):
+        act(span(T.VD, k), T.V[:].indirect(span(T.DU, k, 0, 16)), AF.Copy, ch("V") + ["DU.%d" % (k[0] // 1024), "VD.%d" % (k[0] // 1024)], ["u%d" % k[0]])
+
+    def u_p(q, k):
+        win, rd = T.PZ[:].indirect(span(T.GO, k, 0, 16)), ch("pz") + ["GO.%d" % (k[0] // 1024), "SW"]
+        if q == "act":
+            act(span(T.SW, k), win, AF.Copy, rd, ["p%d" % k[0]], scale=1.0 / 64)
+        else:
+            ts(span(T.SW, k), win, 1.0 / 64, None, A.mult, None, rd, ["p%d" % k[0]])
+
+    def u_mult(k):
+        tt(span(T.VD, k), T.RT[:, 128:182].indirect(span(T.IX, k, 0, 16)), span(T.VD, k), A.mult, ["RT2", "IX.%d" % (k[0] // 1024), "u%d" % k[0]], ["u%d" % k[0]])
+
+    def u_send(k):
+        c = k[0] // 1024
+        send([([T.cores[c]], mk(c), "u%d_%d" % (r, k[0] % 1024 // 512), [span(T.VD, k), span(T.SW, k)], [span(T.ST, k, 1024 * ((r - c) % N - 1 - c))], 1)],
+             ["u%d" % k[0], "p%d" % k[0]])
+    passes(0)
+    passes(1)
+    rest = []
+    for j, c in enumerate(blocks):
+        ka, kb = (1024 * c, 512), (1024 * c + 512, 512)
+        du, t1, add, ix, go = lists(j)
+        du()
+        u_v(ka)
+        u_v(kb)
+        for f in [t1] + rest[:1] + [add] + rest[1:2] + [ix] + rest[2:] + [go]:
+            f()
+        if j < 2:
+            passes(j + 2)
+        u_p("act", ka)
+        u_p("dve" if c == r else "act", kb)
+        u_mult(ka)
+        rest = [lambda kb=kb: u_mult(kb)]
+        if c != r:
+            u_send(ka)
+            rest.append(lambda kb=kb: u_send(kb))
+    rest[0]()
     gat("act", c4(T.RR, 0), T.MP[:], o4(T.MU, r), ch("MP") + ["MU.%d" % (r // 2)], ["RR.0"])
     for q in others:
-        arrive("u%d" % q, nk(q), ["LU.%d" % ((q - r) % N - 1)])
-    late = [q for q in far if [c for c in [(q + k) % N for k in range(1, N)] if topo.chip(T.cores[c]) != topo.chip(T.cores[q])][1] == r]
-    tail = (late + far)[0]
-    lu = [(q - r) % N - 1 for q in [c for c in far if c != tail] + near + [tail]]
-    parts = [(T.IDF, T.SW, 1024 * r, ["IDF", "pp%d" % r]), (T.IDF, T.VD, 1024 * r, ["IDF", "VD.%d" % r]), (T.I32, T.RR, 0, ["I32", "RR.0"]),
-             (T.IDF, T.ST, 1024 * lu[0], ["IDF", "LU.%d" % lu[0]]), (T.IDF, T.ST, 1024 * lu[1], ["IDF", "LU.%d" % lu[1]])]
-    for k, (l, src, o, keys) in enumerate(parts):
         for h in range(2):
-            mm(T.P0[:, 512 * h:512 * h + 512], l[:], src[:, o + 512 * h:o + 512 * h + 512], k == 0, k == len(parts) - 1, keys, [("P0", "P5")[h]])
+            arrive("u%d_%d" % (q, h), nk(q), ["LU%d.%d" % (q, h)])
+
+    def landed(q, h):
+        o = 1024 * ((q - r) % N - 1) + 512 * h
+        return T.ST[:, o:o + 512], "LU%d.%d" % (q, h)
+    for k in range(3):
+        for h in range(2):
+            a = 1024 * r + 512 * h
+            l, src, key = [(T.IDF,) + landed(far[0], h), (T.IDF, T.SW[:, a:a + 512], "p%d" % a), (T.I32, T.RR[:, 512 * h:512 * h + 512], "RR.0")][k]
+            mm(pb(("PA", "PB")[h], 0, 512), l[:], src, k == 0, k == 2, ["IDF", "I32", key], [("PA", "PB")[h]])
     for h in range(2):
-        a = slice(512 * h, 512 * h + 512)
-        o = 1024 * lu[2] + 512 * h
-        tt(T.ST[:, 3072 + 512 * h:3584 + 512 * h], T.ST[:, o:o + 512], T.P0[:, a], A.add, ["LU.%d" % lu[2], ("P0", "P5")[h]], ["Y%d" % h, "ST.3"])
-        dma(("sp", "act")[h], T.y[:, a], T.ST[:, 3072 + 512 * h:3584 + 512 * h], ["Y%d" % h], ["y%d" % h])
+        b, a = ("PA", "PB")[h], 1024 * r + 512 * h
+        tt(pb(b, 0, 512), T.VD[:, a:a + 512], pb(b, 0, 512), A.add, ["u%d" % a, b], [b])
+    for h in range(2):
+        b, y = ("PA", "PB")[h], T.ST[:, 3072 + 512 * h:3584 + 512 * h]
+        tt(pb(b, 0, 512), landed(near[0], h)[0], pb(b, 0, 512), A.add, [landed(near[0], h)[1], b], [b])
+        tt(y, landed(far[1], h)[0], pb(b, 0, 512), A.add, [landed(far[1], h)[1], b], ["Y%d" % h, "ST.3"])
+        dma(("sp", "act")[h], T.y[:, 512 * h:512 * h + 512], y, ["Y%d" % h], ["y%d" % h])
     for s in cnt:
         wait("pool", (s, cnt[s]))

from concourse.bass import DstId, RemoteDMATransfer
from concourse.mybir import AluOpType as A, AxisListType, ActivationFunctionType as AF

W = 4096
MAG = 12582912.0
F32, BF, F16, I32, U16 = "float32", "bfloat16", "float16", "int32", "uint16"
NKW = 1024
G1P = (768, 768, 768, 768, 512, 512)


def _sb(n, d):
    return ("sbuf", [128, n], d)


SCRATCH = {
    "X": _sb(W, BF), "XP": _sb(W, BF), "MP": _sb(W, BF), "MS": _sb(W, BF), "MR": _sb(W, BF), "LX": _sb(6144, BF), "D": _sb(2 * W, BF),
    "V": _sb(W, F32), "VD": _sb(W, F32), "PZ": _sb(W, F32), "PAY": _sb(W, BF),
    "WG": _sb(W, BF), "G1": _sb(W, BF), "G2": _sb(W, BF),
    "SW": _sb(W + 256, F32), "ST": _sb(W, F32), "RR": _sb(W, BF),
    "NK": _sb(2 * NKW, BF),
    "PI": _sb(4, I32), "KI": _sb(256, I32), "TI": _sb(256, I32), "TJ": _sb(256, I32), "GS": _sb(256, I32), "GA": _sb(256, I32),
    "EI": _sb(256, I32),
    "CI": _sb(256, F32), "CG": _sb(160, F32), "CO": _sb(32, F32), "OH": _sb(16, F32), "T1": _sb(256, F32), "T2": _sb(256, F32),
    "EE": _sb(7 * 144, BF), "ID": _sb(128, BF), "NID": _sb(128, BF), "ID2": _sb(128, BF), "I32": _sb(128, BF), "CM": _sb(128, BF),
    "IDF": _sb(128, F32), "GM4": _sb(128, F32), "GN4": _sb(128, F32), "KC": _sb(4, F32),
    "QI": _sb(128, F16), "LZ": _sb(4 * 160, F16), "S1": _sb(128, F16), "S2": _sb(128, F16),
    "BC": _sb(256, F32), "DUMP": _sb(16, F32), "B64": _sb(16, F32), "ZR": _sb(256, F32), "PO": _sb(16, U16),
    "TOP": _sb(260, F32), "EX": _sb(256, F32), "MM": _sb(256, F32), "NN": _sb(260, F32),
    "TA": _sb(72, F32), "TB": _sb(64, F32), "TC": _sb(64, F32), "MK": _sb(64, F32),
    "NH": _sb(264, F16), "TR": ("sbuf", [128, 8, 2, 16], F16), "FF": _sb(20, F32), "FA": _sb(48, F32), "SO": _sb(16, U16), "SRC": _sb(256, F32),
    "HL": _sb(512, BF),
    "LW": _sb(1024, F32), "EU": _sb(256, U16), "GO": _sb(256, U16), "GN": _sb(256, U16), "IN": _sb(256, U16), "HT": _sb(512, BF), "HN": _sb(1024, BF),
    "MO": _sb(256, F16), "ML": _sb(9 * 256, F16), "MU": _sb(256, U16), "MV": _sb(128, U16), "MH": _sb(264, F16),
    "ACC": _sb(72, F32), "EL": _sb(8, F32), "CS": _sb(16, U16), "CU": _sb(256, U16),
    "DU": _sb(256, U16), "IX": _sb(256, U16), "RHO": _sb(8, F32), "RB": _sb(8, F32), "RT": _sb(192, F32),
    "LENT": ("dram", [2, 128, 2048], BF),
    "PA": ("psum", [128, 512], F32), "PB": ("psum", [128, 512], F32), "PD": ("psum", [128, 512], F32),
    "P0": ("psum", [128, 1024], F32), "P1": ("psum", [128, 1024], F32),
    "P4": ("psum", [128, 16, 2, 16], F32),
}
REMOTE = (["g%d" % t for t in range(3)] + ["a0", "a1"] + ["c_%d" % q for q in range(4)]
          + ["m%d_%d" % (t, h) for t in range(3) for h in range(2)] + ["x%d" % t for t in range(1, 4)]
          + ["b%d_%d" % (t, q) for t in range(4) for q in range(4)] + ["u%d_%d" % (q, h) for q in range(4) for h in range(2)]
          + ["s%d" % t for t in range(2)] + ["n%d" % t for t in range(2)] + ["%s%d" % (k, t) for t in range(2) for k in "fhl"])
SEMAPHORES = ["pe", "dve", "act", "pool"] + ["r" + k for k in REMOTE] + ["q%d" % i for i in range(90)]


def _bits(m):
    return [e for e in range(m.bit_length()) if m >> e & 1]


def _helper(core, T, topo):
    return [c for c in topo.cores_of(core) if topo.die(c) == topo.die(core) and T.rank_of(c) is None][0]


def helper_program(g, core, owner, T, topo):
    rid, pid, _ = topo.addr(owner)
    r = T.rank_of(owner)
    side = int(r > [T.rank_of(c) for c in T.cores if c != owner and topo.chip(c) == topo.chip(owner)][0])
    m = topo.mask(core, owner)
    far = [c for c in T.cores if topo.chip(c) != topo.chip(owner)][0]
    n_in = len(_bits(topo.mask(owner, core) & ~topo.mask(owner, far)))
    g.wait_ge(T.sem["rc_%d" % r], n_in)
    g.remote_dma(T.MS[:, 2048 + 512 * r:2560 + 512 * r], T.X[:, 0:512], T.sem["rc_%d" % r], T.sem.q0, pid, rid, m)
    for t in range(3):
        s = T.sem["rb%d_%d" % (t + 1, r)]
        g.wait_ge(s, n_in)
        g.remote_dma(T.MP[:, 1024 * r:1024 * r + 1024], T.X[:, 1024 * t + 1024:1024 * t + 2048], s, T.sem.q0, pid, rid, m)
        if t < 2:
            g.wait_ge(T.sem["rf%d" % t], len(_bits(topo.mask(owner, core))))
            g.remote_dma(T.G1[:, 2048 * side:2048 * side + 2048], T.G1[:, 2048 * t:2048 * t + 2048], T.sem["rf%d" % t], T.sem.q0, pid, rid, m)
    g.wait_ge(T.sem.q0, 6 * len(_bits(m)))


def rank_program(g, core, T, topo):
    r = T.rank_of(core)
    if r is None:
        for c in T.cores:
            if _helper(c, T, topo) == core:
                helper_program(g, core, c, T, topo)
        return
    N = len(T.cores)

    Q = {"pe": g.tensor, "dve": g.vector, "act": g.scalar, "pool": g, "sp": g.sync}
    cnt = {}
    waited = {k: {} for k in Q}
    lastw, readers = {}, {}
    nq = [0]

    def wait(q, tok):
        s, v = tok[0], tok[1]
        if waited[q].get(s, 0) < v:
            Q[q].wait_ge(T.sem[s], v)
            waited[q][s] = v

    def deps(q, rd, wr, inorder):
        for k in rd:
            for tok in lastw.get(k, []):
                if not (q == "pe" and tok[0] == "pe"):
                    wait(q, tok)
        for k in wr:
            for tok in lastw.get(k, []) + readers.get(k, []):
                if not (inorder and tok[0] == q):
                    wait(q, tok)

    def done(tok, rd, wr, more=False):
        for k in rd:
            readers.setdefault(k, []).append(tok)
        for k in wr:
            lastw[k] = lastw[k] + [tok] if more else [tok]
            readers[k] = []

    held = []

    def later(*fns):
        held.append([])
        for f in fns:
            f()
        return held.pop()

    def op(q, fn, rd, wr):
        if held:
            return held[0].append(lambda: op(q, fn, rd, wr))
        ps = [k for k in rd if k[0] == "P" and len(k) == 2]
        deps(q, rd, wr, q == "pe")
        for k in ps:
            for tok in readers.get(k, []):
                if tok[0] != q:
                    wait(q, tok)
        cnt[q] = cnt.get(q, 0) + 1
        fn().then_inc(T.sem[q], 1)
        done((q, cnt[q]), rd, wr)

    def fresh():
        nq[0] += 1
        return "q%d" % (nq[0] - 1)

    def dma(q, out, in_, rd, wr, **kw):
        deps(q, rd, wr, False)
        s = fresh()
        Q[q].dma_start(out, in_, **kw).then_inc(T.sem[s], 16)
        cnt[s] = 16
        done((s, 16), rd, wr)

    def dma2(q, pairs, rd, wr):
        if held:
            return held[0].append(lambda: dma2(q, pairs, rd, wr))
        deps(q, rd, wr, False)
        s = fresh()
        for out, in_ in pairs:
            Q[q].dma_start(out, in_).then_inc(T.sem[s], 16)
        cnt[s] = 16 * len(pairs)
        done((s, cnt[s]), rd, wr)

    def back(out, in_):
        return [(out[0:112], in_[16:128]), (out[112:128], in_[0:16])]

    def arrive(key, n, wr, more=False):
        cnt["r" + key] = cnt.get("r" + key, 0) + n
        done(("r" + key, cnt["r" + key]), [], wr, more)

    def send(trs, rd, extra=()):
        deps("pool", list(rd) + list(extra), [], False)
        s = fresh()
        tot = 0
        L = []
        for cores, m, key, srcs, dsts, alu in trs:
            ids = [DstId(rid=topo.addr(c)[0], pnc=topo.addr(c)[1]) for c in cores]
            L.append(RemoteDMATransfer(dst_ids=ids, dma_engine_mask=m, remote_sem=T.sem["r" + key], srcs=srcs, dsts=dsts, alu_op=alu))
            tot += len(_bits(m))
        g.remote_dma_fused(L, local_sem=T.sem[s])
        cnt[s] = tot
        done((s, tot), rd, [])
        return (s, tot)

    V_, S_, P_ = g.vector, g.scalar, g.tensor

    def ts(out, in0, s1, s2, o0, o1, rd, wr):
        if o1 is None:
            op("dve", lambda: V_.tensor_scalar(out, in0, s1, None, o0), rd, wr)
        else:
            op("dve", lambda: V_.tensor_scalar(out, in0, s1, s2, o0, o1), rd, wr)

    def tt(out, a, b, o, rd, wr):
        op("dve", lambda: V_.tensor_tensor(out, a, b, o), rd, wr)

    def cp(out, a, rd, wr):
        op("dve", lambda: V_.tensor_copy(out, a), rd, wr)

    def ms(out, v, wr):
        op("dve", lambda: V_.memset(out, v), [], wr)

    def red(out, a, o, rd, wr, **kw):
        op("dve", lambda: V_.tensor_reduce(out, a, AxisListType.X, o, **kw), rd, wr)

    def scan(out, d0, d1, ini, o0, o1, rd, wr):
        op("dve", lambda: V_.tensor_tensor_scan(out, d0, d1, ini, o0, o1), rd, wr)

    def turn(out, a, rd, wr):
        op("dve", lambda: V_.transpose(out, a), rd, wr)

    def act(out, a, f, rd, wr, **kw):
        op("act", lambda: S_.activation(out, a, f, **kw), rd, wr)

    def mm(out, l, rhs, st, sp, rd, wr):
        op("pe", lambda: P_.matmul(out, l, rhs, st, sp), rd, wr)

    def gat(q, out, win, off, rd, wr):
        if q == "dve":
            cp(out, win.indirect(off), rd, wr)
        else:
            act(out, win.indirect(off), AF.Copy, rd, wr)

    def ch(name, cs=range(4)):
        return ["%s.%d" % (name, c) for c in cs]

    def c4(t, c, base=0):
        return t[:, base + 1024 * c:base + 1024 * c + 1024]

    def o4(t, c, base=0):
        return t[:, base + 64 * c:base + 64 * c + 64]

    def rows(t, a, b, c):
        return t[a:b, 1024 * c:1024 * c + 1024]

    BANK = {"PA": (T.PA, 0), "PB": (T.PB, 0), "PD": (T.PD, 0), "P0": (T.P0, 0), "P5": (T.P0, 512), "P1": (T.P1, 0), "P6": (T.P1, 512)}

    def pb(b, a, n):
        return BANK[b][0][:, BANK[b][1] + a:BANK[b][1] + a + n]

    others = [(r + k) % N for k in range(1, N)]
    far = [q for q in others if topo.chip(T.cores[q]) != topo.chip(core)]
    near = [q for q in others if q not in far]
    side = int(r > near[0])
    far = sorted(far, reverse=bool(side))
    last = far + near + [r]
    mine, theirs = [2 * side, 2 * side + 1], [2 - 2 * side, 3 - 2 * side]
    hc = _helper(core, T, topo)
    m_far = topo.mask(core, T.cores[far[0]])
    m_near = topo.mask(core, T.cores[near[0]]) & ~m_far
    fb = _bits(m_far)
    m_half = [sum(1 << e for e in fb[:len(fb) // 2]), sum(1 << e for e in fb[len(fb) // 2:])]
    n_far, n_near = len(fb), len(_bits(m_near))
    prev, nxt = (r - 1) % N, (r + 1) % N

    def mk(q):
        return m_far if q in far else m_near

    def nk(q):
        return n_far if q in far else n_near

    dma2("sp", back(T.GS, T.gam), [], ["GS"])
    for p in range(2):
        a = slice(2048 * p, 2048 * p + 2048)
        dma2("sp", [(T.D[0:112, a], T.xs[16:128, a]), (T.D[112:128, a], T.xs[0:16, a])], [], ch("D", (2 * p, 2 * p + 1)))
    dma("sp", T.GA[:], T.gam[:], [], ["GA"])
    dma("sp", T.EI[:], T.ew[:, 0:256], [], ["EI"])
    dma("sp", T.X[:], T.xs[:], [], ch("X"))
    dma("sp", T.PAY[:], T.pay[:], ["X.0"], ["pay"])
    dma("sp", T.RHO[:, 0:5], T.rho[:], [], ["RHO"])

    op("pool", lambda: g.iota(T.PI[:, 0:1], [[0, 1]], 0, 1), [], ["PI0"])
    op("pool", lambda: g.iota(T.KI[:], [[1, 256]], 0, 0), [], ["KI"])
    op("pool", lambda: g.iota(T.BC[:], [[1, 16], [16, 16]], 0, 0, allow_small_or_imprecise_dtypes=True), [], ["BC"])
    CO = T.CO

    def col(i):
        return CO[:, i:i + 1]
    ms(T.SW[:, 0:272], 0.0, ["SW0"])
    for k in range(4):
        act(T.SW[:, 272 << k:544 << k], T.SW[:, 0:272 << k], AF.Copy, ["SW%d" % i for i in range(k + 1)], ["SW%d" % (k + 1)])
    ms(T.ZR[:], 0.0, ["ZR"])
    ms(T.MK[:, 0:32], 1.0, ["MK"])
    ms(T.MK[:, 32:64], 0.0, ["MK2"])
    ms(T.TA[:], 0.0, ["TA0", "TA1"])
    ms(T.MK[:, 0:32:16], 0.0, ["MK"])
    ms(T.MK[:, 47:64:16], 4096.0, ["MK2"])
    ms(T.TOP[:, 0:1], 0.0, ["TOP0"])
    ms(T.NN[:, 256:257], 4096.0, ["NNe"])
    ts(T.PI[:, 1:2], T.PI[:, 0:1], 15, None, A.bitwise_and, None, ["PI0"], ["PI1"])
    ts(T.PI[:, 2:3], T.PI[:, 0:1], 16, None, A.bitwise_and, None, ["PI0"], ["PI2"])
    cp(T.CI[:], T.KI[:], ["KI"], ["CI"])
    cp(CO[:, 0:2], T.PI[:, 0:2], ["PI0", "PI1"], ["c0", "c1"])
    ts(T.TI[:, 0:160], T.KI[:, 0:160], 240, None, A.bitwise_and, None, ["KI"], ["TI"])
    tt(col(2), col(0), col(1), A.subtract, ["c0", "c1"], ["c2"])
    ts(T.OH[:], T.CI[:, 0:16], col(1), None, A.is_equal, None, ["CI", "c1"], ["OH"])
    cp(T.CG[:], T.TI[:, 0:160], ["TI"], ["CG"])
    ts(col(6), T.PI[:, 2:3], 0.0625, None, A.mult, None, ["PI2"], ["c6"])
    ts(col(8), col(0), 16.0, None, A.add, None, ["c0"], ["c8"])
    ts(col(9), col(2), 16.0, None, A.add, None, ["c2"], ["c9"])
    ts(col(10), col(1), 16.0, None, A.mult, None, ["c1"], ["c10"])
    ts(col(5), T.OH[:, 0:1], -1.0, 1.0, A.mult, A.add, ["OH"], ["c5"])
    ts(col(7), col(6), -1.0, 1.0, A.mult, A.add, ["c6"], ["c7"])
    ts(T.T1[:, 0:160], T.CI[:, 0:160], col(8), None, A.is_equal, None, ["CI", "c8"], ["T1"])
    ts(T.PO[:], T.CI[:, 0:16], col(10), None, A.add, None, ["CI", "c10"], ["po"])
    for z in range(2):
        ts(T.LZ[:, 320 + 160 * z:480 + 160 * z], T.T1[:, 0:160], col(7 - z), None, A.mult, None, ["T1", "c6", "c7"], ["LP%d" % z])

    def regroup(base, key):
        for z in range(2):
            for gb in range(2):
                o = base + 160 * z + 16 - 16 * (gb - z)
                mm(T.P4[:, 0:8, z, :], T.LZ[:, o:o + 128], T.TR[:, :, gb, :], gb == 0, gb == 1, ["TR", key + str(z)], ["P4"])

    def to_blocks(src, key):
        ts(T.NH[:, 0:256], src.indirect(T.PO[:]), -2048.0, None, A.add, None, [key, "po"], ["NH"])
        turn(T.TR[:], T.NH[:, 0:256], ["NH"], ["TR"])
        regroup(320, "LP")

    def x_src(e, c):
        return (c4(T.D, c), "D.%d" % c) if e < 3 else (c4(T.XP, c), "XP.%d" % c)

    def send_x(e, c):
        send([([T.cores[c]], mk(c), "x%d" % e, [x_src(e, c)[0]], [c4(T.LX, (r - c) % N - 1, 3072 * (e % 2))], 0)],
             [x_src(e, c)[1]], ["fold", "MR"])

    def fold_x(e):
        arrive("x%d" % e, sum(nk(q) for q in others), ["LX"])
        srcs = [x_src(e, r)[0]] + [c4(T.LX, k, 3072 * (e % 2)) for k in range(3)]
        key = "b%d_%d" % (e, r)
        lastw["fold"] = [send([([T.cores[q] for q in far], m_far, key, srcs, [c4(T.MP, r)] * len(far), 2),
                               ([hc, T.cores[near[0]]], m_near, key, srcs, [c4(T.X, e), c4(T.MP, r)], 2)], ["LX", x_src(e, r)[1]])]
        for q in range(N):
            arrive("b%d_%d" % (e, q), len(_bits(topo.mask(hc, core))) if q == r else nk(q), ["MP.%d" % q])

    def send_g(t):
        dma("sp", T.HT[:], T.G1[0::8, :], ch("G1"), ["HT"])
        send([([T.cores[prev]], mk(prev), "g%d" % t, [T.HT[:]], [T.HN[:, 512 * t - 512:512 * t]], 0)], ["HT"])
        arrive("g%d" % t, nk(nxt), ["HN%d" % t])

    def piece(t, p, q):
        return t[:, 2048 * p + 512 * q:2048 * p + 512 * q + 512]

    def send_first(p):
        send([([T.cores[q]], m_near if q in near else m_half[far.index(q)], "a%d" % p, [piece(T.D, p, q)], [piece(T.LX, 0, 3 * p + (r - q) % N - 1)], 0)
              for q in others], ch("D", (2 * p, 2 * p + 1)))

    def fold_first(p):
        arrive("a%d" % p, n_far + n_near, ["LX%d" % p])
        srcs = [piece(T.D, p, r)] + [piece(T.LX, 0, 3 * p + k) for k in range(3)]
        key, to = "%s_%d" % (("b0", "c")[p], r), piece(T.MS, p, r)
        lastw["fold"] = lastw.get("fold", []) + [send([([T.cores[q] for q in far], m_far, key, srcs, [to] * len(far), 2),
                                                       ([hc] * p + [T.cores[near[0]]], m_near, key, srcs, [piece(T.X, 0, 0)] * p + [to], 2)],
                                                      ["LX%d" % p] + ch("D", (2 * p, 2 * p + 1)))]
        for q in range(N):
            arrive("%s_%d" % (("b0", "c")[p], q), len(_bits(topo.mask(hc, core))) if p and q == r else nk(q), ["MS.%d" % (2 * p + q // 2)], q % 2)

    def hand_back(key, part, pk):
        key = "%s_%d" % (key, near[0])
        wait("pool", ("r" + key, n_near))
        tok = send([([T.cores[near[0]]], m_near, key, [part], [part], 0)], [])
        lastw["fold"].append(tok)
        done(tok, [pk], [])

    send([([T.cores[prev]], mk(prev), "g0", [T.GS[:]], [T.TJ[:]], 0)], ["GS"])
    arrive("g0", nk(nxt), ["TJ"])
    send_first(0)
    send_first(1)

    def emat(k, a, b):
        ts(T.EE[:, 144 * k:144 * k + 144], T.CI[:, 0:144], col(a), col(b), A.is_equal, A.mult, ["CI", "c%d" % a, "c%d" % b], ["E%d" % k])

    def weight(k, a):
        ts(col(k), T.OH[:, a:a + 1], 64.0, T.OH[:, a + 8:a + 9], A.mult, A.add, ["OH"], ["c%d" % k])

    def KK(u):
        return 2.0 ** (20 * u - 50)

    def nk_ap(u):
        return T.NK[:, NKW * (u % 2):NKW * (u % 2) + NKW]

    def nk_tile(u):
        a, b, k = NKW * (u % 2), NKW * ((u - 1) % 2), "NK%d" % (u % 2)
        act(T.NK[:, a:a + 256], T.NK[:, b:b + 256], AF.Copy, ["NKa%d" % ((u - 1) % 2)], [k, "NKa%d" % (u % 2)], scale=KK(u) / KK(u - 1))
        dma2("sp", [(T.NK[:, a + 256 * i:a + 256 * i + 256], T.NK[:, a:a + 256]) for i in range(1, NKW // 256)], [], [k])

    def consts2():
        ts(T.T2[:, 0:160], T.CG[:], col(9), T.OH[:, 0:1], A.is_equal, A.mult, ["CG", "c9", "OH"], ["T2"])
        ts(col(11), col(1), 4096.0, None, A.add, None, ["c1"], ["c11"])
        tt(T.T1[:, 0:160], T.T1[:, 0:160], T.T2[:, 0:160], A.subtract, ["T1", "T2"], ["T1"])
        ts(T.BC[:], T.BC[:], T.OH[:, 0:1], None, A.mult, None, ["BC", "OH"], ["BC"])
        for z in range(2):
            ts(T.LZ[:, 160 * z:160 + 160 * z], T.T1[:, 0:160], col(7 - z), None, A.mult, None, ["T1", "c6", "c7"], ["LZ%d" % z])
        ts(T.DUMP[:], T.CI[:, 0:16], 16.0, col(11), A.mult, A.add, ["CI", "c11"], ["DUMP"])
        ts(col(12), T.OH[:, 0:1], 255.0, 1.0, A.mult, A.add, ["OH"], ["c12"])
        ts(col(24), col(5), -KK(0), None, A.mult, None, ["c5"], ["c24"])
        act(nk_ap(0), T.SW[:, 0:NKW], AF.Identity, ["SW0", "SW1", "SW2", "c24"], ["NK0", "NKa0"], bias=col(24))

    def consts3():
        ts(col(3), col(2), 15.0, None, A.add, None, ["c2"], ["c3"])
        ts(col(14), T.OH[:, 0:1], -17.0, 1.0, A.mult, A.add, ["OH"], ["c14"])
        emat(4, 3, 14)
        ts(T.EE[:, 864:1008], T.CI[:, 0:144], col(3), None, A.is_equal, None, ["CI", "c3"], ["E6"])

        ts(T.IDF[:], T.CI[:, 0:128], col(0), None, A.is_equal, None, ["CI", "c0"], ["IDF"])

    def identities():
        for k, v in (("ID", 1.0), ("NID", -1.0), ("ID2", 2.0), ("I32", 1.0 / 32)):
            act(T[k][:], T.IDF[:], AF.Copy, ["IDF"], [k], scale=v)

    def consts4():
        ts(T.GM4[:], T.CG[:, 0:128], col(2), 4.0, A.is_equal, A.mult, ["CG", "c2"], ["GM4"])
        ts(T.KC[:], T.CI[:, 0:4], -1.5, None, A.add, None, ["CI"], ["KC"])
        ts(T.B64[:], T.DUMP[:], -4095.625, 4.0, A.add, A.mult, ["DUMP"], ["B64"])
        ts(T.LW[:, 0::4], T.CI[:], 16.0, col(1), A.mult, A.add, ["CI", "c1"], ["LW.0"])
        weight(15, 0)
        emat(0, 3, 15)

    def places():
        for k, (pat, base) in enumerate((([[1, 4], [0, 64]], 0), ([[0, 4], [1, 64]], 0), ([[0, 4], [1, 64]], 1))):
            op("pool", lambda k=k, pat=pat, base=base: g.iota(T.G2[:, 256 * k:256 * k + 256], pat, base, 0, allow_small_or_imprecise_dtypes=True), [], ["PL%d." % k])
        ts(col(25), col(1), 4.0, None, A.mult, None, ["c1"], ["c25"])
        ts(T.G2[:, 0:256], T.G2[:, 0:256], col(25), None, A.add, None, ["PL0.", "c25"], ["PL0."])
        dma2("sp", [(T.WG[row::16, :], T.G2[:, 256 * k:256 * k + 256]) for row, k in ((1, 0), (2, 0), (4, 0), (9, 1), (12, 1), (10, 2))],
             ["PL0.", "PL1.", "PL2.", "G2.0"], ["WGp"])
        dma2("sp", [(T.WG[a::b, :], T.xs[a::b, :]) for a, b in ((3, 4), (5, 8), (6, 8))], [], ["WGg"])

    def own_rows():
        ts(T.TI[:], T.P4[:, 0:8, :, :], 2048.0, None, A.add, None, ["P4"], ["TI"])
        ts(T.KI[:], T.TI[:], 6, None, A.logical_shift_right, None, ["TI"], ["KI"])
        ts(T.TI[:], T.TI[:], 63, None, A.bitwise_and, None, ["TI"], ["TI"])
        cp(T.HL[:, 0:256], T.KI[:], ["KI"], ["HL0"])
        cp(T.HL[:, 256:512], T.TI[:], ["TI"], ["HL1"])
        dma2("sp", [(T.WG[8 * k::16, :], T.HL[:, 256 * k:256 * k + 256]) for k in range(2)], ["HL0", "HL1"], ["WGr"])

    def consts5():
        ts(T.QI[:], T.IDF[:], 0.25, None, A.mult, None, ["IDF"], ["QI"])
        ms(T.CM[:], -0.375, ["CM"])
        act(T.GN4[:], T.GM4[:], AF.Copy, ["GM4"], ["GN4"], scale=-1.0)
        ts(T.PI[:, 3:4], T.PI[:, 0:1], 112.0, None, A.add, None, ["PI0"], ["PI3"])
        weight(16, 1)
        ts(T.PI[:, 3:4], T.PI[:, 3:4], 127, None, A.bitwise_and, None, ["PI3"], ["PI3"])
        weight(17, 2)
        cp(col(13), T.PI[:, 3:4], ["PI3"], ["c13"])
        weight(21, 5)
        ts(col(4), col(13), col(1), 15.0, A.subtract, A.add, ["c13", "c1"], ["c4"])
        weight(22, 4)
        ts(col(20), col(0), -1.0, None, A.add, None, ["c0"], ["c20"])
        ts(col(18), col(17), col(16), 6.0, A.subtract, A.mult, ["c16", "c17"], ["c18"])
        emat(1, 4, 21)
        emat(2, 3, 16)
        emat(3, 3, 18)
        emat(5, 3, 22)

    def consts6():
        ts(T.T1[:, 0:128], T.CI[:, 0:128], col(20), col(5), A.is_equal, A.mult, ["CI", "c20", "c5"], ["T1"])
        ts(T.S2[:], T.CI[:, 0:128], col(3), T.OH[:, 0:1], A.is_equal, A.mult, ["CI", "c3", "OH"], ["S2"])
        tt(T.S1[:], T.T1[:, 0:128], T.IDF[:], A.subtract, ["T1", "IDF"], ["S1"])
        ts(T.MH[:, 256:257], col(0), 0.0, -8192.0, A.mult, A.add, ["c0"], ["MHe"])
        cp(T.RB[:, 1:6], T.RHO[:, 0:5], ["RHO"], ["RBa"])
        cp(T.RB[:, 0:1], T.RHO[:, 1:2], ["RHO"], ["RBb"])
        rt = ["RT1.%d" % a for a in range(9)]
        for a in range(9):
            s = abs(a - 4)
            ts(T.RT[:, 64 + 6 * a:70 + 6 * a], T.RB[:, 0:6], T.RHO[:, s:s + 1], None, A.mult, None, ["RBa", "RBb", "RHO"], [rt[a]])
        ts(T.RT[:, 0:54], T.RT[:, 64:118], 32.0, None, A.mult, None, rt, ["RT0"])
        ts(T.RT[:, 128:182], T.RT[:, 64:118], 1.0 / 128, None, A.mult, None, rt, ["RT2", "RT1"])

    def bits_of(out, win, off, c, rd, key, n, mult=None):
        def one(i):
            a, b = 1024 * c + 1024 // n * i, 1024 * c + 1024 // n * (i + 1)
            wr = [key] if i == 0 else []
            if mult:
                tt(out[:, a:b], win.indirect(off[:, a // 16:b // 16]), out[:, a:b], A.mult, rd + [key] * (i == 0), wr)
            else:
                cp(out[:, a:b], win.indirect(off[:, a // 16:b // 16]), rd, wr)
            lastw[key] = [("dve", cnt["dve"])]
        return [lambda i=i: one(i) for i in range(n)]

    def chain(Wa, Wr, wkey, u, fill=()):
        fill = list(fill)

        def gap():
            if fill:
                fill.pop(0)()
        scan(T.TOP[:, 1:257], Wa, T.ZR[:], 0.0, A.max, A.max, [wkey, "ZR"], ["TOP"])
        gap()
        turn(T.TA[:, 1:33], T.TOP[:, 225:257], ["TOP"], ["TA0"])
        gap()
        scan(T.TB[:, 0:32], T.TA[:, 0:32], T.MK[:, 0:32], 0.0, A.max, A.mult, ["TA0", "MK"], ["TB0"])
        gap()
        turn(T.TC[:, 0:32], T.TB[:, 0:32], ["TB0"], ["TC0"])
        gap()
        ts(T.EX[:], T.TOP[:, 0:256], T.TC[:, 31:32], None, A.max, None, ["TOP", "TOP0", "TC0"], ["EX"])
        gap()
        tt(T.MM[:], T.EX[:], Wa, A.is_ge, ["EX", wkey], ["MM"])
        gap()
        scan(T.NN[:, 255::-1], T.MM[:, ::-1], Wr, 4096.0, A.mult, A.max, ["MM", wkey], ["NN"])
        gap()
        turn(T.TA[:, 36:68], T.NN[:, 0:32], ["NN"], ["TA1"])
        ts(T.NN[:, 0:1], T.NN[:, 0:1], col(5), None, A.mult, None, ["NN", "c5"], ["NN"])
        scan(T.TB[:, 63:31:-1], T.TA[:, 68:36:-1], T.MK[:, 63:31:-1], 4096.0, A.min, A.max, ["TA1", "MK2"], ["TB1"])
        gap()
        turn(T.TC[:, 32:64], T.TB[:, 32:64], ["TB1"], ["TC1"])
        gap()
        ts(T.NH[:, 0:257], T.NN[:, 0:257], T.TC[:, 32:33], -2048.0, A.min, A.add, ["NN", "NNe", "TC1"], ["NH"])
        ts(T.FF[:, 0:17], T.NN[:, 0:257:16], T.TC[:, 32:33], None, A.min, None, ["NN", "NNe", "TC1"], ["FF"])
        turn(T.TR[:], T.NH[:, 0:256], ["NH"], ["TR"])
        regroup(0, "LZ")
        tt(T.FA[:, 0:16], T.FF[:, 0:16], T.FF[:, 1:17], A.is_ge, ["FF"], ["FA0"])
        gap()
        tt(T.FA[:, 16:32], T.FA[:, 0:16], T.DUMP[:], A.mult, ["FA0", "DUMP"], ["FA1"])
        gap()
        tt(T.FA[:, 32:48], T.FA[:, 16:32], T.FF[:, 0:16], A.max, ["FA1", "FF"], ["FA2"])
        tt(T.SRC[:], T.BC[:], T.P4[:, 0:8, :, :], A.add, ["BC", "P4"], ["SRC"])
        cp(T.SO[:], T.FA[:, 32:48], ["FA2"], ["SO"])
        gap()
        ts(T.SW[:].indirect(T.SO[:]), T.SRC[:], KK(u), 0.0, A.mult, A.add, ["SO", "SRC"], ["SW", "SW0", "SW1", "SW2", "SW3", "SW4"])
        return fill

    def wr_pass(bank, o, e, src, skey, c, n=1):
        for i in range(16):
            mm(pb(bank, o + 64 * c, 64 * n), T.EE[:, 144 * e + 15 - i:144 * e + 143 - i], src[:, 1024 * c + i:1024 * (c + n):16], i == 0, i == 15,
               ["E%d" % e] + ch(skey, range(c, c + n)), [bank])

    def b_pass(e, src, skey, c, first, end):
        for i in range(4 * c, 4 * c + 4):
            mm(T.PA[:, 0:256], T.EE[:, 144 * e + 15 - i:144 * e + 143 - i], src[:, 256 * i:256 * i + 256], first and i % 4 == 0, end and i % 4 == 3,
               ["E%d" % e, "%s.%d" % (skey, c)], ["PA"])

    def count_down(u, c):
        ini = 0.0 if c == 0 else T.ST[:, 1024 * c - 1:1024 * c]
        scan(c4(T.ST, c), nk_ap(u), c4(T.SW, c), ini, A.add, A.max,
             ["SW", "NK%d" % (u % 2)] + (["ST.%d" % (c - 1)] if c else []), ["ST.%d" % c])

    def run_out(u, c):
        act(c4(T.RR, c), c4(T.ST, c), AF.Relu, ["ST.%d" % c, "c12"], ["RR.%d" % c], bias=col(12), scale=-1.0 / KK(u))

    def evac_i():
        ts(T.IN[:], pb("PB", 0, 256), MAG + 4096, MAG, A.add, A.subtract, ["PB"], ["IN"])

    def evac_m(t, h):
        a = slice(128 * h, 128 * h + 128)
        b = "PB" if h == 0 else "P1"
        ts(T.MO[:, a], pb(b, 128 * h, 128), MAG + 2048, MAG, A.add, A.subtract, [b], ["MO.%d" % h])
        trs = []
        for q in others:
            o = 768 * t + 256 * ((r - q) % N - 1) + 128 * h
            trs.append(([T.cores[q]], m_near if q in near else m_half[far.index(q)], "m%d_%d" % (t, h), [T.MO[:, a]], [T.ML[:, o:o + 128]], 0))
        send(trs, ["MO.%d" % h])
        arrive("m%d_%d" % (t, h), n_near * len(near) + n_far, ["ML%d.%d" % (t, h)])

    ring, jk = [0], [0]
    LIST = {1: (T.EU, "EU"), 2: (T.GN, "GN"), 3: (T.IN, "IN")}

    HOME = {0: ("X", 0), 1: ("D", 4), 2: ("G1", 0), 3: ("XP", 0)}
    SUMS = {0: ("PB", "G1"), 3: ("PA", "XP")}

    def slot(tr, c):
        b, k = HOME[tr]
        return c4(T[b], c + k), "%s.%d" % (b, c + k)

    def acc(tr, j):
        return T.ACC[:, 4 * j + tr:4 * j + tr + 1], "A%d.%d" % (tr, j)

    def diff(tr, c):
        d, dk = slot(tr, c)
        tt(d, T.X[:].indirect(o4(LIST[tr][0], c)), c4(T.MS, c), A.subtract, ch("X") + [LIST[tr][1], "MS.%d" % c], [dk])

    def size(q, tr, c):
        d, dk = slot(tr, c)
        a, ak = acc(tr, 2 * c)
        if q == "act":
            act(d, d, AF.Abs, [dk], [dk, ak], accum_out=a)
        else:
            red(a, d, A.add, [dk], [ak], apply_absolute_value=True)

    def raw(tr, c):
        d, dk = slot(tr, c)
        gat("act", d, T.X[:], o4(LIST[tr][0], c), ch("X") + [LIST[tr][1]], [dk])

    def size_pe(tr, c, junk="MP"):
        dk = slot(tr, c)[1]
        ring[0] += 1
        B, keys = (T.P0, ["P0", "P5"]) if ring[0] % 2 else (T.P1, ["P1", "P6"])
        src, base = T[HOME[tr][0]], 1024 * (c + HOME[tr][1])
        for i in range(2):
            out = B[:, 512 * i:512 * i + 512]
            mm(out, T.ID[:], src[:, base + 512 * i:base + 512 * i + 512], True, False, ["ID", dk], [keys[i]])
            mm(out, T.NID[:], T.MS[:, 1024 * c + 512 * i:1024 * c + 512 * i + 512], False, True, ["NID", "MS.%d" % c], [keys[i]])
        a, ak = acc(tr, 2 * c)
        jk[0] += 1
        act(c4(T[junk], jk[0] % 4), B[:], AF.Abs, keys, ["%s.%d" % (junk, jk[0] % 4), ak], accum_out=a)

    def lend_x(t):
        deps("pool", [], ch("G1") + ["G1x", "G1n"], False)
        send([([T.cores[near[0]]], topo.mask(core, T.cores[near[0]]), "l%d" % t, [T.X[:, 1024 * theirs[0]:1024 * theirs[0] + 2048]],
               [T.LENT[t]], 0)], ch("X", theirs))
        arrive("l%d" % t, len(_bits(topo.mask(T.cores[near[0]], core))), ["lent"])

    def fold_max(t, own):
        a = slice(2048 * side, 2048 * side + 2048)
        if own:
            send([([hc], topo.mask(core, hc), "f%d" % t, [T.X[:, a], T.MS[:, a]], [T.G1[:, 2048 * t:2048 * t + 2048]], 2)], ch("X", mine) + ch("MS", mine))
            return arrive("f%d" % t, len(_bits(topo.mask(hc, core))), ch("G1", mine))
        send([([T.cores[near[0]]], topo.mask(core, T.cores[near[0]]), "h%d" % t, [T.LENT[t], T.MS[:, a]], [T.G1[:, a]], 2)], ch("MS", mine) + ["lent"])
        arrive("h%d" % t, len(_bits(topo.mask(T.cores[near[0]], core))), ch("G1", theirs))

    def add_up(tr, c, first=False, end=False):
        b, sk = SUMS[tr]
        for i in range(4):
            a = 1024 * c + 256 * i
            mm(pb(b, 0, 256), T.ID2[:], T[sk][:, a:a + 256], first and i == 0, end and i == 3,
               ["ID2", "%s.%d" % (sk, c)] + ["XPz"] * (tr == 3 and end and i == 3), [b])

    def inverse_sum(step):
        if step == 0:
            tt(T.EX[:], T.NH[:, 0:256], T.NH[:, 1:257], A.subtract, ["NH"], ["EX"])
        elif step == 1:
            tt(T.MM[:], T.EX[:], T.PA[:, 0:256], A.mult, ["EX", "PA"], ["MM"])
        else:
            red(acc(3, 1)[0], T.MM[:], A.add, ["MM"], [acc(3, 1)[1]])

    def greater(c, end=False):
        a, b = 1024 * c, 1024 * c + (768 if end else 1024)
        tt(T.XP[:, a:b], T.X[:].indirect(T.IN[:, a // 16:b // 16]), T.MS[:, a:b], A.max, ch("X") + ["IN", "MS.%d" % c], ["XP.%d" % c])
        if end:
            tt(T.XP[:, b:b + 256], T.X[:].indirect(T.IN[:, b // 16:b // 16 + 16]), T.MS[:, b:b + 256], A.max, ch("X") + ["IN", "MS.%d" % c], ["XPz"])

    def size_sum(tr, j=3, b=None):
        b = b or SUMS[tr][0]
        red(acc(tr, j)[0], pb(b, 0, 256), A.add, [b], [acc(tr, j)[1]])

    def clear_sums(n):
        ms(T.ACC[:, 0:4 * n], 0.0, ["A%d.%d" % (tr, j) for tr in range(4) for j in range(n)])

    def tally(js, first=False, end=False):
        if first:
            mm(T.P4[:, 8, 0, 0:4], T.IDF[:], T.KC[:], True, False, ["IDF", "KC"], ["P4"])
        for j in js:
            gm = "GM4" if j < 14 else "GN4"
            for z in range(2 if j in (8, 11) else 1):
                mm(T.P4[:, 8, 0, 0:4], T[gm][:], T.ACC[:, 4 * j + z:4 * j + z + 4], False, end and j == js[-1], [gm] + ["A%d.%d" % (tr, j) for tr in range(4)], ["P4"])

    def elect():
        red(T.EL[:, 0:1], T.P4[:, 8, 0, 0:4], A.min, ["P4"], ["EL0"])
        ts(T.EL[:, 1:2], T.EL[:, 0:1], 0.25, MAG, A.mult, A.add, ["EL0"], ["EL1"])
        ts(T.EL[:, 2:3], T.EL[:, 1:2], MAG, -4.0, A.subtract, A.mult, ["EL1"], ["EL2"])
        ts(T.CS[:], T.B64[:], T.EL[:, 0:1], T.EL[:, 2:3], A.add, A.add, ["B64", "EL0", "EL2"], ["CS"])
        ts(T.CU[:], T.LW[:].indirect(T.CS[:]), MAG, MAG, A.add, A.subtract, ch("LW") + ["CS"], ["CU"])

    def gamma_c():
        deps("dve", [], ch("G1"), False)
        deps("act", [], ch("G1"), False)
        a, toks = 0, []
        for k, n in enumerate(G1P):
            q, key = ("dve", "act")[k % 2], "G1p%d" % k
            gat(q, T.G1[:, a:a + n], T.WG[:], T.CU[:, a // 16:(a + n) // 16], ["WGg", "WGp", "WGr", "CU"], [key])
            toks = toks[-1:] + lastw[key]
            for i in range(a // 256, (a + n) // 256):
                mm(T.PA[:, 0:256], T.EE[:, 15 - i:143 - i], T.G1[:, 256 * i:256 * i + 256], i == 0, i == 15, ["E0", key], ["PA"])
            a += n
        for k in ch("G1"):
            lastw[k], readers[k] = toks, list(lastw["PA"])

    def x_c(t, c):
        gat("act", c4(T.XP, c), T.X[:], o4(T.CU, c), ch("X") + ["CU"], ["XP.%d" % c, "XPz"])
        if t < 2:
            dma2("sp", [(rows(T.D, 0, 112, c), rows(T.XP, 16, 128, c)), (rows(T.D, 112, 128, c), rows(T.XP, 0, 16, c))], ["XP.%d" % c], ["D.%d" % c])
        if c != r:
            send_x(t + 1, c)

    def mean(t, h):
        a = slice(128 * h, 128 * h + 128)
        b = "PD" if h == 0 else "P0"
        mm(T[b][:, a], T.ID[:], T.CM[:], True, False, ["ID", "CM"], [b])
        mm(T[b][:, a], T.QI[:], T.MO[:, a], False, False, ["QI", "MO.%d" % h], [b])
        for k in range(3):
            o = 768 * t + 256 * k + 128 * h
            mm(T[b][:, a], T.QI[:], T.ML[:, o:o + 128], False, k == 2, ["QI", "ML%d.%d" % (t, h)], [b])
        ts(T.MU[:, a], T[b][:, a], MAG + 2048, MAG, A.add, A.subtract, [b], ["MU.%d" % h])

    def gamma_mu(q, c):
        gat(q, c4(T.G2, c), T.G1[:], o4(T.MU, c), ch("G1") + ["G1n", "G1x", "MU.%d" % (c // 2)], ["G2.%d" % c])

    def x_mu(c):
        gat("act", c4(T.X, c), T.XP[:], o4(T.MU, c), ch("XP") + ["MU.%d" % (c // 2)], ["X.%d" % c])

    def m_mu(t):
        half = T.MS[:, 2048 * side:2048 * side + 2048]
        act(half, T.MP[:].indirect(T.MV[:]), AF.Copy, ch("MP") + ["MV"], ch("MS", mine) + [acc(2, 8)[1]], accum_out=acc(2, 8)[0])
        send([([T.cores[near[0]]], topo.mask(core, T.cores[near[0]]), "s%d" % t, [half], [half], 0)], ch("MS", mine))
        arrive("s%d" % t, len(_bits(topo.mask(T.cores[near[0]], core))), ch("MS", theirs))

    def m_sums(t):
        send([([T.cores[near[0]]], m_near, "n%d" % t, [T.ACC[:, 32:36]], [T.ACC[:, 44:48]], 0)], ["A%d.8" % tr for tr in range(4)])
        arrive("n%d" % t, n_near, ["A%d.11" % tr for tr in range(4)])

    def slope_mu(bm, o=0):
        ts(T.MH[:, 0:256], T.MU[:], -2048.0, None, A.add, None, ["MU.0", "MU.1"], ["MH"])
        mm(pb(bm, o, 256), T.S1[:], T.MH[:, 0:256], True, False, ["S1", "MH"], [bm])
        mm(pb(bm, o, 256), T.S2[:], T.MH[:, 1:257], False, True, ["S2", "MH", "MHe"], [bm])

    def composed(bd, a=0, n=256):
        cp(T.DU[:, a:a + n], pb(bd, a, n), [bd], ch("DU", range(a // 64, (a + n) // 64)))

    def slope_m(bm, o=0):
        ts(T.T2[:], pb(bm, o, 256), -1.0, 4.0, A.max, A.min, [bm], ["T2"])

    def slopes(bs, o, a=0, n=256, steps=range(3)):
        k = "T1.%d" % a
        if 0 in steps:
            ts(T.T1[:, a:a + n], pb(bs, o + a, n), -24.0, 24.0, A.max, A.min, [bs], [k, "T1"])
        if 1 in steps:
            tt(T.T1[:, a:a + n], T.T1[:, a:a + n], T.T2[:, a:a + n], A.add, [k, "T2"], [k])
        if 2 in steps:
            ts(T.IX[:, a:a + n], T.T1[:, a:a + n], 25.0, None, A.add, None, [k], ch("IX", range(a // 64, (a + n) // 64)))

    VB = ("VD", "V", "VD")

    def v_gather(t, c):
        win, k = (T.PAY, ["pay"]) if t == 0 else (T[VB[t - 1]], ch(VB[t - 1]))
        gat("act", c4(T[VB[t]], c), win[:], o4(T.DU, c), k + ["DU.%d" % c], ["%s.%d" % (VB[t], c)])

    def v_mult(t, c):
        v, k = c4(T[VB[t]], c), "%s.%d" % (VB[t], c)
        tt(v, T.RT[:, 64 * t:64 * t + 54].indirect(o4(T.IX, c)), v, A.mult, ["RT%d" % t, "IX.%d" % c, k], [k])

    def v_add(t, c, n):
        a = slice(1024 * c, 1024 * (c + n))
        dma("pool", T[VB[t]][:, a], T.MR[:, a], ["MR"], ch(VB[t], range(c, c + n)), accum_op=A.add, max_dma_last_dim=4096)

    def v_add_pe(c):
        B, keys = ((T.P0, ["P0", "P5"]), (T.P1, ["P1", "P6"]))[c % 2]
        for i in range(2):
            a = slice(1024 * c + 512 * i, 1024 * c + 512 * i + 512)
            mm(B[:, 512 * i:512 * i + 512], T.ID[:], T.MR[:, a], True, False, ["ID", "MR"], [keys[i]])
            mm(B[:, 512 * i:512 * i + 512], T.IDF[:], T.V[:, a], False, True, ["IDF", "V.%d" % c], [keys[i]])
        act(c4(T.V, c), B[:], AF.Copy, keys, ["V.%d" % c])

    def p_zero(c):
        act(c4(T.PZ, c), T.PAY[:].indirect(o4(T.GO, c)), AF.Copy, ["pay", "GO"], ["pz.%d" % c], scale=16.0)

    order = [1 - r // 2, r // 2, 3 - r // 2, 2 + r // 2]
    cp(T.EU[:], T.EI[:], ["EI"], ["EU"])
    to_blocks(T.GA[:], "GA")
    cp(T.GO[:], T.GA[:], ["GA"], ["GO"])
    consts2()
    rows_, places_ = later(own_rows), later(places)
    for f in rows_[:1] + places_[:3]:
        f()
    fold_first(0)
    fold_first(1)
    hand_back("b0", piece(T.MS, 0, near[0]), "MS.%d" % (near[0] // 2))
    for c in order:
        raw(1, c)
    consts3()
    to_blocks(T.TJ[:], "TJ")
    cp(T.GN[:], T.TJ[:], ["TJ"], ["GN"])
    ts(T.T2[:], T.P4[:, 0:8, :, :], 2048.0, None, A.add, None, ["P4"], ["T2"])
    identities()
    for c in range(2):
        p_zero(c)
    fill = chain(T.T2[:], T.T2[:, ::-1], "T2", 0, rows_[1:] + places_[3:] + later(lambda: clear_sums(18), consts4))
    early = [later(lambda: size_pe(tr, order[0])) for tr in (1, 0)]
    for c in range(4):
        count_down(0, c)
        run_out(0, c)
        if c == 1:
            for f in early[0][:4] + early[1][:4]:
                f()
        if c % 2:
            wr_pass("PB", 0, 4, T.RR, "RR", c - 1, 2)
        if fill:
            fill.pop(0)()
    for f in fill:
        f()
    cp(T.LW[:, 1::4], T.EI[:], ["EI"], ["LW.1"])
    cp(T.LW[:, 2::4], T.TJ[:], ["TJ"], ["LW.2"])
    made = [(2, c) for c in order[:2]] + [(tr, c) for k, c in enumerate(order) for tr in (3, 2) if tr == 3 or k >= 2]
    for k, tc in enumerate(made):
        if k == 2:
            evac_i()
        diff(*tc)
    cp(T.LW[:, 3::4], T.IN[:], ["IN"], ["LW.3"])
    early[0][4]()
    early[1][4]()
    for k, tc in enumerate([(tr, c) for c in order[1:] for tr in (1, 0)]):
        if k < 5:
            size("act", *made[k])
        size_pe(*tc)
    tally([2 * c for c in order[:2]], True)
    for tc in made[5:]:
        size("dve", *tc)
    tally([2 * c for c in order[2:]], end=True)
    HOME[2] = ("D", 0)

    for t in range(3):
        for u in range(2 * t + 1, min(2 * t + 3, 6)):
            nk_tile(u)
        if t:
            v_gather(t - 1, 0)
        elect()
        gamma_c()
        if t:
            slopes("PB", 256, steps=[1, 2])
        if t < 2:
            send_g(t + 1)
        wait("sp", readers["G1.0"][0])
        dma("sp", T.G1[2::8, 0:W - 1], T.G1[1::8, 1:W], ch("G1"), ["G1x"])
        for c in last:
            x_c(t, c)
        if t < 2:
            dma("sp", T.G1[5::8, :], T.HN[:, 512 * t:512 * t + 512], ["HN%d" % (t + 1)] + ch("G1"), ["G1n"])
            dma("sp", T.EI[:], T.ew[:, 256 * t + 256:256 * t + 512], [], ["EI"])
        if t:
            v_gather(t - 1, 1)
        fill = chain(T.PA[:, 0:256], T.PA[:, 255::-1], "PA", 2 * t + 1, [] if t else later(consts5))
        for c in range(4):
            count_down(2 * t + 1, c)
            run_out(2 * t + 1, c)
            wr_pass("PB" if c < 2 else "P1", 0, 4, T.RR, "RR", c)
        if t == 0:
            evac_m(t, 0)
            for f in fill:
                f()
            evac_m(t, 1)
            fold_x(t + 1)
            for c in range(2, 4):
                p_zero(c)
            fill = later(consts6, lambda: clear_sums(8))
            between = [fill[:8], fill[8:]]
        else:
            evac_m(t, 0)
            v_mult(t - 1, 0)
            for c in range(2, 4):
                v_gather(t - 1, c)
            evac_m(t, 1)
            if t == 2:
                v_add_pe(0)
                for c in range(1, 4):
                    if c == 3:
                        mean(2, 0)
                        gamma_mu("act", side)
                        gamma_mu("act", 1 - side)
                    v_mult(t - 1, c)
                    if c < 3:
                        v_add(t - 1, c, 1)
                break
            fold_x(t + 1)
            between = [[lambda: v_mult(0, 1)], [lambda: v_mult(0, 2)]]
        for f in between[0]:
            f()
        mean(t, 0)
        gamma_mu("act", 0)
        gamma_mu("act", 1)
        for f in between[1]:
            f()
        mean(t, 1)
        a = slice(128 * side, 128 * side + 128)
        dma2("sp", [(T.MV[0:112], T.MU[16:128, a]), (T.MV[112:128], T.MU[0:16, a])], ["MU.%d" % side], ["MV"])
        gamma_mu("dve", 2)
        gamma_mu("act", 3)
        x_mu(0)
        for c in range(4):
            b_pass(1, T.G2, "G2", c, c == 0, c == 3)
        dma("sp", T.WG[0::4, :], T.G2[0::4, :], ch("G2"), ["WGr"])
        cp(T.EU[:], T.EI[:], ["EI"], ["EU"])
        cp(T.LW[:, 1::4], T.EI[:], ["EI"], ["LW.1"])
        for c in range(1, 4):
            if c != theirs[1]:
                x_mu(c)
        slope_mu("PD", 256)
        wr_pass("P1", 0, 1, T.G2, "G2", 0, 4)
        fill = bits_of(T.X, T.XP[:], T.MU, theirs[1], ch("XP") + ["MU.1"], "X.%d" % theirs[1], 8)
        if t == 1:
            fill += bits_of(T.VD, T.RT[:, 0:54], T.IX, 3, ["RT0", "IX.3"], "VD.3", 4, True)
        wr_pass("PD", 0, 2, T.G2, "G2", 0, 2)
        for f in chain(T.PA[:, 0:256], T.PA[:, 255::-1], "PA", 2 * t + 2, fill):
            f()
        cp(T.GN[:], pb("P1", 0, 256), ["P1"], ["GN"])
        for c in range(4):
            b_pass(6, T.X, "X", c, c == 0, c == 3)
        wr_pass("PD", 0, 2, T.G2, "G2", 2, 2)
        for c in range(4):
            count_down(2 * t + 2, c)
            if c < 3:
                inverse_sum(c)
        cp(T.LW[:, 2::4], T.GN[:], ["GN"], ["LW.2"])
        size_sum(0, 14, "PA")
        order = mine + theirs
        raw(1, order[0])
        lend_x(t)
        m_mu(t)
        for c in range(4):
            run_out(2 * t + 2, c)
        for c in order[1:]:
            raw(1, c)
        fold_max(t, True)
        fold_max(t, False)
        m_sums(t)
        wr_pass("PB", 256, 3, T.G2, "G2", 0, 4)
        tally([8, 1], first=True)
        wr_pass("PB", 0, 4, T.RR, "RR", 0, 4)
        for c in mine:
            diff(2, c)
        evac_i()
        for c in theirs:
            diff(2, c)
        for c in mine:
            greater(c)
        cp(T.LW[:, 3::4], T.IN[:], ["IN"], ["LW.3"])
        for c in theirs:
            greater(c, c == theirs[1])
        for k, c in enumerate(order):
            size_pe(1, c, "RR")
            size("act", 2, c)
            if k == 1:
                tally([14, 11])
            if k >= 2:
                add_up(0, c, k == 2)
        add_up(3, mine[0], True)
        add_up(3, mine[1])
        for c in mine:
            add_up(0, c, end=c == mine[1])
        tally([2 * c for c in order[:3]])
        add_up(3, theirs[0])
        size_sum(0)
        add_up(3, theirs[1], end=True)
        composed("PD")
        slope_m("PD", 256)
        size_sum(3)
        tally([2 * order[3], 3], end=True)
        slopes("PB", 256, steps=[0])
        if t == 1:
            v_add(0, 0, 4)
        else:
            dma("pool", T.PZ[:], T.xs[:], [], ch("pz"), accum_op=A.add, max_dma_last_dim=4096)
        dma2("sp", [(T.MR[16:128], T.MS[0:112]), (T.MR[0:16], T.MS[112:128])], ch("MS"), ["MR"])

    fold_x(3)
    mean(2, 1)
    blocks = [far[0], near[0], far[1], r]
    first = [c for c in blocks if c >= 2][0]
    gamma_mu("act", 5 - first)
    gamma_mu("dve", first)
    v_add_pe(3)
    slope_mu("P5")
    slope_m("P5")
    banks = (("PA", "PB", "PD"), ("P1", "P6", "P0"))

    def passes(j):
        for k in range(3):
            wr_pass(banks[j % 2][k], 0, (2, 3, 5)[k], T.G2, "G2", blocks[j])

    def lists(j):
        c, b = blocks[j], banks[j % 2]
        return later(lambda: composed(b[0], 64 * c, 64), lambda: slopes(b[1], 0, 64 * c, 64),
                     lambda: cp(o4(T.GO, c), pb(b[2], 64 * c, 64), [b[2]], ["GO.%d" % c, "GO"]))

    def span(t, k, base=0, unit=1):
        return t[:, (base + k[0]) // unit:(base + k[0] + k[1]) // unit]

    def u_v(k):
        act(span(T.VD, k), T.V[:].indirect(span(T.DU, k, 0, 16)), AF.Copy, ch("V") + ["DU.%d" % (k[0] // 1024), "VD.%d" % (k[0] // 1024)], ["u%d" % k[0]])

    def u_p(q, k):
        win, rd = T.PZ[:].indirect(span(T.GO, k, 0, 16)), ch("pz") + ["GO.%d" % (k[0] // 1024), "SW"]
        if q == "act":
            act(span(T.SW, k), win, AF.Copy, rd, ["p%d" % k[0]], scale=1.0 / 64)
        else:
            ts(span(T.SW, k), win, 1.0 / 64, None, A.mult, None, rd, ["p%d" % k[0]])

    def u_mult(k):
        tt(span(T.VD, k), T.RT[:, 128:182].indirect(span(T.IX, k, 0, 16)), span(T.VD, k), A.mult, ["RT2", "IX.%d" % (k[0] // 1024), "u%d" % k[0]], ["u%d" % k[0]])

    def u_send(k):
        c = k[0] // 1024
        send([([T.cores[c]], mk(c), "u%d_%d" % (r, k[0] % 1024 // 512), [span(T.VD, k), span(T.SW, k)], [span(T.ST, k, 1024 * ((r - c) % N - 1 - c))], 1)],
             ["u%d" % k[0], "p%d" % k[0]])
    passes(0)
    passes(1)
    rest = []
    for j, c in enumerate(blocks):
        ka, kb = (1024 * c, 512), (1024 * c + 512, 512)
        du, t1, add, ix, go = lists(j)
        du()
        u_v(ka)
        u_v(kb)
        for f in [t1] + rest[:1] + [add] + rest[1:2] + [ix] + rest[2:] + [go]:
            f()
        if j < 2:
            passes(j + 2)
        u_p("act", ka)
        u_p("dve" if c == r else "act", kb)
        u_mult(ka)
        rest = [lambda kb=kb: u_mult(kb)]
        if c != r:
            u_send(ka)
            rest.append(lambda kb=kb: u_send(kb))
    rest[0]()
    gat("act", c4(T.RR, 0), T.MP[:], o4(T.MU, r), ch("MP") + ["MU.%d" % (r // 2)], ["RR.0"])
    for q in others:
        for h in range(2):
            arrive("u%d_%d" % (q, h), nk(q), ["LU%d.%d" % (q, h)])

    def landed(q, h):
        o = 1024 * ((q - r) % N - 1) + 512 * h
        return T.ST[:, o:o + 512], "LU%d.%d" % (q, h)
    for k in range(3):
        for h in range(2):
            a = 1024 * r + 512 * h
            l, src, key = [(T.IDF,) + landed(far[0], h), (T.IDF, T.SW[:, a:a + 512], "p%d" % a), (T.I32, T.RR[:, 512 * h:512 * h + 512], "RR.0")][k]
            mm(pb(("PA", "PB")[h], 0, 512), l[:], src, k == 0, k == 2, ["IDF", "I32", key], [("PA", "PB")[h]])
    for h in range(2):
        b, a = ("PA", "PB")[h], 1024 * r + 512 * h
        tt(pb(b, 0, 512), T.VD[:, a:a + 512], pb(b, 0, 512), A.add, ["u%d" % a, b], [b])
    for h in range(2):
        b, y = ("PA", "PB")[h], T.ST[:, 3072 + 512 * h:3584 + 512 * h]
        tt(pb(b, 0, 512), landed(near[0], h)[0], pb(b, 0, 512), A.add, [landed(near[0], h)[1], b], [b])
        tt(y, landed(far[1], h)[0], pb(b, 0, 512), A.add, [landed(far[1], h)[1], b], ["Y%d" % h, "ST.3"])
        dma(("sp", "act")[h], T.y[:, 512 * h:512 * h + 512], y, ["Y%d" % h], ["y%d" % h])
    for s in cnt:
        wait("pool", (s, cnt[s]))
